import numpy as np
import ml_dtypes


def mxq(x, axis, fmt="e4m3"):
    dtype, down = {"e4m3": (ml_dtypes.float8_e4m3fn, 7), "e5m2": (ml_dtypes.float8_e5m2, 14)}[fmt]
    v = np.moveaxis(np.asarray(x, np.float32).astype(ml_dtypes.bfloat16).astype(np.float64), axis, -1)
    blocks = v.reshape(v.shape[:-1] + (-1, 32))
    amax = np.abs(blocks).max(-1, keepdims=True)
    byte = np.maximum(np.where(amax > 0, np.frexp(amax)[1] - 1 + 127, 0) - down, 1)
    scale = np.exp2(byte - 127.0)
    codes = (blocks / scale).astype(np.float32).astype(dtype).astype(np.float64)
    return np.moveaxis((codes * scale).reshape(v.shape), -1, axis)


WIDE = False


def mx_kscale(k):
    if not WIDE:
        return np.ones(k)
    levels = np.array([10, -10, 5, -5, 0])
    if k % 512:
        return np.exp2(np.random.permutation(np.resize(levels, k // 32))).repeat(32)
    a = np.empty((k // 512, 16))
    for p in range(k // 512):
        a[p, :8] = np.random.permutation(np.resize(levels, 8))
        for g in range(8):
            far = levels[np.abs(levels - a[p, g]) >= 10]
            a[p, g + 8] = far[np.random.randint(len(far))]
    return np.exp2(a.ravel()).repeat(32)


def f64(x):
    return np.asarray(x).astype(np.float64)


def striped(idx):
    return np.tile(idx.reshape(-1, 16).T, (8, 1)).astype(np.uint16)


def unstriped(offs):
    return offs[:16].T.reshape(-1).astype(np.int64)


def striped8(idx):
    return np.concatenate([x.reshape(-1, 16).T for x in idx]).astype(np.uint16)


def runs(offs, k):
    lists = np.stack([offs[16 * r : 16 * r + 16].T.reshape(-1) for r in range(8)]).astype(np.int64)
    return lists[np.arange(k) % 512 // 64]


def pack_weight(w):
    k, n = w.shape
    w = f64(np.asarray(w, np.float32).astype(ml_dtypes.bfloat16)).reshape(k // 32, 32, n)
    amax = np.abs(w).max(1)
    byte = np.clip(np.where(amax > 0, np.frexp(amax)[1] - 1 + 127 - 7, 1), 1, 254)
    scaled = (w * np.exp2(127.0 - byte)[:, None, :]).reshape(k, n).astype(np.float32)
    words = np.ascontiguousarray(scaled.reshape(k // 512, 128, 4, n).transpose(0, 1, 3, 2)).astype(ml_dtypes.float8_e4m3fn).view(np.uint8)
    return words, np.ascontiguousarray(byte.astype(np.uint8).reshape(k // 512, 16, n))


def unpack_weight(words, scales):
    g, p, n, _ = words.shape
    vals = np.ascontiguousarray(words).view(ml_dtypes.float8_e4m3fn).astype(np.float64) * np.repeat(np.exp2(scales.astype(np.float64) - 127.0), 8, axis=1)[..., None]
    return vals.transpose(0, 1, 3, 2).reshape(g * 512, n)


def sigmoid(v):
    return 1.0 / (1.0 + np.exp(-np.maximum(v, -700.0)))

def planes(y):
    n, m = y.shape
    v = y.astype(np.float32).astype(ml_dtypes.bfloat16).astype(np.float64).reshape(n // 32, 32, m)
    top = np.abs(v).max(1)
    byte = np.clip(np.where(top > 0, np.frexp(top)[1] - 1 + 127 - 7, 1), 1, 254)
    codes = (v * np.exp2(127.0 - byte)[:, None, :]).reshape(n, m).astype(np.float32).astype(ml_dtypes.float8_e4m3fn).view(np.uint8)
    words = codes.reshape(n // 512, 128, 4, m).transpose(0, 1, 3, 2)
    return np.ascontiguousarray(words), np.ascontiguousarray(byte.astype(np.uint8).reshape(n // 512, 16, m))


K, T, S, V, N, H = 512, 2048, 512, 512, 512, 512


def setup_inputs():
    n = np.random.standard_normal
    s = mx_kscale(K)[:, None]
    u = mx_kscale(H)
    packed_xT = pack_weight(n((K, T)) * s)
    packed_w2 = pack_weight(n((H, N)) / np.sqrt(H) / u[:, None])
    packed_w3 = pack_weight(n((K, N)) / np.sqrt(K) / s)
    return {
        "x_words": packed_xT[0],
        "x_scales": packed_xT[1],
        "w1": (n((K, H)) / np.sqrt(K) / s * u).astype(np.float32),
        "a1": np.repeat(np.random.uniform(0.1, 0.6, (8, V)), 64, axis=0).astype(np.float32),
        "a2": np.repeat(np.random.uniform(0.1, 0.6, (8, V)), 64, axis=0).astype(np.float32),
        "a3": np.repeat(np.random.uniform(0.1, 0.6, (8, V)), 64, axis=0).astype(np.float32),
        "w2_words": packed_w2[0],
        "w2_scales": packed_w2[1],
        "w3_words": packed_w3[0],
        "w3_scales": packed_w3[1],
        "offs": striped(np.random.permutation(T)[:S]),
        "p1": striped8(np.stack([np.random.permutation(S) for _ in range(8)])),
        "p2": striped8(np.stack([np.random.permutation(S) for _ in range(8)])),
        "p3": striped8(np.stack([np.random.permutation(S) for _ in range(8)])),
        "own": striped(np.random.permutation(T)[:V]),
    }


def reference(x_words, x_scales, w1, a1, a2, a3, w2_words, w2_scales, w3_words, w3_scales, offs, p1, p2, p3, own):
    xq = unpack_weight(x_words, x_scales)[:, unstriped(offs)]
    y = mxq(f64(w1), 0, "e4m3").T @ xq
    z = (y[np.arange(H)[:, None], runs(p1, H)]) * f64(a1) + (y[np.arange(H)[:, None], runs(p2, H)]) * f64(a2) + (y[np.arange(H)[:, None], runs(p3, H)]) * f64(a3)
    o = unpack_weight(w2_words, w2_scales).T @ mxq(z, 0, "e4m3")
    x_own = unpack_weight(x_words, x_scales)[:, unstriped(own)]
    s = sigmoid(unpack_weight(w3_words, w3_scales).T @ x_own)
    out_0 = o * s
    return (out_0,) + planes(out_0)

@@ -1,0 +1,202 @@
+from contextlib import ExitStack
+
+import concourse.mybir as mybir
+from concourse.masks import make_identity
+
+K, T, S, V, N, H = 512, 2048, 512, 512, 512, 512
+FLOPS = 2 * K * H * S + 2 * H * N * V + 2 * K * N * V
+
+F32 = mybir.dt.float32
+BF16 = mybir.dt.bfloat16
+I32 = mybir.dt.int32
+U32 = mybir.dt.uint32
+U16 = mybir.dt.uint16
+U8 = mybir.dt.uint8
+FP8X4 = mybir.dt.float8_e4m3fn_x4
+MULT = mybir.AluOpType.mult
+SIGMOID = mybir.ActivationFunctionType.Sigmoid
+
+P = 128
+PACK = 4
+BLOCK = 128
+PIECES = (256, 128, 128)
+
+
+def load_scale_rows(queue, plane, rows, first):
+    for q in range(4):
+        queue.dma_start(
+            out=plane[32 * q + first : 32 * q + first + 4, :].bitcast(I32),
+            in_=rows[4 * q : 4 * q + 4, :].bitcast(I32),
+        )
+
+
+def as_words(packed):
+    return packed[0].rearrange("p n t -> p (n t)").bitcast(I32)
+
+
+def tile_picked_gatehead_none_po_kernel(
+    tc, x_words, x_scales, w1, a1, a2, a3, w2_words, w2_scales, w3_words, w3_scales,
+    offs, p1, p2, p3, own, out_0, out_1, out_2,
+):
+    nc = tc.nc
+    with ExitStack() as ctx:
+        keep = ctx.enter_context(tc.tile_pool(name="keep", bufs=1))
+        work = ctx.enter_context(tc.tile_pool(name="work", bufs=4))
+        psum = ctx.enter_context(tc.psum_pool(name="psum", bufs=1))
+
+        def load_list(src, name):
+            tile = keep.tile([P, S // 16], U16, name=name)
+            nc.sync.dma_start(tile[:], src)
+            return tile
+
+        xs_table = keep.tile([P, T], U8, name="xs_table", align_bytes=64)
+        nc.gpsimd.memset(xs_table[:].bitcast(I32), 0)
+        load_scale_rows(nc.scalar, xs_table, x_scales[0], 0)
+        w23s_raw = keep.tile([P, N], U8, name="w23s_raw")
+        nc.gpsimd.memset(w23s_raw[:].bitcast(I32), 0)
+        load_scale_rows(nc.scalar, w23s_raw, w2_scales[0], 0)
+        load_scale_rows(nc.gpsimd, w23s_raw, w3_scales[0], 4)
+        offs_sb = load_list(offs, "offs_sb")
+        own_sb = load_list(own, "own_sb")
+        xw_table = keep.tile([P, T], U32, name="xw_table", align_bytes=64)
+        nc.sync.dma_start(out=xw_table[:].bitcast(I32), in_=as_words(x_words))
+        w1_raw = keep.tile([P, PACK, H], F32, name="w1_raw")
+        nc.sync.dma_start(out=w1_raw[:], in_=w1.rearrange("(p j) c -> p j c", j=PACK))
+        lists = [load_list(p1, "p0_sb")]
+        w23_raw = keep.tile([P, 2, N], I32, name="w23_raw")
+        nc.sync.dma_start(out=w23_raw[:, 0, :], in_=as_words(w2_words))
+        nc.sync.dma_start(out=w23_raw[:, 1, :], in_=as_words(w3_words))
+        weights = []
+        for n, (p, a) in enumerate(((p1, a1), (p2, a2), (p3, a3))):
+            if n:
+                lists.append(load_list(p, f"p{n}_sb"))
+            a_sb = keep.tile([P, V], F32, name=f"a{n}_sb")
+            nc.sync.dma_start(out=a_sb[:], in_=a.rearrange("(p j) v -> p j v", j=PACK)[:, 0, :])
+            weights.append(a_sb)
+
+        ident = keep.tile([P, P], F32, name="ident")
+        make_identity(nc, ident[:])
+
+        def pick(table, offsets, dtype, name):
+            tile = keep.tile([P, S], dtype, name=name, align_bytes=64)
+            nc.vector.tensor_copy(out=tile[:], in_=table[:].indirect(offsets[:]))
+            return tile
+
+        xq_scales = pick(xs_table, offs_sb, U8, "xq_scales")
+        xo_scales = pick(xs_table, own_sb, U8, "xo_scales")
+        xq_words = pick(xw_table, offs_sb, U32, "xq_words")
+        xo_words = pick(xw_table, own_sb, U32, "xo_words")
+
+        w1_view = w1_raw[:].rearrange("p j (g t c i) -> p t g c j i", g=8, t=4, c=4, i=4)
+        w1_codes = keep.tile([P, H], U32, name="w1_codes", align_bytes=64)
+        w1_scales = keep.tile([P, H], U8, name="w1_scales", align_bytes=64)
+        y = []
+        for t in range(4):
+            cols = slice(t * P, (t + 1) * P)
+            w1_bf = keep.tile([P, P * PACK], BF16, name=f"w1_bf{t}", align_bytes=64)
+            cast = nc.scalar.copy if t in (1, 2) else nc.vector.tensor_copy
+            cast(
+                out=w1_bf[:].rearrange("p (g c i j) -> p g c j i", g=8, c=4, i=4, j=4),
+                in_=w1_view[:, t],
+            )
+            nc.vector.quantize_mx(out=w1_codes[:, cols].bitcast(FP8X4), scales=w1_scales[:, cols], in_=w1_bf[:])
+            acc = psum.tile([P, S], F32, name="acc", tag="acc", bufs=2)
+            nc.tensor.matmul_mx(
+                out=acc[:], lhsT=w1_codes[:, cols].bitcast(FP8X4), lhsT_scale=w1_scales[:, cols],
+                rhs=xq_words[:].bitcast(FP8X4), rhs_scale=xq_scales[:], start=True, stop=True,
+            )
+            y_t = keep.tile([P, S], F32, name=f"y{t}")
+            nc.scalar.copy(out=y_t[:], in_=acc[:])
+            y.append(y_t)
+
+        w23 = keep.tile([P, 2, N], I32, name="w23", align_bytes=64)
+        nc.vector.tensor_copy(
+            out=w23[:].rearrange("p w (t m) -> p w m t", t=4),
+            in_=w23_raw[:].rearrange("p w (m t) -> p w m t", t=4),
+        )
+        w23s = keep.tile([P, N], U8, name="w23s", align_bytes=64)
+        nc.vector.tensor_copy(
+            out=w23s[:].rearrange("p (t m) -> p m t", t=4),
+            in_=w23s_raw[:].rearrange("p (m t) -> p m t", t=4),
+        )
+
+        gate = keep.tile([P, 4, V], F32, name="gate")
+        for t in range(4):
+            cols = slice(t * P, (t + 1) * P)
+            acc = psum.tile([P, V], F32, name="acc", tag="acc", bufs=2)
+            nc.tensor.matmul_mx(
+                out=acc[:], lhsT=w23[:, 1, cols].bitcast(FP8X4), lhsT_scale=w23s[4:P, cols],
+                rhs=xo_words[:].bitcast(FP8X4), rhs_scale=xo_scales[:], start=True, stop=True,
+            )
+            nc.scalar.activation(out=gate[:, t, :], in_=acc[:], func=SIGMOID)
+
+        z_codes = keep.tile([P, V], U32, name="z_codes", align_bytes=64)
+        z_scales = keep.tile([P, V], U8, name="z_scales", align_bytes=64)
+        o_codes = keep.tile([P, V], U32, name="o_codes", align_bytes=64)
+        o_scales = keep.tile([P, V], U8, name="o_scales", align_bytes=64)
+        out_rows = out_0.rearrange("(p t) v -> p t v", t=4)
+        out_words = as_words(out_1)
+
+        def finish(v0, z_t):
+            cols = slice(v0, v0 + BLOCK)
+            zt_bf = work.tile([P, H], BF16, name="zt_bf")
+            nc.scalar.copy(
+                out=zt_bf[:].rearrange("v (g t r) -> v g t r", g=8, t=4),
+                in_=z_t[:].rearrange("v (t g r) -> v g t r", g=8, t=4),
+            )
+            pairs = zt_bf[:].bitcast(F32)
+            back = psum.tile([P, 2, BLOCK], F32, name="back", tag="back", bufs=2)
+            for u in range(2):
+                nc.tensor.transpose(back[:, u, :], pairs[:, u : H // 2 : 2], ident[:])
+            z_bf = work.tile([P, BLOCK * PACK], BF16, name="z_bf", align_bytes=64)
+            nc.scalar.copy(
+                out=z_bf[:].bitcast(F32).rearrange("p (v u) -> p v u", u=2),
+                in_=back[:].rearrange("p u v -> p v u"),
+            )
+            nc.vector.quantize_mx(out=z_codes[:, cols].bitcast(FP8X4), scales=z_scales[:, cols], in_=z_bf[:])
+            o = psum.tile([P, 4, BLOCK], F32, name="o", tag="o", bufs=2)
+            for t in range(4):
+                wcols = slice(t * P, (t + 1) * P)
+                nc.tensor.matmul_mx(
+                    out=o[:, t, :], lhsT=w23[:, 0, wcols].bitcast(FP8X4), lhsT_scale=w23s[:, wcols],
+                    rhs=z_codes[:, cols].bitcast(FP8X4), rhs_scale=z_scales[:, cols], start=True, stop=True,
+                )
+            res = keep.tile([P, 4, BLOCK], F32, name=f"res{v0}")
+            nc.vector.tensor_tensor(out=res[:], in0=o[:], in1=gate[:, :, cols], op=MULT)
+            nc.sync.dma_start(out=out_rows[:, :, cols], in_=res[:])
+            res_bf = work.tile([P, BLOCK * PACK], BF16, name="res_bf", align_bytes=64)
+            nc.scalar.copy(
+                out=res_bf[:].rearrange("p (c i t) -> p c t i", i=4, t=4),
+                in_=res[:].rearrange("p t (c i) -> p c t i", i=4),
+            )
+            nc.vector.quantize_mx(out=o_codes[:, cols].bitcast(FP8X4), scales=o_scales[:, cols], in_=res_bf[:])
+            nc.sync.dma_start(out=out_words[:, cols], in_=o_codes[:, cols].bitcast(I32))
+
+        v0 = 0
+        for width in PIECES:
+            blocks = range(width // BLOCK)
+            z_t = [psum.tile([P, H], F32, name="z_t", tag="z_t", bufs=2) for b in blocks]
+            for t in range(4):
+                for n in range(3):
+                    term = work.tile([P, width], F32, name="term", bufs=6)
+                    nc.vector.tensor_tensor(
+                        out=term[:],
+                        in0=y[t][:].indirect(lists[n][:, v0 // 16 : (v0 + width) // 16]),
+                        in1=weights[n][:, v0 : v0 + width],
+                        op=MULT,
+                    )
+                    for b in blocks:
+                        nc.tensor.matmul(
+                            z_t[b][:, t * P : (t + 1) * P], lhsT=term[:, b * BLOCK : (b + 1) * BLOCK], rhs=ident[:],
+                            start=(n == 0), stop=(n == 2), is_transpose=True,
+                        )
+            for b in blocks:
+                finish(v0 + b * BLOCK, z_t[b])
+            v0 = v0 + width
+
+        for q in range(4):
+            queue = nc.scalar if q % 2 else nc.sync
+            queue.dma_start(
+                out=out_2[0][4 * q : 4 * q + 4, :].bitcast(I32),
+                in_=o_scales[32 * q : 32 * q + 4, :].bitcast(I32),
+            )

@@ -19,7 +19,8 @@ SIGMOID = mybir.ActivationFunctionType.Sigmoid
 P = 128
 PACK = 4
 BLOCK = 128
-PIECES = (256, 128, 128)
+RING = 4
+PIECES = (384, 128)
 
 
 def load_scale_rows(queue, plane, rows, first):
@@ -52,20 +53,13 @@ def tile_picked_gatehead_none_po_kernel(
         xs_table = keep.tile([P, T], U8, name="xs_table", align_bytes=64)
         nc.gpsimd.memset(xs_table[:].bitcast(I32), 0)
         load_scale_rows(nc.scalar, xs_table, x_scales[0], 0)
-        w23s_raw = keep.tile([P, N], U8, name="w23s_raw")
-        nc.gpsimd.memset(w23s_raw[:].bitcast(I32), 0)
-        load_scale_rows(nc.scalar, w23s_raw, w2_scales[0], 0)
-        load_scale_rows(nc.gpsimd, w23s_raw, w3_scales[0], 4)
         offs_sb = load_list(offs, "offs_sb")
         own_sb = load_list(own, "own_sb")
         xw_table = keep.tile([P, T], U32, name="xw_table", align_bytes=64)
         nc.sync.dma_start(out=xw_table[:].bitcast(I32), in_=as_words(x_words))
+        lists = [load_list(p1, "p0_sb")]
         w1_raw = keep.tile([P, PACK, H], F32, name="w1_raw")
         nc.sync.dma_start(out=w1_raw[:], in_=w1.rearrange("(p j) c -> p j c", j=PACK))
-        lists = [load_list(p1, "p0_sb")]
-        w23_raw = keep.tile([P, 2, N], I32, name="w23_raw")
-        nc.sync.dma_start(out=w23_raw[:, 0, :], in_=as_words(w2_words))
-        nc.sync.dma_start(out=w23_raw[:, 1, :], in_=as_words(w3_words))
         weights = []
         for n, (p, a) in enumerate(((p1, a1), (p2, a2), (p3, a3))):
             if n:
@@ -73,6 +67,13 @@ def tile_picked_gatehead_none_po_kernel(
             a_sb = keep.tile([P, V], F32, name=f"a{n}_sb")
             nc.sync.dma_start(out=a_sb[:], in_=a.rearrange("(p j) v -> p j v", j=PACK)[:, 0, :])
             weights.append(a_sb)
+        w23_raw = keep.tile([P, 2, N], I32, name="w23_raw")
+        nc.sync.dma_start(out=w23_raw[:, 0, :], in_=as_words(w2_words))
+        nc.sync.dma_start(out=w23_raw[:, 1, :], in_=as_words(w3_words))
+        w23s_raw = keep.tile([P, N], U8, name="w23s_raw")
+        nc.vector.memset(w23s_raw[:].bitcast(I32), 0)
+        load_scale_rows(nc.sync, w23s_raw, w2_scales[0], 0)
+        load_scale_rows(nc.sync, w23s_raw, w3_scales[0], 4)
 
         ident = keep.tile([P, P], F32, name="ident")
         make_identity(nc, ident[:])
@@ -100,7 +101,7 @@ def tile_picked_gatehead_none_po_kernel(
                 in_=w1_view[:, t],
             )
             nc.vector.quantize_mx(out=w1_codes[:, cols].bitcast(FP8X4), scales=w1_scales[:, cols], in_=w1_bf[:])
-            acc = psum.tile([P, S], F32, name="acc", tag="acc", bufs=2)
+            acc = psum.tile([P, S], F32, name="acc", tag="bank", bufs=5)
             nc.tensor.matmul_mx(
                 out=acc[:], lhsT=w1_codes[:, cols].bitcast(FP8X4), lhsT_scale=w1_scales[:, cols],
                 rhs=xq_words[:].bitcast(FP8X4), rhs_scale=xq_scales[:], start=True, stop=True,
@@ -123,7 +124,7 @@ def tile_picked_gatehead_none_po_kernel(
         gate = keep.tile([P, 4, V], F32, name="gate")
         for t in range(4):
             cols = slice(t * P, (t + 1) * P)
-            acc = psum.tile([P, V], F32, name="acc", tag="acc", bufs=2)
+            acc = psum.tile([P, V], F32, name="acc", tag="bank", bufs=5)
             nc.tensor.matmul_mx(
                 out=acc[:], lhsT=w23[:, 1, cols].bitcast(FP8X4), lhsT_scale=w23s[4:P, cols],
                 rhs=xo_words[:].bitcast(FP8X4), rhs_scale=xo_scales[:], start=True, stop=True,
@@ -137,15 +138,36 @@ def tile_picked_gatehead_none_po_kernel(
         out_rows = out_0.rearrange("(p t) v -> p t v", t=4)
         out_words = as_words(out_1)
 
-        def finish(v0, z_t):
-            cols = slice(v0, v0 + BLOCK)
-            zt_bf = work.tile([P, H], BF16, name="zt_bf")
-            nc.scalar.copy(
-                out=zt_bf[:].rearrange("v (g t r) -> v g t r", g=8, t=4),
-                in_=z_t[:].rearrange("v (t g r) -> v g t r", g=8, t=4),
-            )
-            pairs = zt_bf[:].bitcast(F32)
-            back = psum.tile([P, 2, BLOCK], F32, name="back", tag="back", bufs=2)
+        zt_bf = [keep.tile([P, H], BF16, name=f"zt_bf{b}") for b in range(V // BLOCK)]
+
+        def look_up(v0, width):
+            blocks = range(v0 // BLOCK, (v0 + width) // BLOCK)
+            for t in range(4):
+                z_t = {b: psum.tile([P, P], F32, name="z_t", tag="bank", bufs=5) for b in blocks}
+                for n in range(3):
+                    term = work.tile([P, width], F32, name="term", bufs=RING)
+                    nc.vector.tensor_tensor(
+                        out=term[:],
+                        in0=y[t][:].indirect(lists[n][:, v0 // 16 : (v0 + width) // 16]),
+                        in1=weights[n][:, v0 : v0 + width],
+                        op=MULT,
+                    )
+                    for b in blocks:
+                        c0 = b * BLOCK - v0
+                        nc.tensor.matmul(
+                            z_t[b][:], lhsT=term[:, c0 : c0 + BLOCK], rhs=ident[:],
+                            start=(n == 0), stop=(n == 2), is_transpose=True,
+                        )
+                for b in blocks:
+                    nc.scalar.copy(
+                        out=zt_bf[b][:].rearrange("v (g t r) -> v g t r", g=8, t=4)[:, :, t, :],
+                        in_=z_t[b][:].rearrange("v (g r) -> v g r", g=8),
+                    )
+
+        def quantise_z(b):
+            cols = slice(b * BLOCK, (b + 1) * BLOCK)
+            pairs = zt_bf[b][:].bitcast(F32)
+            back = psum.tile([P, 2, BLOCK], F32, name="back", bufs=1)
             for u in range(2):
                 nc.tensor.transpose(back[:, u, :], pairs[:, u : H // 2 : 2], ident[:])
             z_bf = work.tile([P, BLOCK * PACK], BF16, name="z_bf", align_bytes=64)
@@ -154,18 +176,22 @@ def tile_picked_gatehead_none_po_kernel(
                 in_=back[:].rearrange("p u v -> p v u"),
             )
             nc.vector.quantize_mx(out=z_codes[:, cols].bitcast(FP8X4), scales=z_scales[:, cols], in_=z_bf[:])
-            o = psum.tile([P, 4, BLOCK], F32, name="o", tag="o", bufs=2)
+
+        def finish(b):
+            cols = slice(b * BLOCK, (b + 1) * BLOCK)
+            o = psum.tile([P, 4, BLOCK], F32, name="o", bufs=2)
             for t in range(4):
                 wcols = slice(t * P, (t + 1) * P)
                 nc.tensor.matmul_mx(
                     out=o[:, t, :], lhsT=w23[:, 0, wcols].bitcast(FP8X4), lhsT_scale=w23s[:, wcols],
                     rhs=z_codes[:, cols].bitcast(FP8X4), rhs_scale=z_scales[:, cols], start=True, stop=True,
                 )
-            res = keep.tile([P, 4, BLOCK], F32, name=f"res{v0}")
+            res = work.tile([P, 4, BLOCK], F32, name="res")
             nc.vector.tensor_tensor(out=res[:], in0=o[:], in1=gate[:, :, cols], op=MULT)
             nc.sync.dma_start(out=out_rows[:, :, cols], in_=res[:])
             res_bf = work.tile([P, BLOCK * PACK], BF16, name="res_bf", align_bytes=64)
-            nc.scalar.copy(
+            cast = nc.vector.tensor_copy if (b + 1) * BLOCK == V else nc.scalar.copy
+            cast(
                 out=res_bf[:].rearrange("p (c i t) -> p c t i", i=4, t=4),
                 in_=res[:].rearrange("p t (c i) -> p c t i", i=4),
             )
@@ -174,25 +200,12 @@ def tile_picked_gatehead_none_po_kernel(
 
         v0 = 0
         for width in PIECES:
-            blocks = range(width // BLOCK)
-            z_t = [psum.tile([P, H], F32, name="z_t", tag="z_t", bufs=2) for b in blocks]
-            for t in range(4):
-                for n in range(3):
-                    term = work.tile([P, width], F32, name="term", bufs=6)
-                    nc.vector.tensor_tensor(
-                        out=term[:],
-                        in0=y[t][:].indirect(lists[n][:, v0 // 16 : (v0 + width) // 16]),
-                        in1=weights[n][:, v0 : v0 + width],
-                        op=MULT,
-                    )
-                    for b in blocks:
-                        nc.tensor.matmul(
-                            z_t[b][:, t * P : (t + 1) * P], lhsT=term[:, b * BLOCK : (b + 1) * BLOCK], rhs=ident[:],
-                            start=(n == 0), stop=(n == 2), is_transpose=True,
-                        )
-            for b in blocks:
-                finish(v0 + b * BLOCK, z_t[b])
+            look_up(v0, width)
+            for b in range(v0 // BLOCK, (v0 + width) // BLOCK):
+                quantise_z(b)
             v0 = v0 + width
+        for b in range(V // BLOCK):
+            finish(b)
 
         for q in range(4):
             queue = nc.scalar if q % 2 else nc.sync

@@ -51,8 +51,12 @@ def tile_picked_gatehead_none_po_kernel(
             return tile
 
         xs_table = keep.tile([P, T], U8, name="xs_table", align_bytes=64)
-        nc.gpsimd.memset(xs_table[:].bitcast(I32), 0)
+        nc.vector.memset(xs_table[:].bitcast(I32), 0)
         load_scale_rows(nc.scalar, xs_table, x_scales[0], 0)
+        w23s_raw = keep.tile([P, N], U8, name="w23s_raw")
+        nc.vector.memset(w23s_raw[:].bitcast(I32), 0)
+        load_scale_rows(nc.scalar, w23s_raw, w2_scales[0], 0)
+        load_scale_rows(nc.scalar, w23s_raw, w3_scales[0], 4)
         offs_sb = load_list(offs, "offs_sb")
         own_sb = load_list(own, "own_sb")
         xw_table = keep.tile([P, T], U32, name="xw_table", align_bytes=64)
@@ -70,10 +74,6 @@ def tile_picked_gatehead_none_po_kernel(
         w23_raw = keep.tile([P, 2, N], I32, name="w23_raw")
         nc.sync.dma_start(out=w23_raw[:, 0, :], in_=as_words(w2_words))
         nc.sync.dma_start(out=w23_raw[:, 1, :], in_=as_words(w3_words))
-        w23s_raw = keep.tile([P, N], U8, name="w23s_raw")
-        nc.vector.memset(w23s_raw[:].bitcast(I32), 0)
-        load_scale_rows(nc.sync, w23s_raw, w2_scales[0], 0)
-        load_scale_rows(nc.sync, w23s_raw, w3_scales[0], 4)
 
         ident = keep.tile([P, P], F32, name="ident")
         make_identity(nc, ident[:])
@@ -95,13 +95,12 @@ def tile_picked_gatehead_none_po_kernel(
         for t in range(4):
             cols = slice(t * P, (t + 1) * P)
             w1_bf = keep.tile([P, P * PACK], BF16, name=f"w1_bf{t}", align_bytes=64)
-            cast = nc.scalar.copy if t in (1, 2) else nc.vector.tensor_copy
-            cast(
+            nc.vector.tensor_copy(
                 out=w1_bf[:].rearrange("p (g c i j) -> p g c j i", g=8, c=4, i=4, j=4),
                 in_=w1_view[:, t],
             )
             nc.vector.quantize_mx(out=w1_codes[:, cols].bitcast(FP8X4), scales=w1_scales[:, cols], in_=w1_bf[:])
-            acc = psum.tile([P, S], F32, name="acc", tag="bank", bufs=5)
+            acc = psum.tile([P, S], F32, name="acc", tag="bank", bufs=7)
             nc.tensor.matmul_mx(
                 out=acc[:], lhsT=w1_codes[:, cols].bitcast(FP8X4), lhsT_scale=w1_scales[:, cols],
                 rhs=xq_words[:].bitcast(FP8X4), rhs_scale=xq_scales[:], start=True, stop=True,
@@ -112,19 +111,19 @@ def tile_picked_gatehead_none_po_kernel(
 
         w23 = keep.tile([P, 2, N], I32, name="w23", align_bytes=64)
         nc.vector.tensor_copy(
-            out=w23[:].rearrange("p w (t m) -> p w m t", t=4),
-            in_=w23_raw[:].rearrange("p w (m t) -> p w m t", t=4),
+            out=w23[:].rearrange("p w (t c i) -> p w c t i", t=4, i=4),
+            in_=w23_raw[:].rearrange("p w (c i t) -> p w c t i", t=4, i=4),
         )
         w23s = keep.tile([P, N], U8, name="w23s", align_bytes=64)
         nc.vector.tensor_copy(
-            out=w23s[:].rearrange("p (t m) -> p m t", t=4),
-            in_=w23s_raw[:].rearrange("p (m t) -> p m t", t=4),
+            out=w23s[:].rearrange("p (t m) -> p t m", t=4),
+            in_=w23s_raw[:].rearrange("p (m t) -> p t m", t=4),
         )
 
         gate = keep.tile([P, 4, V], F32, name="gate")
         for t in range(4):
             cols = slice(t * P, (t + 1) * P)
-            acc = psum.tile([P, V], F32, name="acc", tag="bank", bufs=5)
+            acc = psum.tile([P, V], F32, name="acc", tag="bank", bufs=7)
             nc.tensor.matmul_mx(
                 out=acc[:], lhsT=w23[:, 1, cols].bitcast(FP8X4), lhsT_scale=w23s[4:P, cols],
                 rhs=xo_words[:].bitcast(FP8X4), rhs_scale=xo_scales[:], start=True, stop=True,
@@ -143,11 +142,13 @@ def tile_picked_gatehead_none_po_kernel(
         def look_up(v0, width):
             blocks = range(v0 // BLOCK, (v0 + width) // BLOCK)
             for t in range(4):
-                z_t = {b: psum.tile([P, P], F32, name="z_t", tag="bank", bufs=5) for b in blocks}
+                z_t = {b: psum.tile([P, P], F32, name="z_t", tag="bank", bufs=7) for b in blocks}
                 for n in range(3):
-                    term = work.tile([P, width], F32, name="term", bufs=RING)
+                    if n * width % PIECES[0] == 0:
+                        terms = work.tile([P, PIECES[0]], F32, name="terms", bufs=RING)
+                    term = terms[:, n * width % PIECES[0] : n * width % PIECES[0] + width]
                     nc.vector.tensor_tensor(
-                        out=term[:],
+                        out=term,
                         in0=y[t][:].indirect(lists[n][:, v0 // 16 : (v0 + width) // 16]),
                         in1=weights[n][:, v0 : v0 + width],
                         op=MULT,
@@ -179,7 +180,7 @@ def tile_picked_gatehead_none_po_kernel(
 
         def finish(b):
             cols = slice(b * BLOCK, (b + 1) * BLOCK)
-            o = psum.tile([P, 4, BLOCK], F32, name="o", bufs=2)
+            o = psum.tile([P, 4, BLOCK], F32, name="o", tag="bank", bufs=7)
             for t in range(4):
                 wcols = slice(t * P, (t + 1) * P)
                 nc.tensor.matmul_mx(

@@ -18,21 +18,27 @@ SIGMOID = mybir.ActivationFunctionType.Sigmoid
 
 P = 128
 PACK = 4
+TILES = 4
+HEADS = 8
+POINTS = 3
+QUADRANTS = 4
+W3_ROW = 4
 BLOCK = 128
-RING = 4
-PIECES = (384, 128)
+WIDE = V - BLOCK
+EARLY = 2
+BANKS = 7
 
 
-def load_scale_rows(queue, plane, rows, first):
-    for q in range(4):
-        queue.dma_start(
+def load_scale_rows(queues, plane, rows, first):
+    for q in range(QUADRANTS):
+        queues[q].dma_start(
             out=plane[32 * q + first : 32 * q + first + 4, :].bitcast(I32),
             in_=rows[4 * q : 4 * q + 4, :].bitcast(I32),
         )
 
 
 def as_words(packed):
-    return packed[0].rearrange("p n t -> p (n t)").bitcast(I32)
+    return packed[0].rearrange("p n j -> p (n j)").bitcast(I32)
 
 
 def tile_picked_gatehead_none_po_kernel(
@@ -42,7 +48,7 @@ def tile_picked_gatehead_none_po_kernel(
     nc = tc.nc
     with ExitStack() as ctx:
         keep = ctx.enter_context(tc.tile_pool(name="keep", bufs=1))
-        work = ctx.enter_context(tc.tile_pool(name="work", bufs=4))
+        work = ctx.enter_context(tc.tile_pool(name="work", bufs=V // BLOCK))
         psum = ctx.enter_context(tc.psum_pool(name="psum", bufs=1))
 
         def load_list(src, name):
@@ -50,30 +56,32 @@ def tile_picked_gatehead_none_po_kernel(
             nc.sync.dma_start(tile[:], src)
             return tile
 
-        xs_table = keep.tile([P, T], U8, name="xs_table", align_bytes=64)
-        nc.vector.memset(xs_table[:].bitcast(I32), 0)
-        load_scale_rows(nc.scalar, xs_table, x_scales[0], 0)
-        w23s_raw = keep.tile([P, N], U8, name="w23s_raw")
-        nc.vector.memset(w23s_raw[:].bitcast(I32), 0)
-        load_scale_rows(nc.scalar, w23s_raw, w2_scales[0], 0)
-        load_scale_rows(nc.scalar, w23s_raw, w3_scales[0], 4)
+        def bank(shape, name):
+            return psum.tile(shape, F32, name=name, tag="bank", bufs=BANKS)
+
         offs_sb = load_list(offs, "offs_sb")
         own_sb = load_list(own, "own_sb")
+        xs_table = keep.tile([P, T], U8, name="xs_table", align_bytes=64)
+        nc.gpsimd.memset(xs_table[:].bitcast(I32), 0)
+        load_scale_rows((nc.sync, nc.sync, nc.scalar, nc.scalar), xs_table, x_scales[0], 0)
         xw_table = keep.tile([P, T], U32, name="xw_table", align_bytes=64)
         nc.sync.dma_start(out=xw_table[:].bitcast(I32), in_=as_words(x_words))
-        lists = [load_list(p1, "p0_sb")]
         w1_raw = keep.tile([P, PACK, H], F32, name="w1_raw")
         nc.sync.dma_start(out=w1_raw[:], in_=w1.rearrange("(p j) c -> p j c", j=PACK))
-        weights = []
-        for n, (p, a) in enumerate(((p1, a1), (p2, a2), (p3, a3))):
-            if n:
-                lists.append(load_list(p, f"p{n}_sb"))
-            a_sb = keep.tile([P, V], F32, name=f"a{n}_sb")
+        lists, weights = [], []
+        w23_raw = keep.tile([P, 2, N], I32, name="w23_raw")
+        for n, (places, a) in enumerate(((p1, a1), (p2, a2), (p3, a3))):
+            lists.append(load_list(places, f"places{n}"))
+            a_sb = keep.tile([P, V], F32, name=f"weight{n}")
             nc.sync.dma_start(out=a_sb[:], in_=a.rearrange("(p j) v -> p j v", j=PACK)[:, 0, :])
             weights.append(a_sb)
-        w23_raw = keep.tile([P, 2, N], I32, name="w23_raw")
-        nc.sync.dma_start(out=w23_raw[:, 0, :], in_=as_words(w2_words))
-        nc.sync.dma_start(out=w23_raw[:, 1, :], in_=as_words(w3_words))
+            if n == 0:
+                nc.sync.dma_start(out=w23_raw[:, 0, :], in_=as_words(w2_words))
+                nc.sync.dma_start(out=w23_raw[:, 1, :], in_=as_words(w3_words))
+        w23s_raw = keep.tile([P, N], U8, name="w23s_raw", tag="reused")
+        nc.vector.memset(w23s_raw[:].bitcast(I32), 0)
+        load_scale_rows((nc.sync,) * QUADRANTS, w23s_raw, w2_scales[0], 0)
+        load_scale_rows((nc.sync,) * QUADRANTS, w23s_raw, w3_scales[0], W3_ROW)
 
         ident = keep.tile([P, P], F32, name="ident")
         make_identity(nc, ident[:])
@@ -88,19 +96,17 @@ def tile_picked_gatehead_none_po_kernel(
         xq_words = pick(xw_table, offs_sb, U32, "xq_words")
         xo_words = pick(xw_table, own_sb, U32, "xo_words")
 
-        w1_view = w1_raw[:].rearrange("p j (g t c i) -> p t g c j i", g=8, t=4, c=4, i=4)
+        w1_view = w1_raw[:].rearrange("p j (g t r) -> p t g r j", g=HEADS, t=TILES)
         w1_codes = keep.tile([P, H], U32, name="w1_codes", align_bytes=64)
         w1_scales = keep.tile([P, H], U8, name="w1_scales", align_bytes=64)
         y = []
-        for t in range(4):
+        for t in range(TILES):
             cols = slice(t * P, (t + 1) * P)
             w1_bf = keep.tile([P, P * PACK], BF16, name=f"w1_bf{t}", align_bytes=64)
-            nc.vector.tensor_copy(
-                out=w1_bf[:].rearrange("p (g c i j) -> p g c j i", g=8, c=4, i=4, j=4),
-                in_=w1_view[:, t],
-            )
+            cast = nc.scalar.copy if t < TILES // 2 else nc.vector.tensor_copy
+            cast(out=w1_bf[:].rearrange("p (g r j) -> p g r j", g=HEADS, j=PACK), in_=w1_view[:, t])
             nc.vector.quantize_mx(out=w1_codes[:, cols].bitcast(FP8X4), scales=w1_scales[:, cols], in_=w1_bf[:])
-            acc = psum.tile([P, S], F32, name="acc", tag="bank", bufs=7)
+            acc = bank([P, S], "y_acc")
             nc.tensor.matmul_mx(
                 out=acc[:], lhsT=w1_codes[:, cols].bitcast(FP8X4), lhsT_scale=w1_scales[:, cols],
                 rhs=xq_words[:].bitcast(FP8X4), rhs_scale=xq_scales[:], start=True, stop=True,
@@ -111,64 +117,69 @@ def tile_picked_gatehead_none_po_kernel(
 
         w23 = keep.tile([P, 2, N], I32, name="w23", align_bytes=64)
         nc.vector.tensor_copy(
-            out=w23[:].rearrange("p w (t c i) -> p w c t i", t=4, i=4),
-            in_=w23_raw[:].rearrange("p w (c i t) -> p w c t i", t=4, i=4),
-        )
-        w23s = keep.tile([P, N], U8, name="w23s", align_bytes=64)
-        nc.vector.tensor_copy(
-            out=w23s[:].rearrange("p (t m) -> p t m", t=4),
-            in_=w23s_raw[:].rearrange("p (m t) -> p t m", t=4),
+            out=w23[:].rearrange("p w (t c i) -> p w c t i", t=TILES, i=4),
+            in_=w23_raw[:].rearrange("p w (c i t) -> p w c t i", t=TILES, i=4),
         )
 
-        gate = keep.tile([P, 4, V], F32, name="gate")
-        for t in range(4):
+        zt_bf = [keep.tile([P, H], BF16, name=f"zt_bf{b}") for b in range(V // BLOCK)]
+
+        def look_up(v0, width, t, terms):
+            blocks = range(v0 // BLOCK, (v0 + width) // BLOCK)
+            sums = {b: bank([P, P], "z_sum") for b in blocks}
+            for n in range(POINTS):
+                term = terms[:, n * width : (n + 1) * width]
+                nc.vector.tensor_tensor(
+                    out=term,
+                    in0=y[t][:].indirect(lists[n][:, v0 // 16 : (v0 + width) // 16]),
+                    in1=weights[n][:, v0 : v0 + width],
+                    op=MULT,
+                )
+                for b in blocks:
+                    c0 = b * BLOCK - v0
+                    nc.tensor.matmul(
+                        sums[b][:], lhsT=term[:, c0 : c0 + BLOCK], rhs=ident[:],
+                        start=(n == 0), stop=(n == POINTS - 1), is_transpose=True,
+                    )
+            for b in blocks:
+                nc.scalar.copy(
+                    out=zt_bf[b][:].rearrange("v (g t r) -> v g t r", g=HEADS, t=TILES)[:, :, t, :],
+                    in_=sums[b][:].rearrange("v (g r) -> v g r", g=HEADS),
+                )
+
+        wide_room = POINTS * WIDE
+        early_terms = keep.tile([P, EARLY * wide_room], F32, name="early_terms")
+        for t in range(EARLY):
+            look_up(0, WIDE, t, early_terms[:, t * wide_room : (t + 1) * wide_room])
+
+        w23s = keep.tile([P, N], U8, name="w23s", align_bytes=64)
+        nc.vector.tensor_copy(
+            out=w23s[:].rearrange("p (t m) -> p t m", t=TILES),
+            in_=w23s_raw[:].rearrange("p (m t) -> p t m", t=TILES),
+        )
+        late_wide, last_room = (TILES - EARLY) * wide_room, POINTS * BLOCK
+        late_terms = keep.tile([P, late_wide + TILES * last_room], F32, name="late_terms", tag="reused")
+
+        gate = keep.tile([P, TILES, V], F32, name="gate")
+        for t in range(TILES):
             cols = slice(t * P, (t + 1) * P)
-            acc = psum.tile([P, V], F32, name="acc", tag="bank", bufs=7)
+            acc = bank([P, V], "gate_acc")
             nc.tensor.matmul_mx(
-                out=acc[:], lhsT=w23[:, 1, cols].bitcast(FP8X4), lhsT_scale=w23s[4:P, cols],
+                out=acc[:], lhsT=w23[:, 1, cols].bitcast(FP8X4), lhsT_scale=w23s[W3_ROW:P, cols],
                 rhs=xo_words[:].bitcast(FP8X4), rhs_scale=xo_scales[:], start=True, stop=True,
             )
             nc.scalar.activation(out=gate[:, t, :], in_=acc[:], func=SIGMOID)
 
         z_codes = keep.tile([P, V], U32, name="z_codes", align_bytes=64)
         z_scales = keep.tile([P, V], U8, name="z_scales", align_bytes=64)
-        o_codes = keep.tile([P, V], U32, name="o_codes", align_bytes=64)
-        o_scales = keep.tile([P, V], U8, name="o_scales", align_bytes=64)
-        out_rows = out_0.rearrange("(p t) v -> p t v", t=4)
+        out_codes = keep.tile([P, V], U32, name="out_codes", align_bytes=64)
+        out_scales = keep.tile([P, V], U8, name="out_scales", align_bytes=64)
+        out_rows = out_0.rearrange("(p t) v -> p t v", t=TILES)
         out_words = as_words(out_1)
-
-        zt_bf = [keep.tile([P, H], BF16, name=f"zt_bf{b}") for b in range(V // BLOCK)]
-
-        def look_up(v0, width):
-            blocks = range(v0 // BLOCK, (v0 + width) // BLOCK)
-            for t in range(4):
-                z_t = {b: psum.tile([P, P], F32, name="z_t", tag="bank", bufs=7) for b in blocks}
-                for n in range(3):
-                    if n * width % PIECES[0] == 0:
-                        terms = work.tile([P, PIECES[0]], F32, name="terms", bufs=RING)
-                    term = terms[:, n * width % PIECES[0] : n * width % PIECES[0] + width]
-                    nc.vector.tensor_tensor(
-                        out=term,
-                        in0=y[t][:].indirect(lists[n][:, v0 // 16 : (v0 + width) // 16]),
-                        in1=weights[n][:, v0 : v0 + width],
-                        op=MULT,
-                    )
-                    for b in blocks:
-                        c0 = b * BLOCK - v0
-                        nc.tensor.matmul(
-                            z_t[b][:], lhsT=term[:, c0 : c0 + BLOCK], rhs=ident[:],
-                            start=(n == 0), stop=(n == 2), is_transpose=True,
-                        )
-                for b in blocks:
-                    nc.scalar.copy(
-                        out=zt_bf[b][:].rearrange("v (g t r) -> v g t r", g=8, t=4)[:, :, t, :],
-                        in_=z_t[b][:].rearrange("v (g r) -> v g r", g=8),
-                    )
 
         def quantise_z(b):
             cols = slice(b * BLOCK, (b + 1) * BLOCK)
             pairs = zt_bf[b][:].bitcast(F32)
-            back = psum.tile([P, 2, BLOCK], F32, name="back", bufs=1)
+            back = psum.tile([P, 2, BLOCK], F32, name="back")
             for u in range(2):
                 nc.tensor.transpose(back[:, u, :], pairs[:, u : H // 2 : 2], ident[:])
             z_bf = work.tile([P, BLOCK * PACK], BF16, name="z_bf", align_bytes=64)
@@ -180,37 +191,37 @@ def tile_picked_gatehead_none_po_kernel(
 
         def finish(b):
             cols = slice(b * BLOCK, (b + 1) * BLOCK)
-            o = psum.tile([P, 4, BLOCK], F32, name="o", tag="bank", bufs=7)
-            for t in range(4):
-                wcols = slice(t * P, (t + 1) * P)
+            o = bank([P, TILES, BLOCK], "o")
+            for t in range(TILES):
+                w_cols = slice(t * P, (t + 1) * P)
                 nc.tensor.matmul_mx(
-                    out=o[:, t, :], lhsT=w23[:, 0, wcols].bitcast(FP8X4), lhsT_scale=w23s[:, wcols],
+                    out=o[:, t, :], lhsT=w23[:, 0, w_cols].bitcast(FP8X4), lhsT_scale=w23s[:, w_cols],
                     rhs=z_codes[:, cols].bitcast(FP8X4), rhs_scale=z_scales[:, cols], start=True, stop=True,
                 )
-            res = work.tile([P, 4, BLOCK], F32, name="res")
+            res = work.tile([P, TILES, BLOCK], F32, name="res")
             nc.vector.tensor_tensor(out=res[:], in0=o[:], in1=gate[:, :, cols], op=MULT)
             nc.sync.dma_start(out=out_rows[:, :, cols], in_=res[:])
             res_bf = work.tile([P, BLOCK * PACK], BF16, name="res_bf", align_bytes=64)
             cast = nc.vector.tensor_copy if (b + 1) * BLOCK == V else nc.scalar.copy
-            cast(
-                out=res_bf[:].rearrange("p (c i t) -> p c t i", i=4, t=4),
-                in_=res[:].rearrange("p t (c i) -> p c t i", i=4),
-            )
-            nc.vector.quantize_mx(out=o_codes[:, cols].bitcast(FP8X4), scales=o_scales[:, cols], in_=res_bf[:])
-            nc.sync.dma_start(out=out_words[:, cols], in_=o_codes[:, cols].bitcast(I32))
+            cast(out=res_bf[:].rearrange("p (v t) -> p v t", t=TILES), in_=res[:].rearrange("p t v -> p v t"))
+            nc.vector.quantize_mx(out=out_codes[:, cols].bitcast(FP8X4), scales=out_scales[:, cols], in_=res_bf[:])
+            nc.sync.dma_start(out=out_words[:, cols], in_=out_codes[:, cols].bitcast(I32))
 
-        v0 = 0
-        for width in PIECES:
-            look_up(v0, width)
-            for b in range(v0 // BLOCK, (v0 + width) // BLOCK):
-                quantise_z(b)
-            v0 = v0 + width
+        for t in range(EARLY, TILES):
+            at = (t - EARLY) * wide_room
+            look_up(0, WIDE, t, late_terms[:, at : at + wide_room])
+        for b in range(WIDE // BLOCK):
+            quantise_z(b)
+        for t in range(TILES):
+            at = late_wide + t * last_room
+            look_up(WIDE, BLOCK, t, late_terms[:, at : at + last_room])
+        quantise_z(WIDE // BLOCK)
         for b in range(V // BLOCK):
             finish(b)
 
-        for q in range(4):
+        for q in range(QUADRANTS):
             queue = nc.scalar if q % 2 else nc.sync
             queue.dma_start(
                 out=out_2[0][4 * q : 4 * q + 4, :].bitcast(I32),
-                in_=o_scales[32 * q : 32 * q + 4, :].bitcast(I32),
+                in_=out_scales[32 * q : 32 * q + 4, :].bitcast(I32),
             )

@@ -103,7 +103,7 @@ def tile_picked_gatehead_none_po_kernel(
         for t in range(TILES):
             cols = slice(t * P, (t + 1) * P)
             w1_bf = keep.tile([P, P * PACK], BF16, name=f"w1_bf{t}", align_bytes=64)
-            cast = nc.scalar.copy if t < TILES // 2 else nc.vector.tensor_copy
+            cast = nc.vector.tensor_copy if t < TILES // 2 else nc.scalar.copy
             cast(out=w1_bf[:].rearrange("p (g r j) -> p g r j", g=HEADS, j=PACK), in_=w1_view[:, t])
             nc.vector.quantize_mx(out=w1_codes[:, cols].bitcast(FP8X4), scales=w1_scales[:, cols], in_=w1_bf[:])
             acc = bank([P, S], "y_acc")

@@ -21,17 +21,24 @@ PACK = 4
 TILES = 4
 HEADS = 8
 POINTS = 3
+GROUP = 16
 QUADRANTS = 4
 W3_ROW = 4
-BLOCK = 128
-WIDE = V - BLOCK
-EARLY = 2
-BANKS = 7
+SPREAD = 8
+STRIP = 128
+STRIPS = V // STRIP
+LAST = STRIPS - 1
+WHOLE_TILES = 2
+WIDE = LAST * STRIP
+ZEROED_BY_GPSIMD = 3 * T // 4
+
+SUM_BANKS = ((4, 5, 6, 7), (4, 5, 6, 7), (4, 5, 6, 4), (2, 3, 7, 7))
+O_BANKS = ((5,), (7,), (2,), (3, 0))
 
 
-def load_scale_rows(queues, plane, rows, first):
+def load_scale_rows(nc, plane, rows, first):
     for q in range(QUADRANTS):
-        queues[q].dma_start(
+        nc.sync.dma_start(
             out=plane[32 * q + first : 32 * q + first + 4, :].bitcast(I32),
             in_=rows[4 * q : 4 * q + 4, :].bitcast(I32),
         )
@@ -41,6 +48,10 @@ def as_words(packed):
     return packed[0].rearrange("p n j -> p (n j)").bitcast(I32)
 
 
+def queries(first, last):
+    return slice(first * STRIP, (last + 1) * STRIP)
+
+
 def tile_picked_gatehead_none_po_kernel(
     tc, x_words, x_scales, w1, a1, a2, a3, w2_words, w2_scales, w3_words, w3_scales,
     offs, p1, p2, p3, own, out_0, out_1, out_2,
@@ -48,176 +59,243 @@ def tile_picked_gatehead_none_po_kernel(
     nc = tc.nc
     with ExitStack() as ctx:
         keep = ctx.enter_context(tc.tile_pool(name="keep", bufs=1))
-        work = ctx.enter_context(tc.tile_pool(name="work", bufs=V // BLOCK))
         psum = ctx.enter_context(tc.psum_pool(name="psum", bufs=1))
 
+        def bank(number, shape, name):
+            return psum.tile(shape, F32, name=name, tag=f"bank{number}")
+
         def load_list(src, name):
-            tile = keep.tile([P, S // 16], U16, name=name)
+            tile = keep.tile([P, S // GROUP], U16, name=name)
             nc.sync.dma_start(tile[:], src)
             return tile
 
-        def bank(shape, name):
-            return psum.tile(shape, F32, name=name, tag="bank", bufs=BANKS)
+        def load_weight(a, name):
+            tile = keep.tile([P, V], F32, name=name, align_bytes=64)
+            nc.sync.dma_start(out=tile[:], in_=a.rearrange("(p j) v -> p j v", j=PACK)[:, 0, :])
+            return tile
 
         offs_sb = load_list(offs, "offs_sb")
         own_sb = load_list(own, "own_sb")
+        lists = [load_list(p1, "places0")]
         xs_table = keep.tile([P, T], U8, name="xs_table", align_bytes=64)
-        nc.gpsimd.memset(xs_table[:].bitcast(I32), 0)
-        load_scale_rows((nc.sync, nc.sync, nc.scalar, nc.scalar), xs_table, x_scales[0], 0)
+        nc.gpsimd.memset(xs_table[:, :ZEROED_BY_GPSIMD].bitcast(I32), 0)
+        nc.vector.memset(xs_table[:, ZEROED_BY_GPSIMD:].bitcast(I32), 0)
+        nc.sync.dma_start(out=xs_table[0:P:SPREAD, :].bitcast(I32), in_=x_scales[0].bitcast(I32))
         xw_table = keep.tile([P, T], U32, name="xw_table", align_bytes=64)
         nc.sync.dma_start(out=xw_table[:].bitcast(I32), in_=as_words(x_words))
         w1_raw = keep.tile([P, PACK, H], F32, name="w1_raw")
         nc.sync.dma_start(out=w1_raw[:], in_=w1.rearrange("(p j) c -> p j c", j=PACK))
-        lists, weights = [], []
+
+        picked = keep.tile([P, S + V], U8, name="picked", align_bytes=64)
+        nc.vector.tensor_copy(out=picked[:, :S], in_=xs_table[:].indirect(offs_sb[:]))
+        nc.vector.tensor_copy(out=picked[:, S:], in_=xs_table[:].indirect(own_sb[:]))
+        x_plane = keep.tile([P, S + V], U8, name="x_plane", align_bytes=64)
+        nc.vector.memset(x_plane[:].bitcast(I32), 0)
+        for r in range(4):
+            nc.sync.dma_start(out=x_plane[r:P:32, :].bitcast(I32), in_=picked[SPREAD * r : P : 32, :].bitcast(I32))
+        xq_scales, xo_scales = x_plane[:, :S], x_plane[:, S:]
+
         w23_raw = keep.tile([P, 2, N], I32, name="w23_raw")
-        for n, (places, a) in enumerate(((p1, a1), (p2, a2), (p3, a3))):
-            lists.append(load_list(places, f"places{n}"))
-            a_sb = keep.tile([P, V], F32, name=f"weight{n}")
-            nc.sync.dma_start(out=a_sb[:], in_=a.rearrange("(p j) v -> p j v", j=PACK)[:, 0, :])
-            weights.append(a_sb)
-            if n == 0:
-                nc.sync.dma_start(out=w23_raw[:, 0, :], in_=as_words(w2_words))
-                nc.sync.dma_start(out=w23_raw[:, 1, :], in_=as_words(w3_words))
-        w23s_raw = keep.tile([P, N], U8, name="w23s_raw", tag="reused")
+        w23s_raw = keep.tile([P, N], U8, name="w23s_raw", tag="later_terms")
         nc.vector.memset(w23s_raw[:].bitcast(I32), 0)
-        load_scale_rows((nc.sync,) * QUADRANTS, w23s_raw, w2_scales[0], 0)
-        load_scale_rows((nc.sync,) * QUADRANTS, w23s_raw, w3_scales[0], W3_ROW)
+        nc.sync.dma_start(out=w23_raw[:, 0, :], in_=as_words(w2_words))
+        nc.sync.dma_start(out=w23_raw[:, 1, :], in_=as_words(w3_words))
+        weights = [load_weight(a1, "weight0")]
+        lists.append(load_list(p2, "places1"))
+        weights.append(load_weight(a2, "weight1"))
+        load_scale_rows(nc, w23s_raw, w2_scales[0], 0)
+        lists.append(load_list(p3, "places2"))
+        weights.append(load_weight(a3, "weight2"))
+        load_scale_rows(nc, w23s_raw, w3_scales[0], W3_ROW)
 
         ident = keep.tile([P, P], F32, name="ident")
         make_identity(nc, ident[:])
 
-        def pick(table, offsets, dtype, name):
-            tile = keep.tile([P, S], dtype, name=name, align_bytes=64)
-            nc.vector.tensor_copy(out=tile[:], in_=table[:].indirect(offsets[:]))
+        def pick_words(offsets, name, tag):
+            tile = keep.tile([P, GROUP * offsets.shape[1]], U32, name=name, tag=tag, align_bytes=64)
+            nc.vector.tensor_copy(out=tile[:], in_=xw_table[:].indirect(offsets))
             return tile
 
-        xq_scales = pick(xs_table, offs_sb, U8, "xq_scales")
-        xo_scales = pick(xs_table, own_sb, U8, "xo_scales")
-        xq_words = pick(xw_table, offs_sb, U32, "xq_words")
-        xo_words = pick(xw_table, own_sb, U32, "xo_words")
+        half_list = V // GROUP // 2
+        xq_words = pick_words(offs_sb[:], "xq_words", "xq_words")
+        xo_words = [pick_words(own_sb[:, :half_list], "xo_words0", "xo_words0")]
 
-        w1_view = w1_raw[:].rearrange("p j (g t r) -> p t g r j", g=HEADS, t=TILES)
+        w1_view = w1_raw[:].rearrange("p j (g h i u e) -> p u h g i j e", g=HEADS, h=2, u=2, e=2)
         w1_codes = keep.tile([P, H], U32, name="w1_codes", align_bytes=64)
         w1_scales = keep.tile([P, H], U8, name="w1_scales", align_bytes=64)
-        y = []
+        y = [
+            keep.tile([P, 2 * S if t < WHOLE_TILES else S], F32, name=f"y{t}", align_bytes=64) for t in range(TILES)
+        ]
+        nc.vector.memset(y[0][:, S:], 0.0)
+        nc.scalar.copy(out=y[1][:, S:], in_=y[0][:, S:])
         for t in range(TILES):
             cols = slice(t * P, (t + 1) * P)
-            w1_bf = keep.tile([P, P * PACK], BF16, name=f"w1_bf{t}", align_bytes=64)
-            cast = nc.vector.tensor_copy if t < TILES // 2 else nc.scalar.copy
-            cast(out=w1_bf[:].rearrange("p (g r j) -> p g r j", g=HEADS, j=PACK), in_=w1_view[:, t])
-            nc.vector.quantize_mx(out=w1_codes[:, cols].bitcast(FP8X4), scales=w1_scales[:, cols], in_=w1_bf[:])
-            acc = bank([P, S], "y_acc")
-            nc.tensor.matmul_mx(
-                out=acc[:], lhsT=w1_codes[:, cols].bitcast(FP8X4), lhsT_scale=w1_scales[:, cols],
-                rhs=xq_words[:].bitcast(FP8X4), rhs_scale=xq_scales[:], start=True, stop=True,
+            w1_bf = keep.tile(
+                [P, P * PACK], BF16, name=f"w1_bf{t}", tag=f"w1_bf{1 if t == TILES - 1 else t}", align_bytes=64
             )
-            y_t = keep.tile([P, S], F32, name=f"y{t}")
-            nc.scalar.copy(out=y_t[:], in_=acc[:])
-            y.append(y_t)
+            cast = nc.vector.tensor_copy if t == 0 else nc.scalar.copy
+            cast(
+                out=w1_bf[:].rearrange("p (g i e j) -> p g i j e", g=HEADS, e=2, j=PACK),
+                in_=w1_view[:, t // 2, t % 2],
+            )
+            nc.vector.quantize_mx(out=w1_codes[:, cols].bitcast(FP8X4), scales=w1_scales[:, cols], in_=w1_bf[:])
+            parts = 2 if t == 0 else 1
+            for k in range(parts):
+                part = slice(k * S // parts, (k + 1) * S // parts)
+                acc = bank(t + TILES * k, [P, S // parts], "y_acc")
+                nc.tensor.matmul_mx(
+                    out=acc[:], lhsT=w1_codes[:, cols].bitcast(FP8X4), lhsT_scale=w1_scales[:, cols],
+                    rhs=xq_words[:, part].bitcast(FP8X4), rhs_scale=xq_scales[:, part], start=True, stop=True,
+                )
+                nc.scalar.copy(out=y[t][:, part], in_=acc[:])
+            if t == 0:
+                xo_words.append(pick_words(own_sb[:, half_list:], "xo_words1", "w1_bf0"))
 
-        w23 = keep.tile([P, 2, N], I32, name="w23", align_bytes=64)
+        w23 = keep.tile([P, TILES, 2 * P], I32, name="w23", align_bytes=64)
         nc.vector.tensor_copy(
-            out=w23[:].rearrange("p w (t c i) -> p w c t i", t=TILES, i=4),
-            in_=w23_raw[:].rearrange("p w (c i t) -> p w c t i", t=TILES, i=4),
+            out=w23[:].rearrange("p (s e) (c i) -> p c s i e", e=2, i=4),
+            in_=w23_raw[:].rearrange("p w (c i s e) -> p (w c) s i e", s=2, e=2, i=4),
         )
 
-        zt_bf = [keep.tile([P, H], BF16, name=f"zt_bf{b}") for b in range(V // BLOCK)]
+        zt_bf = [keep.tile([P, H], BF16, name=f"zt_bf{b}", tag=f"zt_bf{b}", align_bytes=64) for b in range(STRIPS)]
+        sums = {}
 
-        def look_up(v0, width, t, terms):
-            blocks = range(v0 // BLOCK, (v0 + width) // BLOCK)
-            sums = {b: bank([P, P], "z_sum") for b in blocks}
-            for n in range(POINTS):
-                term = terms[:, n * width : (n + 1) * width]
-                nc.vector.tensor_tensor(
-                    out=term,
-                    in0=y[t][:].indirect(lists[n][:, v0 // 16 : (v0 + width) // 16]),
-                    in1=weights[n][:, v0 : v0 + width],
-                    op=MULT,
+        def look_up(v0, width, t, n, term):
+            u, h = divmod(t, 2)
+            together = t < WHOLE_TILES
+            nc.vector.tensor_tensor(
+                out=term,
+                in0=y[t][:].indirect(lists[n][:, v0 // GROUP : (v0 + width) // GROUP]),
+                in1=weights[n][:, v0 : v0 + width],
+                op=MULT,
+            )
+            for b in range(v0 // STRIP, (v0 + width) // STRIP):
+                if n == 0 and not (together and h == 1):
+                    sums[b] = bank(SUM_BANKS[t][b], [P, 2, P], "z_sum")
+                c0 = b * STRIP - v0
+                nc.tensor.matmul(
+                    sums[b][:, h, :], lhsT=term[:, c0 : c0 + STRIP], rhs=ident[:],
+                    start=(n == 0), stop=(n == POINTS - 1), is_transpose=True,
                 )
-                for b in blocks:
-                    c0 = b * BLOCK - v0
-                    nc.tensor.matmul(
-                        sums[b][:], lhsT=term[:, c0 : c0 + BLOCK], rhs=ident[:],
-                        start=(n == 0), stop=(n == POINTS - 1), is_transpose=True,
+                if n == POINTS - 1 and not (together and h == 0):
+                    done = slice(0, 2) if together else slice(h, h + 1)
+                    nc.scalar.copy(
+                        out=zt_bf[b][:].rearrange("v (u g h r) -> v u g h r", u=2, g=HEADS, h=2)[:, u, :, done, :],
+                        in_=sums[b][:].rearrange("v h (g r) -> v g h r", g=HEADS)[:, :, done, :],
                     )
-            for b in blocks:
-                nc.scalar.copy(
-                    out=zt_bf[b][:].rearrange("v (g t r) -> v g t r", g=HEADS, t=TILES)[:, :, t, :],
-                    in_=sums[b][:].rearrange("v (g r) -> v g r", g=HEADS),
+
+        def look_ups(v0, width, tiles, room):
+            at = 0
+            for t in tiles:
+                for n in range(POINTS):
+                    look_up(v0, width, t, n, room[:, at : at + width])
+                    at = at + width
+
+        gate = keep.tile([P, TILES, V], F32, name="gate")
+        z_scales = keep.tile([P, V], U8, name="z_scales", align_bytes=64)
+        out_codes = keep.tile([P, V], U32, name="out_codes", align_bytes=64)
+        out_scales = keep.tile([P, V], U8, name="out_scales", align_bytes=64)
+        res = keep.tile([P, TILES, V], F32, name="res")
+        out_rows = out_0.rearrange("(p t) v -> p t v", t=TILES)
+        out_words = as_words(out_1)
+        back = {}
+        o = {}
+
+        def turn_back(b, u):
+            if u == 0 and b % 2 == 0:
+                back[b // 2] = bank(b // 2, [P, 2, 2, STRIP], "back")
+            words = zt_bf[b][:].bitcast(F32)
+            nc.tensor.transpose(back[b // 2][:, b % 2, u, :], words[:, u * P : (u + 1) * P], ident[:])
+
+        def interleave(b, copy):
+            tile = keep.tile([P, STRIP * PACK], BF16, name=f"z_bf{b}", align_bytes=64)
+            copy(
+                out=tile[:].bitcast(F32).rearrange("p (v u) -> p v u", u=2),
+                in_=back[b // 2][:, b % 2].rearrange("p u v -> p v u"),
+            )
+            return tile
+
+        def project(b, z_strip):
+            cols = queries(b, b)
+            z_codes = keep.tile([P, STRIP], U32, name=f"z_codes{b}", align_bytes=64)
+            nc.vector.quantize_mx(out=z_codes[:].bitcast(FP8X4), scales=z_scales[:, cols], in_=z_strip[:])
+            o[b] = []
+            per_bank = TILES // len(O_BANKS[b])
+            for t in range(TILES):
+                if t % per_bank == 0:
+                    o[b].append(bank(O_BANKS[b][t // per_bank], [P, per_bank, STRIP], "o"))
+                nc.tensor.matmul_mx(
+                    out=o[b][-1][:, t % per_bank, :],
+                    lhsT=w23[:, t, :P].bitcast(FP8X4), lhsT_scale=w23s[:, t * P : (t + 1) * P],
+                    rhs=z_codes[:].bitcast(FP8X4), rhs_scale=z_scales[:, cols], start=True, stop=True,
                 )
 
-        wide_room = POINTS * WIDE
-        early_terms = keep.tile([P, EARLY * wide_room], F32, name="early_terms")
-        for t in range(EARLY):
-            look_up(0, WIDE, t, early_terms[:, t * wide_room : (t + 1) * wide_room])
+        def gate_and_store(b):
+            cols = queries(b, b)
+            per_bank = TILES // len(o[b])
+            for k, part in enumerate(o[b]):
+                rows = slice(k * per_bank, (k + 1) * per_bank)
+                nc.vector.tensor_tensor(out=res[:, rows, cols], in0=part[:], in1=gate[:, rows, cols], op=MULT)
+            nc.sync.dma_start(out=out_rows[:, :, cols], in_=res[:, :, cols])
+
+        def quantise_out(b, cast):
+            cols = queries(b, b)
+            res_bf = keep.tile([P, STRIP * PACK], BF16, name=f"res_bf{b}", tag=f"zt_bf{LAST - b}", align_bytes=64)
+            cast(
+                out=res_bf[:].rearrange("p (c e t) -> p c t e", e=2, t=TILES),
+                in_=res[:, :, cols].rearrange("p t (c e) -> p c t e", e=2),
+            )
+            nc.vector.quantize_mx(out=out_codes[:, cols].bitcast(FP8X4), scales=out_scales[:, cols], in_=res_bf[:])
+
+        def store_codes(first, last):
+            cols = queries(first, last)
+            nc.sync.dma_start(out=out_words[:, cols], in_=out_codes[:, cols].bitcast(I32))
+
+        first_terms = keep.tile([P, POINTS * V], F32, name="first_terms")
+        look_ups(0, V, (0,), first_terms)
 
         w23s = keep.tile([P, N], U8, name="w23s", align_bytes=64)
         nc.vector.tensor_copy(
             out=w23s[:].rearrange("p (t m) -> p t m", t=TILES),
             in_=w23s_raw[:].rearrange("p (m t) -> p t m", t=TILES),
         )
-        late_wide, last_room = (TILES - EARLY) * wide_room, POINTS * BLOCK
-        late_terms = keep.tile([P, late_wide + TILES * last_room], F32, name="late_terms", tag="reused")
+        wide_at = POINTS * V
+        last_at = wide_at + 2 * POINTS * WIDE
+        later_terms = keep.tile([P, last_at + 2 * POINTS * STRIP], F32, name="later_terms", tag="later_terms")
 
-        gate = keep.tile([P, TILES, V], F32, name="gate")
         for t in range(TILES):
-            cols = slice(t * P, (t + 1) * P)
-            acc = bank([P, V], "gate_acc")
-            nc.tensor.matmul_mx(
-                out=acc[:], lhsT=w23[:, 1, cols].bitcast(FP8X4), lhsT_scale=w23s[W3_ROW:P, cols],
-                rhs=xo_words[:].bitcast(FP8X4), rhs_scale=xo_scales[:], start=True, stop=True,
-            )
+            acc = bank(t, [P, V], "gate_acc")
+            for k in range(2):
+                half = slice(k * V // 2, (k + 1) * V // 2)
+                nc.tensor.matmul_mx(
+                    out=acc[:, half],
+                    lhsT=w23[:, t, P:].bitcast(FP8X4), lhsT_scale=w23s[W3_ROW:P, t * P : (t + 1) * P],
+                    rhs=xo_words[k][:].bitcast(FP8X4), rhs_scale=xo_scales[:, half], start=True, stop=True,
+                )
             nc.scalar.activation(out=gate[:, t, :], in_=acc[:], func=SIGMOID)
 
-        z_codes = keep.tile([P, V], U32, name="z_codes", align_bytes=64)
-        z_scales = keep.tile([P, V], U8, name="z_scales", align_bytes=64)
-        out_codes = keep.tile([P, V], U32, name="out_codes", align_bytes=64)
-        out_scales = keep.tile([P, V], U8, name="out_scales", align_bytes=64)
-        out_rows = out_0.rearrange("(p t) v -> p t v", t=TILES)
-        out_words = as_words(out_1)
-
-        def quantise_z(b):
-            cols = slice(b * BLOCK, (b + 1) * BLOCK)
-            pairs = zt_bf[b][:].bitcast(F32)
-            back = psum.tile([P, 2, BLOCK], F32, name="back")
-            for u in range(2):
-                nc.tensor.transpose(back[:, u, :], pairs[:, u : H // 2 : 2], ident[:])
-            z_bf = work.tile([P, BLOCK * PACK], BF16, name="z_bf", align_bytes=64)
-            nc.scalar.copy(
-                out=z_bf[:].bitcast(F32).rearrange("p (v u) -> p v u", u=2),
-                in_=back[:].rearrange("p u v -> p v u"),
-            )
-            nc.vector.quantize_mx(out=z_codes[:, cols].bitcast(FP8X4), scales=z_scales[:, cols], in_=z_bf[:])
-
-        def finish(b):
-            cols = slice(b * BLOCK, (b + 1) * BLOCK)
-            o = bank([P, TILES, BLOCK], "o")
-            for t in range(TILES):
-                w_cols = slice(t * P, (t + 1) * P)
-                nc.tensor.matmul_mx(
-                    out=o[:, t, :], lhsT=w23[:, 0, w_cols].bitcast(FP8X4), lhsT_scale=w23s[:, w_cols],
-                    rhs=z_codes[:, cols].bitcast(FP8X4), rhs_scale=z_scales[:, cols], start=True, stop=True,
-                )
-            res = work.tile([P, TILES, BLOCK], F32, name="res")
-            nc.vector.tensor_tensor(out=res[:], in0=o[:], in1=gate[:, :, cols], op=MULT)
-            nc.sync.dma_start(out=out_rows[:, :, cols], in_=res[:])
-            res_bf = work.tile([P, BLOCK * PACK], BF16, name="res_bf", align_bytes=64)
-            cast = nc.vector.tensor_copy if (b + 1) * BLOCK == V else nc.scalar.copy
-            cast(out=res_bf[:].rearrange("p (v t) -> p v t", t=TILES), in_=res[:].rearrange("p t v -> p v t"))
-            nc.vector.quantize_mx(out=out_codes[:, cols].bitcast(FP8X4), scales=out_scales[:, cols], in_=res_bf[:])
-            nc.sync.dma_start(out=out_words[:, cols], in_=out_codes[:, cols].bitcast(I32))
-
-        for t in range(EARLY, TILES):
-            at = (t - EARLY) * wide_room
-            look_up(0, WIDE, t, late_terms[:, at : at + wide_room])
-        for b in range(WIDE // BLOCK):
-            quantise_z(b)
-        for t in range(TILES):
-            at = late_wide + t * last_room
-            look_up(WIDE, BLOCK, t, late_terms[:, at : at + last_room])
-        quantise_z(WIDE // BLOCK)
-        for b in range(V // BLOCK):
-            finish(b)
+        look_ups(0, V, (1,), later_terms[:, :wide_at])
+        for b in range(STRIPS):
+            turn_back(b, 0)
+        look_ups(0, WIDE, (2, 3), later_terms[:, wide_at:last_at])
+        for b in range(LAST):
+            turn_back(b, 1)
+        z_bf = [interleave(b, nc.scalar.copy) for b in range(LAST - 1)]
+        look_ups(WIDE, STRIP, (2, 3), later_terms[:, last_at:])
+        z_bf.append(interleave(LAST - 1, nc.vector.tensor_copy))
+        turn_back(LAST, 1)
+        z_bf.append(interleave(LAST, nc.scalar.copy))
+        for b in range(LAST):
+            project(b, z_bf[b])
+        gate_and_store(0)
+        project(LAST, z_bf[LAST])
+        for b in range(1, STRIPS):
+            gate_and_store(b)
+        for b in range(LAST):
+            quantise_out(b, nc.scalar.copy)
+        store_codes(0, LAST - 1)
+        quantise_out(LAST, nc.vector.tensor_copy)
+        store_codes(LAST, LAST)
 
         for q in range(QUADRANTS):
             queue = nc.scalar if q % 2 else nc.sync

@@ -85,6 +85,8 @@ def tile_picked_gatehead_none_po_kernel(
         nc.sync.dma_start(out=xw_table[:].bitcast(I32), in_=as_words(x_words))
         w1_raw = keep.tile([P, PACK, H], F32, name="w1_raw")
         nc.sync.dma_start(out=w1_raw[:], in_=w1.rearrange("(p j) c -> p j c", j=PACK))
+        w23_raw = keep.tile([P, 2, N], I32, name="w23_raw")
+        nc.sync.dma_start(out=w23_raw[:, 0, :], in_=as_words(w2_words))
 
         picked = keep.tile([P, S + V], U8, name="picked", align_bytes=64)
         nc.vector.tensor_copy(out=picked[:, :S], in_=xs_table[:].indirect(offs_sb[:]))
@@ -95,10 +97,8 @@ def tile_picked_gatehead_none_po_kernel(
             nc.sync.dma_start(out=x_plane[r:P:32, :].bitcast(I32), in_=picked[SPREAD * r : P : 32, :].bitcast(I32))
         xq_scales, xo_scales = x_plane[:, :S], x_plane[:, S:]
 
-        w23_raw = keep.tile([P, 2, N], I32, name="w23_raw")
         w23s_raw = keep.tile([P, N], U8, name="w23s_raw", tag="later_terms")
         nc.vector.memset(w23s_raw[:].bitcast(I32), 0)
-        nc.sync.dma_start(out=w23_raw[:, 0, :], in_=as_words(w2_words))
         nc.sync.dma_start(out=w23_raw[:, 1, :], in_=as_words(w3_words))
         weights = [load_weight(a1, "weight0")]
         lists.append(load_list(p2, "places1"))
@@ -130,9 +130,7 @@ def tile_picked_gatehead_none_po_kernel(
         nc.scalar.copy(out=y[1][:, S:], in_=y[0][:, S:])
         for t in range(TILES):
             cols = slice(t * P, (t + 1) * P)
-            w1_bf = keep.tile(
-                [P, P * PACK], BF16, name=f"w1_bf{t}", tag=f"w1_bf{1 if t == TILES - 1 else t}", align_bytes=64
-            )
+            w1_bf = keep.tile([P, P * PACK], BF16, name=f"w1_bf{t}", tag=f"w1_bf{t}", align_bytes=64)
             cast = nc.vector.tensor_copy if t == 0 else nc.scalar.copy
             cast(
                 out=w1_bf[:].rearrange("p (g i e j) -> p g i j e", g=HEADS, e=2, j=PACK),

@@ -24,13 +24,14 @@ POINTS = 3
 GROUP = 16
 QUADRANTS = 4
 W3_ROW = 4
-SPREAD = 8
+XS_ROW = P - 16
 STRIP = 128
 STRIPS = V // STRIP
 LAST = STRIPS - 1
 WHOLE_TILES = 2
 WIDE = LAST * STRIP
-ZEROED_BY_GPSIMD = 3 * T // 4
+SCALAR_HEADS = 2
+Y0_BANKS = (0, 4, 5, 6)
 
 SUM_BANKS = ((4, 5, 6, 7), (4, 5, 6, 7), (4, 5, 6, 4), (2, 3, 7, 7))
 O_BANKS = ((5,), (7,), (2,), (3, 0))
@@ -74,18 +75,17 @@ def tile_picked_gatehead_none_po_kernel(
             nc.sync.dma_start(out=tile[:], in_=a.rearrange("(p j) v -> p j v", j=PACK)[:, 0, :])
             return tile
 
+        xs_table = keep.tile([P, T], U8, name="xs_table", tag="xs_table", align_bytes=64)
+        nc.vector.memset(xs_table[0:XS_ROW, :].bitcast(I32), 0)
+        nc.sync.dma_start(out=xs_table[XS_ROW:P, :].bitcast(I32), in_=x_scales[0].bitcast(I32))
         offs_sb = load_list(offs, "offs_sb")
         own_sb = load_list(own, "own_sb")
-        lists = [load_list(p1, "places0")]
-        xs_table = keep.tile([P, T], U8, name="xs_table", align_bytes=64)
-        nc.gpsimd.memset(xs_table[:, :ZEROED_BY_GPSIMD].bitcast(I32), 0)
-        nc.vector.memset(xs_table[:, ZEROED_BY_GPSIMD:].bitcast(I32), 0)
-        nc.sync.dma_start(out=xs_table[0:P:SPREAD, :].bitcast(I32), in_=x_scales[0].bitcast(I32))
         xw_table = keep.tile([P, T], U32, name="xw_table", align_bytes=64)
         nc.sync.dma_start(out=xw_table[:].bitcast(I32), in_=as_words(x_words))
+        lists = [load_list(p1, "places0")]
         w1_raw = keep.tile([P, PACK, H], F32, name="w1_raw")
         nc.sync.dma_start(out=w1_raw[:], in_=w1.rearrange("(p j) c -> p j c", j=PACK))
-        w23_raw = keep.tile([P, 2, N], I32, name="w23_raw")
+        w23_raw = keep.tile([P, 2, N], I32, name="w23_raw", tag="w23_raw", align_bytes=64)
         nc.sync.dma_start(out=w23_raw[:, 0, :], in_=as_words(w2_words))
 
         picked = keep.tile([P, S + V], U8, name="picked", align_bytes=64)
@@ -93,8 +93,11 @@ def tile_picked_gatehead_none_po_kernel(
         nc.vector.tensor_copy(out=picked[:, S:], in_=xs_table[:].indirect(own_sb[:]))
         x_plane = keep.tile([P, S + V], U8, name="x_plane", align_bytes=64)
         nc.vector.memset(x_plane[:].bitcast(I32), 0)
-        for r in range(4):
-            nc.sync.dma_start(out=x_plane[r:P:32, :].bitcast(I32), in_=picked[SPREAD * r : P : 32, :].bitcast(I32))
+        for q in range(QUADRANTS):
+            nc.sync.dma_start(
+                out=x_plane[32 * q : 32 * q + 4, :].bitcast(I32),
+                in_=picked[XS_ROW + 4 * q : XS_ROW + 4 * q + 4, :].bitcast(I32),
+            )
         xq_scales, xo_scales = x_plane[:, :S], x_plane[:, S:]
 
         w23s_raw = keep.tile([P, N], U8, name="w23s_raw", tag="later_terms")
@@ -116,44 +119,61 @@ def tile_picked_gatehead_none_po_kernel(
             nc.vector.tensor_copy(out=tile[:], in_=xw_table[:].indirect(offsets))
             return tile
 
-        half_list = V // GROUP // 2
         xq_words = pick_words(offs_sb[:], "xq_words", "xq_words")
+        half_list = V // GROUP // 2
         xo_words = [pick_words(own_sb[:, :half_list], "xo_words0", "xo_words0")]
 
         w1_view = w1_raw[:].rearrange("p j (g h i u e) -> p u h g i j e", g=HEADS, h=2, u=2, e=2)
-        w1_codes = keep.tile([P, H], U32, name="w1_codes", align_bytes=64)
         w1_scales = keep.tile([P, H], U8, name="w1_scales", align_bytes=64)
         y = [
-            keep.tile([P, 2 * S if t < WHOLE_TILES else S], F32, name=f"y{t}", align_bytes=64) for t in range(TILES)
+            keep.tile([P, 2 * S if t < WHOLE_TILES else S], F32, name=f"y{t}", tag=f"y{t}", align_bytes=64)
+            for t in range(TILES)
         ]
         nc.vector.memset(y[0][:, S:], 0.0)
         nc.scalar.copy(out=y[1][:, S:], in_=y[0][:, S:])
-        for t in range(TILES):
-            cols = slice(t * P, (t + 1) * P)
-            w1_bf = keep.tile([P, P * PACK], BF16, name=f"w1_bf{t}", tag=f"w1_bf{t}", align_bytes=64)
-            cast = nc.vector.tensor_copy if t == 0 else nc.scalar.copy
-            cast(
-                out=w1_bf[:].rearrange("p (g i e j) -> p g i j e", g=HEADS, e=2, j=PACK),
-                in_=w1_view[:, t // 2, t % 2],
-            )
-            nc.vector.quantize_mx(out=w1_codes[:, cols].bitcast(FP8X4), scales=w1_scales[:, cols], in_=w1_bf[:])
-            parts = 2 if t == 0 else 1
-            for k in range(parts):
-                part = slice(k * S // parts, (k + 1) * S // parts)
-                acc = bank(t + TILES * k, [P, S // parts], "y_acc")
-                nc.tensor.matmul_mx(
-                    out=acc[:], lhsT=w1_codes[:, cols].bitcast(FP8X4), lhsT_scale=w1_scales[:, cols],
-                    rhs=xq_words[:, part].bitcast(FP8X4), rhs_scale=xq_scales[:, part], start=True, stop=True,
+
+        def round_w1(tiles, tag):
+            tile = keep.tile([P, len(tiles) * P * PACK], BF16, name=f"w1_bf{tiles[0]}", tag=tag, align_bytes=64)
+            for k, t in enumerate(tiles):
+                out = tile[:, k * P * PACK : (k + 1) * P * PACK].rearrange(
+                    "p (g i e j) -> p g i j e", g=HEADS, e=2, j=PACK
                 )
-                nc.scalar.copy(out=y[t][:, part], in_=acc[:])
-            if t == 0:
-                xo_words.append(pick_words(own_sb[:, half_list:], "xo_words1", "w1_bf0"))
+                in_ = w1_view[:, t // 2, t % 2]
+                if t == 0:
+                    nc.scalar.copy(out=out[:, :SCALAR_HEADS], in_=in_[:, :SCALAR_HEADS])
+                    nc.vector.tensor_copy(out=out[:, SCALAR_HEADS:], in_=in_[:, SCALAR_HEADS:])
+                else:
+                    nc.scalar.copy(out=out, in_=in_)
+            return tile
+
+        def make_y(tiles, w1_bf, tag):
+            codes = keep.tile([P, len(tiles) * P], U32, name=f"w1_codes{tiles[0]}", tag=tag, align_bytes=64)
+            scales = w1_scales[:, tiles[0] * P : (tiles[-1] + 1) * P]
+            nc.vector.quantize_mx(out=codes[:].bitcast(FP8X4), scales=scales, in_=w1_bf[:])
+            for k, t in enumerate(tiles):
+                cols = slice(k * P, (k + 1) * P)
+                parts = len(Y0_BANKS) if t == 0 else 1
+                for h in range(parts):
+                    part = slice(h * S // parts, (h + 1) * S // parts)
+                    acc = bank(Y0_BANKS[h] if t == 0 else t, [P, S // parts], "y_acc")
+                    nc.tensor.matmul_mx(
+                        out=acc[:], lhsT=codes[:, cols].bitcast(FP8X4), lhsT_scale=scales[:, cols],
+                        rhs=xq_words[:, part].bitcast(FP8X4), rhs_scale=xq_scales[:, part], start=True, stop=True,
+                    )
+                    nc.scalar.copy(out=y[t][:, part], in_=acc[:])
+
+        make_y((0,), round_w1((0,), "w1_bf0"), "w1_codes0")
+        xo_words.append(pick_words(own_sb[:, half_list:], "xo_words1", "w1_bf0"))
+        make_y((1,), round_w1((1,), "w1_bf1"), "w1_codes1")
+        make_y((2,), round_w1((2,), "w1_bf2"), "w1_codes2")
 
         w23 = keep.tile([P, TILES, 2 * P], I32, name="w23", align_bytes=64)
         nc.vector.tensor_copy(
             out=w23[:].rearrange("p (s e) (c i) -> p c s i e", e=2, i=4),
             in_=w23_raw[:].rearrange("p w (c i s e) -> p (w c) s i e", s=2, e=2, i=4),
         )
+
+        make_y((3,), round_w1((3,), "w23_raw"), "w1_codes3")
 
         zt_bf = [keep.tile([P, H], BF16, name=f"zt_bf{b}", tag=f"zt_bf{b}", align_bytes=64) for b in range(STRIPS)]
         sums = {}

@@ -33,8 +33,9 @@ WIDE = LAST * STRIP
 SCALAR_HEADS = 2
 Y0_BANKS = (0, 4, 5, 6)
 
-SUM_BANKS = ((4, 5, 6, 7), (4, 5, 6, 7), (4, 5, 6, 4), (2, 3, 7, 7))
-O_BANKS = ((5,), (7,), (2,), (3, 0))
+SUM_BANKS = ((4, 5, 6, 7), (4, 5, 6, 7), (4, 5, 6, 2), (2, 3, 7, 7))
+BACK_PLACES = ((0, 0), (1, 0), (1, 1), (0, 1))
+O_BANKS = ((5,), (7,), (4,), (3, 6))
 
 
 def load_scale_rows(nc, plane, rows, first):
@@ -77,7 +78,7 @@ def tile_picked_gatehead_none_po_kernel(
 
         xs_table = keep.tile([P, T], U8, name="xs_table", tag="xs_table", align_bytes=64)
         nc.vector.memset(xs_table[0:XS_ROW, :].bitcast(I32), 0)
-        nc.sync.dma_start(out=xs_table[XS_ROW:P, :].bitcast(I32), in_=x_scales[0].bitcast(I32))
+        nc.scalar.dma_start(out=xs_table[XS_ROW:P, :].bitcast(I32), in_=x_scales[0].bitcast(I32))
         offs_sb = load_list(offs, "offs_sb")
         own_sb = load_list(own, "own_sb")
         xw_table = keep.tile([P, T], U32, name="xw_table", align_bytes=64)
@@ -220,16 +221,17 @@ def tile_picked_gatehead_none_po_kernel(
         o = {}
 
         def turn_back(b, u):
-            if u == 0 and b % 2 == 0:
-                back[b // 2] = bank(b // 2, [P, 2, 2, STRIP], "back")
+            number, place = BACK_PLACES[b]
+            if u == 0 and place == 0:
+                back[number] = bank(number, [P, 2, 2, STRIP], "back")
             words = zt_bf[b][:].bitcast(F32)
-            nc.tensor.transpose(back[b // 2][:, b % 2, u, :], words[:, u * P : (u + 1) * P], ident[:])
+            nc.tensor.transpose(back[number][:, place, u, :], words[:, u * P : (u + 1) * P], ident[:])
 
         def interleave(b, copy):
             tile = keep.tile([P, STRIP * PACK], BF16, name=f"z_bf{b}", align_bytes=64)
             copy(
                 out=tile[:].bitcast(F32).rearrange("p (v u) -> p v u", u=2),
-                in_=back[b // 2][:, b % 2].rearrange("p u v -> p v u"),
+                in_=back[BACK_PLACES[b][0]][:, BACK_PLACES[b][1]].rearrange("p u v -> p v u"),
             )
             return tile
 

@@ -38,9 +38,9 @@ BACK_PLACES = ((0, 0), (1, 0), (1, 1), (0, 1))
 O_BANKS = ((5,), (7,), (4,), (3, 6))
 
 
-def load_scale_rows(nc, plane, rows, first):
+def load_scale_rows(queue, plane, rows, first):
     for q in range(QUADRANTS):
-        nc.sync.dma_start(
+        queue.dma_start(
             out=plane[32 * q + first : 32 * q + first + 4, :].bitcast(I32),
             in_=rows[4 * q : 4 * q + 4, :].bitcast(I32),
         )
@@ -79,6 +79,10 @@ def tile_picked_gatehead_none_po_kernel(
         xs_table = keep.tile([P, T], U8, name="xs_table", tag="xs_table", align_bytes=64)
         nc.vector.memset(xs_table[0:XS_ROW, :].bitcast(I32), 0)
         nc.scalar.dma_start(out=xs_table[XS_ROW:P, :].bitcast(I32), in_=x_scales[0].bitcast(I32))
+        w23s_raw = keep.tile([P, N], U8, name="w23s_raw")
+        nc.vector.memset(w23s_raw[0 : P - 32, :].bitcast(I32), 0)
+        nc.scalar.dma_start(out=w23s_raw[P - 32 : P - 16, :].bitcast(I32), in_=w2_scales[0].bitcast(I32))
+        nc.scalar.dma_start(out=w23s_raw[P - 16 : P, :].bitcast(I32), in_=w3_scales[0].bitcast(I32))
         offs_sb = load_list(offs, "offs_sb")
         own_sb = load_list(own, "own_sb")
         xw_table = keep.tile([P, T], U32, name="xw_table", align_bytes=64)
@@ -101,19 +105,25 @@ def tile_picked_gatehead_none_po_kernel(
             )
         xq_scales, xo_scales = x_plane[:, :S], x_plane[:, S:]
 
-        w23s_raw = keep.tile([P, N], U8, name="w23s_raw", tag="later_terms")
-        nc.vector.memset(w23s_raw[:].bitcast(I32), 0)
         nc.sync.dma_start(out=w23_raw[:, 1, :], in_=as_words(w3_words))
         weights = [load_weight(a1, "weight0")]
         lists.append(load_list(p2, "places1"))
         weights.append(load_weight(a2, "weight1"))
-        load_scale_rows(nc, w23s_raw, w2_scales[0], 0)
         lists.append(load_list(p3, "places2"))
         weights.append(load_weight(a3, "weight2"))
-        load_scale_rows(nc, w23s_raw, w3_scales[0], W3_ROW)
 
         ident = keep.tile([P, P], F32, name="ident")
         make_identity(nc, ident[:])
+
+        w23s_dealt = keep.tile([P, N], U8, name="w23s_dealt", tag="later_terms")
+        nc.vector.tensor_copy(
+            out=w23s_dealt[:].rearrange("p (t m) -> p t m", t=TILES),
+            in_=w23s_raw[:].rearrange("p (m t) -> p t m", t=TILES),
+        )
+        w23s = keep.tile([P, N], U8, name="w23s", align_bytes=64)
+        nc.vector.memset(w23s[:].bitcast(I32), 0)
+        load_scale_rows(nc.sync, w23s, w23s_dealt[P - 32 : P - 16, :], 0)
+        load_scale_rows(nc.sync, w23s, w23s_dealt[P - 16 : P, :], W3_ROW)
 
         def pick_words(offsets, name, tag):
             tile = keep.tile([P, GROUP * offsets.shape[1]], U32, name=name, tag=tag, align_bytes=64)
@@ -131,7 +141,7 @@ def tile_picked_gatehead_none_po_kernel(
             for t in range(TILES)
         ]
         nc.vector.memset(y[0][:, S:], 0.0)
-        nc.scalar.copy(out=y[1][:, S:], in_=y[0][:, S:])
+        nc.scalar.activation(out=y[1][:, S:], in_=y[0][:, S:], func=SIGMOID)
 
         def round_w1(tiles, tag):
             tile = keep.tile([P, len(tiles) * P * PACK], BF16, name=f"w1_bf{tiles[0]}", tag=tag, align_bytes=64)
@@ -274,11 +284,6 @@ def tile_picked_gatehead_none_po_kernel(
         first_terms = keep.tile([P, POINTS * V], F32, name="first_terms")
         look_ups(0, V, (0,), first_terms)
 
-        w23s = keep.tile([P, N], U8, name="w23s", align_bytes=64)
-        nc.vector.tensor_copy(
-            out=w23s[:].rearrange("p (t m) -> p t m", t=TILES),
-            in_=w23s_raw[:].rearrange("p (m t) -> p t m", t=TILES),
-        )
         wide_at = POINTS * V
         last_at = wide_at + 2 * POINTS * WIDE
         later_terms = keep.tile([P, last_at + 2 * POINTS * STRIP], F32, name="later_terms", tag="later_terms")

@@ -15,6 +15,7 @@ U8 = mybir.dt.uint8
 FP8X4 = mybir.dt.float8_e4m3fn_x4
 MULT = mybir.AluOpType.mult
 SIGMOID = mybir.ActivationFunctionType.Sigmoid
+COPY = mybir.ActivationFunctionType.Copy
 
 P = 128
 PACK = 4
@@ -31,11 +32,13 @@ LAST = STRIPS - 1
 WHOLE_TILES = 2
 WIDE = LAST * STRIP
 SCALAR_HEADS = 2
+Y_WIDTH = (2 * S, 2 * S, S, 2 * WIDE)
 Y0_BANKS = (0, 4, 5, 6)
 
-SUM_BANKS = ((4, 5, 6, 7), (4, 5, 6, 7), (4, 5, 6, 2), (2, 3, 7, 7))
-BACK_PLACES = ((0, 0), (1, 0), (1, 1), (0, 1))
-O_BANKS = ((5,), (7,), (4,), (3, 6))
+SUM_BANKS = (4, 5, 6, 7)
+LAST_SUM_BANK = 7
+BACK_PLACES = ((4, 0), (5, 0), (5, 1), (4, 1))
+O_BANKS = ((0,), (1,), (6,), (7, 2))
 
 
 def load_scale_rows(queue, plane, rows, first):
@@ -79,19 +82,17 @@ def tile_picked_gatehead_none_po_kernel(
         xs_table = keep.tile([P, T], U8, name="xs_table", tag="xs_table", align_bytes=64)
         nc.vector.memset(xs_table[0:XS_ROW, :].bitcast(I32), 0)
         nc.scalar.dma_start(out=xs_table[XS_ROW:P, :].bitcast(I32), in_=x_scales[0].bitcast(I32))
-        w23s_raw = keep.tile([P, N], U8, name="w23s_raw")
-        nc.vector.memset(w23s_raw[0 : P - 32, :].bitcast(I32), 0)
-        nc.scalar.dma_start(out=w23s_raw[P - 32 : P - 16, :].bitcast(I32), in_=w2_scales[0].bitcast(I32))
-        nc.scalar.dma_start(out=w23s_raw[P - 16 : P, :].bitcast(I32), in_=w3_scales[0].bitcast(I32))
+        w23s_raw = keep.tile([P, 2 * N], U8, name="w23s_raw", align_bytes=64)
+        nc.vector.memset(w23s_raw[0:XS_ROW, :].bitcast(I32), 0)
+        nc.scalar.dma_start(out=w23s_raw[XS_ROW:P, :N].bitcast(I32), in_=w2_scales[0].bitcast(I32))
+        nc.scalar.dma_start(out=w23s_raw[XS_ROW:P, N:].bitcast(I32), in_=w3_scales[0].bitcast(I32))
         offs_sb = load_list(offs, "offs_sb")
         own_sb = load_list(own, "own_sb")
-        xw_table = keep.tile([P, T], U32, name="xw_table", align_bytes=64)
-        nc.sync.dma_start(out=xw_table[:].bitcast(I32), in_=as_words(x_words))
-        lists = [load_list(p1, "places0")]
         w1_raw = keep.tile([P, PACK, H], F32, name="w1_raw")
         nc.sync.dma_start(out=w1_raw[:], in_=w1.rearrange("(p j) c -> p j c", j=PACK))
-        w23_raw = keep.tile([P, 2, N], I32, name="w23_raw", tag="w23_raw", align_bytes=64)
-        nc.sync.dma_start(out=w23_raw[:, 0, :], in_=as_words(w2_words))
+        lists = [load_list(p1, "places0")]
+        xw_table = keep.tile([P, T], U32, name="xw_table", align_bytes=64)
+        nc.sync.dma_start(out=xw_table[:].bitcast(I32), in_=as_words(x_words))
 
         picked = keep.tile([P, S + V], U8, name="picked", align_bytes=64)
         nc.vector.tensor_copy(out=picked[:, :S], in_=xs_table[:].indirect(offs_sb[:]))
@@ -105,6 +106,8 @@ def tile_picked_gatehead_none_po_kernel(
             )
         xq_scales, xo_scales = x_plane[:, :S], x_plane[:, S:]
 
+        w23_raw = keep.tile([P, 2, N], I32, name="w23_raw", tag="w23_raw", align_bytes=64)
+        nc.sync.dma_start(out=w23_raw[:, 0, :], in_=as_words(w2_words))
         nc.sync.dma_start(out=w23_raw[:, 1, :], in_=as_words(w3_words))
         weights = [load_weight(a1, "weight0")]
         lists.append(load_list(p2, "places1"))
@@ -115,68 +118,57 @@ def tile_picked_gatehead_none_po_kernel(
         ident = keep.tile([P, P], F32, name="ident")
         make_identity(nc, ident[:])
 
-        w23s_dealt = keep.tile([P, N], U8, name="w23s_dealt", tag="later_terms")
+        w23s_dealt = keep.tile([P, 2 * N], U8, name="w23s_dealt", align_bytes=64)
         nc.vector.tensor_copy(
-            out=w23s_dealt[:].rearrange("p (t m) -> p t m", t=TILES),
-            in_=w23s_raw[:].rearrange("p (m t) -> p t m", t=TILES),
+            out=w23s_dealt[:].rearrange("p (w t m) -> p w t m", w=2, t=TILES),
+            in_=w23s_raw[:].rearrange("p (w m t) -> p w t m", w=2, t=TILES),
         )
-        w23s = keep.tile([P, N], U8, name="w23s", align_bytes=64)
+        w23s = keep.tile([P, 2 * N], U8, name="w23s", align_bytes=64)
         nc.vector.memset(w23s[:].bitcast(I32), 0)
-        load_scale_rows(nc.sync, w23s, w23s_dealt[P - 32 : P - 16, :], 0)
-        load_scale_rows(nc.sync, w23s, w23s_dealt[P - 16 : P, :], W3_ROW)
-
-        def pick_words(offsets, name, tag):
-            tile = keep.tile([P, GROUP * offsets.shape[1]], U32, name=name, tag=tag, align_bytes=64)
-            nc.vector.tensor_copy(out=tile[:], in_=xw_table[:].indirect(offsets))
-            return tile
-
-        xq_words = pick_words(offs_sb[:], "xq_words", "xq_words")
-        half_list = V // GROUP // 2
-        xo_words = [pick_words(own_sb[:, :half_list], "xo_words0", "xo_words0")]
+        load_scale_rows(nc.sync, w23s, w23s_dealt[XS_ROW:P, :], 0)
 
         w1_view = w1_raw[:].rearrange("p j (g h i u e) -> p u h g i j e", g=HEADS, h=2, u=2, e=2)
         w1_scales = keep.tile([P, H], U8, name="w1_scales", align_bytes=64)
-        y = [
-            keep.tile([P, 2 * S if t < WHOLE_TILES else S], F32, name=f"y{t}", tag=f"y{t}", align_bytes=64)
-            for t in range(TILES)
-        ]
+        w1_codes = keep.tile([P, H], U32, name="w1_codes", align_bytes=64)
+        y = [keep.tile([P, Y_WIDTH[t]], F32, name=f"y{t}", tag=f"y{t}", align_bytes=64) for t in range(TILES)]
         nc.vector.memset(y[0][:, S:], 0.0)
+        nc.vector.memset(y[3][:, S:], 0.0)
         nc.scalar.activation(out=y[1][:, S:], in_=y[0][:, S:], func=SIGMOID)
 
-        def round_w1(tiles, tag):
-            tile = keep.tile([P, len(tiles) * P * PACK], BF16, name=f"w1_bf{tiles[0]}", tag=tag, align_bytes=64)
-            for k, t in enumerate(tiles):
-                out = tile[:, k * P * PACK : (k + 1) * P * PACK].rearrange(
-                    "p (g i e j) -> p g i j e", g=HEADS, e=2, j=PACK
+        for u in range(2):
+            w1_bf = keep.tile([P, 2 * P * PACK], BF16, name=f"w1_bf{u}", align_bytes=64)
+            for h in range(2):
+                cast = nc.vector.tensor_copy if (u, h) == (1, 1) else nc.scalar.copy
+                cast(
+                    out=w1_bf[:, h * P * PACK : (h + 1) * P * PACK].rearrange(
+                        "p (g i e j) -> p g i j e", g=HEADS, e=2, j=PACK
+                    ),
+                    in_=w1_view[:, u, h],
                 )
-                in_ = w1_view[:, t // 2, t % 2]
-                if t == 0:
-                    nc.scalar.copy(out=out[:, :SCALAR_HEADS], in_=in_[:, :SCALAR_HEADS])
-                    nc.vector.tensor_copy(out=out[:, SCALAR_HEADS:], in_=in_[:, SCALAR_HEADS:])
-                else:
-                    nc.scalar.copy(out=out, in_=in_)
-            return tile
+            cols = slice(2 * u * P, 2 * (u + 1) * P)
+            nc.vector.quantize_mx(out=w1_codes[:, cols].bitcast(FP8X4), scales=w1_scales[:, cols], in_=w1_bf[:])
 
-        def make_y(tiles, w1_bf, tag):
-            codes = keep.tile([P, len(tiles) * P], U32, name=f"w1_codes{tiles[0]}", tag=tag, align_bytes=64)
-            scales = w1_scales[:, tiles[0] * P : (tiles[-1] + 1) * P]
-            nc.vector.quantize_mx(out=codes[:].bitcast(FP8X4), scales=scales, in_=w1_bf[:])
-            for k, t in enumerate(tiles):
-                cols = slice(k * P, (k + 1) * P)
-                parts = len(Y0_BANKS) if t == 0 else 1
-                for h in range(parts):
-                    part = slice(h * S // parts, (h + 1) * S // parts)
-                    acc = bank(Y0_BANKS[h] if t == 0 else t, [P, S // parts], "y_acc")
-                    nc.tensor.matmul_mx(
-                        out=acc[:], lhsT=codes[:, cols].bitcast(FP8X4), lhsT_scale=scales[:, cols],
-                        rhs=xq_words[:, part].bitcast(FP8X4), rhs_scale=xq_scales[:, part], start=True, stop=True,
-                    )
-                    nc.scalar.copy(out=y[t][:, part], in_=acc[:])
+        xq_words = keep.tile([P, S], U32, name="xq_words", align_bytes=64)
+        xo_words = keep.tile([P, V], U32, name="xo_words", align_bytes=64)
 
-        make_y((0,), round_w1((0,), "w1_bf0"), "w1_codes0")
-        xo_words.append(pick_words(own_sb[:, half_list:], "xo_words1", "w1_bf0"))
-        make_y((1,), round_w1((1,), "w1_bf1"), "w1_codes1")
-        make_y((2,), round_w1((2,), "w1_bf2"), "w1_codes2")
+        def make_y(t, part, number):
+            cols = slice(t * P, (t + 1) * P)
+            acc = bank(number, [P, part.stop - part.start], "y_acc")
+            nc.tensor.matmul_mx(
+                out=acc[:], lhsT=w1_codes[:, cols].bitcast(FP8X4), lhsT_scale=w1_scales[:, cols],
+                rhs=xq_words[:, part].bitcast(FP8X4), rhs_scale=xq_scales[:, part], start=True, stop=True,
+            )
+            nc.scalar.copy(out=y[t][:, part], in_=acc[:])
+
+        for k in range(2):
+            part = slice(k * S // 2, (k + 1) * S // 2)
+            offsets = offs_sb[:, part.start // GROUP : part.stop // GROUP]
+            nc.vector.tensor_copy(out=xq_words[:, part], in_=xw_table[:].indirect(offsets))
+            for t in range(2):
+                make_y(t, part, 4 * k + t)
+        for t in range(2, TILES):
+            make_y(t, slice(0, S), t)
+        nc.vector.tensor_copy(out=xo_words[:], in_=xw_table[:].indirect(own_sb[:]))
 
         w23 = keep.tile([P, TILES, 2 * P], I32, name="w23", align_bytes=64)
         nc.vector.tensor_copy(
@@ -184,43 +176,56 @@ def tile_picked_gatehead_none_po_kernel(
             in_=w23_raw[:].rearrange("p w (c i s e) -> p (w c) s i e", s=2, e=2, i=4),
         )
 
-        make_y((3,), round_w1((3,), "w23_raw"), "w1_codes3")
-
-        zt_bf = [keep.tile([P, H], BF16, name=f"zt_bf{b}", tag=f"zt_bf{b}", align_bytes=64) for b in range(STRIPS)]
+        zt = [
+            keep.tile([P, STRIPS, H // 2], BF16, name="zt0", align_bytes=64),
+            keep.tile([P, LAST, H // 2], BF16, name="zt1", tag="zt1", align_bytes=64),
+        ]
+        zt_last = keep.tile([P, 1, H // 2], BF16, name="zt_last", tag="zt_last", align_bytes=64)
         sums = {}
 
-        def look_up(v0, width, t, n, term):
-            u, h = divmod(t, 2)
-            together = t < WHOLE_TILES
-            nc.vector.tensor_tensor(
-                out=term,
-                in0=y[t][:].indirect(lists[n][:, v0 // GROUP : (v0 + width) // GROUP]),
-                in1=weights[n][:, v0 : v0 + width],
-                op=MULT,
-            )
-            for b in range(v0 // STRIP, (v0 + width) // STRIP):
-                if n == 0 and not (together and h == 1):
-                    sums[b] = bank(SUM_BANKS[t][b], [P, 2, P], "z_sum")
-                c0 = b * STRIP - v0
+        def fetch(v0, width, t, n, tag):
+            term = keep.tile([P, width], F32, name=f"term{t}{n}", tag=tag)
+            offsets = lists[n][:, v0 // GROUP : (v0 + width) // GROUP]
+            nc.scalar.activation(out=term[:], in_=y[t][:].indirect(offsets), func=COPY)
+            return term
+
+        def add_term(v0, width, t, n, tag, fetched=None):
+            if fetched is None:
+                term = keep.tile([P, width], F32, name=f"term{t}{n}{v0}", tag=tag)
+                in0 = y[t][:].indirect(lists[n][:, v0 // GROUP : (v0 + width) // GROUP])
+            else:
+                term = fetched
+                in0 = fetched[:]
+            nc.vector.tensor_tensor(out=term[:], in0=in0, in1=weights[n][:, v0 : v0 + width], op=MULT)
+            strips = width // STRIP
+            if v0 == 0:
+                if n == 0:
+                    sums[t] = bank(SUM_BANKS[t], [P, strips, P], "z_sum")
+                for b in range(strips):
+                    nc.tensor.matmul(
+                        sums[t][:, b, :], lhsT=term[:, b * STRIP : (b + 1) * STRIP], rhs=ident[:],
+                        start=(n == 0 and b == 0), stop=(n == POINTS - 1 and b == strips - 1), is_transpose=True,
+                    )
+                if n == POINTS - 1:
+                    u, h = divmod(t, 2)
+                    nc.scalar.copy(
+                        out=zt[u][:].rearrange("v b (g h r) -> v b g h r", g=HEADS, h=2)[:, :, :, h, :],
+                        in_=sums[t][:].rearrange("v b (g r) -> v b g r", g=HEADS),
+                    )
+            else:
+                h = t % 2
+                if n == 0 and h == 0:
+                    sums["last"] = bank(LAST_SUM_BANK, [P, 2, P], "z_sum")
                 nc.tensor.matmul(
-                    sums[b][:, h, :], lhsT=term[:, c0 : c0 + STRIP], rhs=ident[:],
+                    sums["last"][:, h, :], lhsT=term[:], rhs=ident[:],
                     start=(n == 0), stop=(n == POINTS - 1), is_transpose=True,
                 )
-                if n == POINTS - 1 and not (together and h == 0):
-                    done = slice(0, 2) if together else slice(h, h + 1)
+                if n == POINTS - 1 and h == 1:
                     nc.scalar.copy(
-                        out=zt_bf[b][:].rearrange("v (u g h r) -> v u g h r", u=2, g=HEADS, h=2)[:, u, :, done, :],
-                        in_=sums[b][:].rearrange("v h (g r) -> v g h r", g=HEADS)[:, :, done, :],
+                        out=zt_last[:, 0, :].rearrange("v (g h r) -> v g h r", g=HEADS, h=2),
+                        in_=sums["last"][:].rearrange("v h (g r) -> v g h r", g=HEADS),
                     )
 
-        def look_ups(v0, width, tiles, room):
-            at = 0
-            for t in tiles:
-                for n in range(POINTS):
-                    look_up(v0, width, t, n, room[:, at : at + width])
-                    at = at + width
-
-        gate = keep.tile([P, TILES, V], F32, name="gate")
         z_scales = keep.tile([P, V], U8, name="z_scales", align_bytes=64)
         out_codes = keep.tile([P, V], U32, name="out_codes", align_bytes=64)
         out_scales = keep.tile([P, V], U8, name="out_scales", align_bytes=64)
@@ -229,13 +234,29 @@ def tile_picked_gatehead_none_po_kernel(
         out_words = as_words(out_1)
         back = {}
         o = {}
+        gate_acc = {}
+        gate = {}
+
+        def gate_product(b):
+            cols = queries(b, b)
+            gate_acc[b] = bank(b, [P, TILES, STRIP], "gate_acc")
+            for t in range(TILES):
+                nc.tensor.matmul_mx(
+                    out=gate_acc[b][:, t, :],
+                    lhsT=w23[:, t, P:].bitcast(FP8X4), lhsT_scale=w23s[:, N + t * P : N + (t + 1) * P],
+                    rhs=xo_words[:, cols].bitcast(FP8X4), rhs_scale=xo_scales[:, cols], start=True, stop=True,
+                )
+
+        def gate_sigmoid(b, tag):
+            gate[b] = keep.tile([P, TILES, STRIP], F32, name=f"gate{b}", tag=tag)
+            nc.scalar.activation(out=gate[b][:], in_=gate_acc[b][:], func=SIGMOID)
 
         def turn_back(b, u):
             number, place = BACK_PLACES[b]
             if u == 0 and place == 0:
                 back[number] = bank(number, [P, 2, 2, STRIP], "back")
-            words = zt_bf[b][:].bitcast(F32)
-            nc.tensor.transpose(back[number][:, place, u, :], words[:, u * P : (u + 1) * P], ident[:])
+            source = zt_last[:, 0, :] if (b == LAST and u == 1) else zt[u][:, b, :]
+            nc.tensor.transpose(back[number][:, place, u, :], source.bitcast(F32), ident[:])
 
         def interleave(b, copy):
             tile = keep.tile([P, STRIP * PACK], BF16, name=f"z_bf{b}", align_bytes=64)
@@ -265,12 +286,14 @@ def tile_picked_gatehead_none_po_kernel(
             per_bank = TILES // len(o[b])
             for k, part in enumerate(o[b]):
                 rows = slice(k * per_bank, (k + 1) * per_bank)
-                nc.vector.tensor_tensor(out=res[:, rows, cols], in0=part[:], in1=gate[:, rows, cols], op=MULT)
+                nc.vector.tensor_tensor(
+                    out=res[:, rows, cols], in0=part[:], in1=gate[b][:, rows, :], op=MULT
+                )
             nc.sync.dma_start(out=out_rows[:, :, cols], in_=res[:, :, cols])
 
         def quantise_out(b, cast):
             cols = queries(b, b)
-            res_bf = keep.tile([P, STRIP * PACK], BF16, name=f"res_bf{b}", tag=f"zt_bf{LAST - b}", align_bytes=64)
+            res_bf = keep.tile([P, STRIP * PACK], BF16, name=f"res_bf{b}", tag="zt_last" if b == 0 else f"res_bf{b}", align_bytes=64)
             cast(
                 out=res_bf[:].rearrange("p (c e t) -> p c t e", e=2, t=TILES),
                 in_=res[:, :, cols].rearrange("p t (c e) -> p c t e", e=2),
@@ -281,35 +304,31 @@ def tile_picked_gatehead_none_po_kernel(
             cols = queries(first, last)
             nc.sync.dma_start(out=out_words[:, cols], in_=out_codes[:, cols].bitcast(I32))
 
-        first_terms = keep.tile([P, POINTS * V], F32, name="first_terms")
-        look_ups(0, V, (0,), first_terms)
-
-        wide_at = POINTS * V
-        last_at = wide_at + 2 * POINTS * WIDE
-        later_terms = keep.tile([P, last_at + 2 * POINTS * STRIP], F32, name="later_terms", tag="later_terms")
-
-        for t in range(TILES):
-            acc = bank(t, [P, V], "gate_acc")
-            for k in range(2):
-                half = slice(k * V // 2, (k + 1) * V // 2)
-                nc.tensor.matmul_mx(
-                    out=acc[:, half],
-                    lhsT=w23[:, t, P:].bitcast(FP8X4), lhsT_scale=w23s[W3_ROW:P, t * P : (t + 1) * P],
-                    rhs=xo_words[k][:].bitcast(FP8X4), rhs_scale=xo_scales[:, half], start=True, stop=True,
-                )
-            nc.scalar.activation(out=gate[:, t, :], in_=acc[:], func=SIGMOID)
-
-        look_ups(0, V, (1,), later_terms[:, :wide_at])
+        fetched1 = [fetch(0, V, 1, n, f"fetched1{n}") for n in range(POINTS)]
+        fetched3 = [fetch(0, WIDE, 3, n, f"fetched3{n}") for n in range(POINTS)]
+        for n in range(POINTS):
+            add_term(0, V, 0, n, f"room{n}")
+        for b in range(STRIPS):
+            gate_product(b)
+        for n in range(POINTS):
+            add_term(0, V, 1, n, None, fetched1[n])
+            add_term(0, WIDE, 2, n, f"room{n}")
+        for n in range(POINTS):
+            add_term(0, WIDE, 3, n, None, fetched3[n])
         for b in range(STRIPS):
             turn_back(b, 0)
-        look_ups(0, WIDE, (2, 3), later_terms[:, wide_at:last_at])
+        for b in range(2):
+            gate_sigmoid(b, f"gate{b}")
         for b in range(LAST):
             turn_back(b, 1)
-        z_bf = [interleave(b, nc.scalar.copy) for b in range(LAST - 1)]
-        look_ups(WIDE, STRIP, (2, 3), later_terms[:, last_at:])
-        z_bf.append(interleave(LAST - 1, nc.vector.tensor_copy))
+        z_bf = [interleave(b, nc.scalar.copy) for b in range(LAST)]
+        for t in (2, 3):
+            for n in range(POINTS):
+                add_term(WIDE, STRIP, t, n, f"fetched{2 * t - 3}{n}")
         turn_back(LAST, 1)
+        gate_sigmoid(2, "fetched32")
         z_bf.append(interleave(LAST, nc.scalar.copy))
+        gate_sigmoid(3, "fetched31")
         for b in range(LAST):
             project(b, z_bf[b])
         gate_and_store(0)

@@ -37,6 +37,8 @@ Y0_BANKS = (0, 4, 5, 6)
 
 SUM_BANKS = (4, 5, 6, 7)
 LAST_SUM_BANK = 7
+FETCHED = ((3, 0), (0, 1), (1, 1), (3, 1), (1, 2), (3, 2))
+TERMS = ((0, 0), (1, 0), (2, 0), (3, 0), (0, 1), (2, 1), (1, 1), (3, 1), (0, 2), (1, 2), (2, 2), (3, 2))
 BACK_PLACES = ((4, 0), (5, 0), (5, 1), (4, 1))
 O_BANKS = ((0,), (1,), (6,), (7, 2))
 
@@ -88,11 +90,13 @@ def tile_picked_gatehead_none_po_kernel(
         nc.scalar.dma_start(out=w23s_raw[XS_ROW:P, N:].bitcast(I32), in_=w3_scales[0].bitcast(I32))
         offs_sb = load_list(offs, "offs_sb")
         own_sb = load_list(own, "own_sb")
-        w1_raw = keep.tile([P, PACK, H], F32, name="w1_raw")
-        nc.sync.dma_start(out=w1_raw[:], in_=w1.rearrange("(p j) c -> p j c", j=PACK))
-        lists = [load_list(p1, "places0")]
         xw_table = keep.tile([P, T], U32, name="xw_table", align_bytes=64)
         nc.sync.dma_start(out=xw_table[:].bitcast(I32), in_=as_words(x_words))
+        w1_rows = w1.rearrange("(p j) c -> p j c", j=PACK)
+        w1_raw = []
+        for k in range(2):
+            w1_raw.append(keep.tile([P, PACK, H // 2], F32, name=f"w1_raw{k}"))
+            nc.sync.dma_start(out=w1_raw[k][:], in_=w1_rows[:, :, k * H // 2 : (k + 1) * H // 2])
 
         picked = keep.tile([P, S + V], U8, name="picked", align_bytes=64)
         nc.vector.tensor_copy(out=picked[:, :S], in_=xs_table[:].indirect(offs_sb[:]))
@@ -106,14 +110,13 @@ def tile_picked_gatehead_none_po_kernel(
             )
         xq_scales, xo_scales = x_plane[:, :S], x_plane[:, S:]
 
-        w23_raw = keep.tile([P, 2, N], I32, name="w23_raw", tag="w23_raw", align_bytes=64)
-        nc.sync.dma_start(out=w23_raw[:, 0, :], in_=as_words(w2_words))
-        nc.sync.dma_start(out=w23_raw[:, 1, :], in_=as_words(w3_words))
+        def load_words(packed, name):
+            tile = keep.tile([P, N], I32, name=name, align_bytes=64)
+            nc.sync.dma_start(out=tile[:], in_=as_words(packed))
+            return tile
+
+        w3_raw = load_words(w3_words, "w3_raw")
         weights = [load_weight(a1, "weight0")]
-        lists.append(load_list(p2, "places1"))
-        weights.append(load_weight(a2, "weight1"))
-        lists.append(load_list(p3, "places2"))
-        weights.append(load_weight(a3, "weight2"))
 
         ident = keep.tile([P, P], F32, name="ident")
         make_identity(nc, ident[:])
@@ -126,30 +129,53 @@ def tile_picked_gatehead_none_po_kernel(
         w23s = keep.tile([P, 2 * N], U8, name="w23s", align_bytes=64)
         nc.vector.memset(w23s[:].bitcast(I32), 0)
         load_scale_rows(nc.sync, w23s, w23s_dealt[XS_ROW:P, :], 0)
+        lists = [load_list(p1, "places0"), load_list(p2, "places1")]
+        weights.append(load_weight(a2, "weight1"))
+        lists.append(load_list(p3, "places2"))
+        weights.append(load_weight(a3, "weight2"))
+        w2_raw = load_words(w2_words, "w2_raw")
 
-        w1_view = w1_raw[:].rearrange("p j (g h i u e) -> p u h g i j e", g=HEADS, h=2, u=2, e=2)
+        xq_words = keep.tile([P, S], U32, name="xq_words", align_bytes=64)
+        nc.vector.tensor_copy(out=xq_words[:], in_=xw_table[:].indirect(offs_sb[:]))
+
+        def pick_own(k, tag):
+            tile = keep.tile([P, V // 2], U32, name=f"xo_words{k}", tag=tag, align_bytes=64)
+            half_list = V // GROUP // 2
+            nc.vector.tensor_copy(out=tile[:], in_=xw_table[:].indirect(own_sb[:, k * half_list : (k + 1) * half_list]))
+            return tile
+
+        xo_words = [pick_own(0, "xo_words0")]
+
         w1_scales = keep.tile([P, H], U8, name="w1_scales", align_bytes=64)
         w1_codes = keep.tile([P, H], U32, name="w1_codes", align_bytes=64)
         y = [keep.tile([P, Y_WIDTH[t]], F32, name=f"y{t}", tag=f"y{t}", align_bytes=64) for t in range(TILES)]
         nc.vector.memset(y[0][:, S:], 0.0)
         nc.vector.memset(y[3][:, S:], 0.0)
         nc.scalar.activation(out=y[1][:, S:], in_=y[0][:, S:], func=SIGMOID)
+        w1_bf0 = keep.tile([P, P * PACK], BF16, name="w1_bf0", tag="w1_bf0", align_bytes=64)
+        w1_bf_rest = keep.tile([P, (TILES - 1) * P * PACK], BF16, name="w1_bf_rest", align_bytes=64)
 
-        for u in range(2):
-            w1_bf = keep.tile([P, 2 * P * PACK], BF16, name=f"w1_bf{u}", align_bytes=64)
-            for h in range(2):
-                cast = nc.vector.tensor_copy if (u, h) == (1, 1) else nc.scalar.copy
-                cast(
-                    out=w1_bf[:, h * P * PACK : (h + 1) * P * PACK].rearrange(
-                        "p (g i e j) -> p g i j e", g=HEADS, e=2, j=PACK
-                    ),
-                    in_=w1_view[:, u, h],
-                )
-            cols = slice(2 * u * P, 2 * (u + 1) * P)
-            nc.vector.quantize_mx(out=w1_codes[:, cols].bitcast(FP8X4), scales=w1_scales[:, cols], in_=w1_bf[:])
+        def w1_bf(start, stop):
+            if start < P * PACK:
+                return w1_bf0[:, start:stop]
+            return w1_bf_rest[:, start - P * PACK : stop - P * PACK]
 
-        xq_words = keep.tile([P, S], U32, name="xq_words", align_bytes=64)
-        xo_words = keep.tile([P, V], U32, name="xo_words", align_bytes=64)
+        def round_w1(k, t, cast):
+            width = P * PACK // 2
+            at = (2 * t + k) * width
+            cast(
+                out=w1_bf(at, at + width).rearrange("p (g i e j) -> p g i j e", g=HEADS // 2, e=2, j=PACK),
+                in_=w1_raw[k][:].rearrange("p j (g h i u e) -> p u h g i j e", g=HEADS // 2, h=2, u=2, e=2)[
+                    :, t // 2, t % 2
+                ],
+            )
+
+        def quantise_w1(first, last):
+            cols = slice(first * P, (last + 1) * P)
+            nc.vector.quantize_mx(
+                out=w1_codes[:, cols].bitcast(FP8X4), scales=w1_scales[:, cols],
+                in_=w1_bf(cols.start * PACK, cols.stop * PACK),
+            )
 
         def make_y(t, part, number):
             cols = slice(t * P, (t + 1) * P)
@@ -160,38 +186,47 @@ def tile_picked_gatehead_none_po_kernel(
             )
             nc.scalar.copy(out=y[t][:, part], in_=acc[:])
 
+        for t in range(TILES):
+            round_w1(0, t, nc.scalar.copy)
+        for t in range(TILES):
+            round_w1(1, t, nc.vector.tensor_copy if t == 0 else nc.scalar.copy)
+        quantise_w1(0, 0)
         for k in range(2):
-            part = slice(k * S // 2, (k + 1) * S // 2)
-            offsets = offs_sb[:, part.start // GROUP : part.stop // GROUP]
-            nc.vector.tensor_copy(out=xq_words[:, part], in_=xw_table[:].indirect(offsets))
-            for t in range(2):
-                make_y(t, part, 4 * k + t)
+            make_y(0, slice(k * S // 2, (k + 1) * S // 2), 4 * k)
+        xo_words.append(pick_own(1, "w1_bf0"))
+        quantise_w1(1, 1)
+        make_y(1, slice(0, S), 1)
+        quantise_w1(2, 3)
         for t in range(2, TILES):
             make_y(t, slice(0, S), t)
-        nc.vector.tensor_copy(out=xo_words[:], in_=xw_table[:].indirect(own_sb[:]))
 
-        w23 = keep.tile([P, TILES, 2 * P], I32, name="w23", align_bytes=64)
-        nc.vector.tensor_copy(
-            out=w23[:].rearrange("p (s e) (c i) -> p c s i e", e=2, i=4),
-            in_=w23_raw[:].rearrange("p w (c i s e) -> p (w c) s i e", s=2, e=2, i=4),
-        )
+        def deal_words(raw, name):
+            tile = keep.tile([P, TILES, P], I32, name=name, align_bytes=64)
+            nc.vector.tensor_copy(
+                out=tile[:].rearrange("p (s e) (c i) -> p c s i e", e=2, i=4),
+                in_=raw[:].rearrange("p (c i s e) -> p c s i e", s=2, e=2, i=4),
+            )
+            return tile
+
+        w3_dealt = deal_words(w3_raw, "w3_dealt")
+        w2_dealt = deal_words(w2_raw, "w2_dealt")
 
         zt = [
-            keep.tile([P, STRIPS, H // 2], BF16, name="zt0", align_bytes=64),
+            keep.tile([P, STRIPS, H // 2], BF16, name="zt0", tag="zt0", align_bytes=64),
             keep.tile([P, LAST, H // 2], BF16, name="zt1", tag="zt1", align_bytes=64),
         ]
         zt_last = keep.tile([P, 1, H // 2], BF16, name="zt_last", tag="zt_last", align_bytes=64)
         sums = {}
 
         def fetch(v0, width, t, n, tag):
-            term = keep.tile([P, width], F32, name=f"term{t}{n}", tag=tag)
+            term = keep.tile([P, width], F32, name=f"term{t}{n}", tag=tag, align_bytes=64)
             offsets = lists[n][:, v0 // GROUP : (v0 + width) // GROUP]
             nc.scalar.activation(out=term[:], in_=y[t][:].indirect(offsets), func=COPY)
             return term
 
         def add_term(v0, width, t, n, tag, fetched=None):
             if fetched is None:
-                term = keep.tile([P, width], F32, name=f"term{t}{n}{v0}", tag=tag)
+                term = keep.tile([P, width], F32, name=f"term{t}{n}", tag=tag) if v0 == 0 else tag
                 in0 = y[t][:].indirect(lists[n][:, v0 // GROUP : (v0 + width) // GROUP])
             else:
                 term = fetched
@@ -243,12 +278,12 @@ def tile_picked_gatehead_none_po_kernel(
             for t in range(TILES):
                 nc.tensor.matmul_mx(
                     out=gate_acc[b][:, t, :],
-                    lhsT=w23[:, t, P:].bitcast(FP8X4), lhsT_scale=w23s[:, N + t * P : N + (t + 1) * P],
-                    rhs=xo_words[:, cols].bitcast(FP8X4), rhs_scale=xo_scales[:, cols], start=True, stop=True,
+                    lhsT=w3_dealt[:, t, :].bitcast(FP8X4), lhsT_scale=w23s[:, N + t * P : N + (t + 1) * P],
+                    rhs=xo_words[b // 2][:, queries(b % 2, b % 2)].bitcast(FP8X4), rhs_scale=xo_scales[:, cols], start=True, stop=True,
                 )
 
         def gate_sigmoid(b, tag):
-            gate[b] = keep.tile([P, TILES, STRIP], F32, name=f"gate{b}", tag=tag)
+            gate[b] = keep.tile([P, TILES, STRIP], F32, name=f"gate{b}", tag=tag, align_bytes=64) if b < 2 else tag
             nc.scalar.activation(out=gate[b][:], in_=gate_acc[b][:], func=SIGMOID)
 
         def turn_back(b, u):
@@ -277,7 +312,7 @@ def tile_picked_gatehead_none_po_kernel(
                     o[b].append(bank(O_BANKS[b][t // per_bank], [P, per_bank, STRIP], "o"))
                 nc.tensor.matmul_mx(
                     out=o[b][-1][:, t % per_bank, :],
-                    lhsT=w23[:, t, :P].bitcast(FP8X4), lhsT_scale=w23s[:, t * P : (t + 1) * P],
+                    lhsT=w2_dealt[:, t, :].bitcast(FP8X4), lhsT_scale=w23s[:, t * P : (t + 1) * P],
                     rhs=z_codes[:].bitcast(FP8X4), rhs_scale=z_scales[:, cols], start=True, stop=True,
                 )
 
@@ -304,31 +339,32 @@ def tile_picked_gatehead_none_po_kernel(
             cols = queries(first, last)
             nc.sync.dma_start(out=out_words[:, cols], in_=out_codes[:, cols].bitcast(I32))
 
-        fetched1 = [fetch(0, V, 1, n, f"fetched1{n}") for n in range(POINTS)]
-        fetched3 = [fetch(0, WIDE, 3, n, f"fetched3{n}") for n in range(POINTS)]
-        for n in range(POINTS):
-            add_term(0, V, 0, n, f"room{n}")
+        widths = (V, V, WIDE, WIDE)
         for b in range(STRIPS):
             gate_product(b)
-        for n in range(POINTS):
-            add_term(0, V, 1, n, None, fetched1[n])
-            add_term(0, WIDE, 2, n, f"room{n}")
-        for n in range(POINTS):
-            add_term(0, WIDE, 3, n, None, fetched3[n])
+        fetched = {}
+        for t, n in FETCHED:
+            fetched[t, n] = fetch(0, widths[t], t, n, f"room{t}{n}")
+        for t, n in TERMS:
+            if (t, n) == (0, POINTS - 1):
+                gate_sigmoid(0, "room31")
+            add_term(0, widths[t], t, n, f"room{t}{n}", fetched.get((t, n)))
         for b in range(STRIPS):
             turn_back(b, 0)
-        for b in range(2):
-            gate_sigmoid(b, f"gate{b}")
         for b in range(LAST):
             turn_back(b, 1)
-        z_bf = [interleave(b, nc.scalar.copy) for b in range(LAST)]
+        z_bf = [interleave(b, nc.scalar.copy) for b in range(LAST - 1)]
+        gate_sigmoid(1, "zt0")
+        z_bf.append(interleave(LAST - 1, nc.scalar.copy))
+        last_terms = keep.tile([P, 2, POINTS, STRIP], F32, name="last_terms", tag="room12", align_bytes=64)
         for t in (2, 3):
             for n in range(POINTS):
-                add_term(WIDE, STRIP, t, n, f"fetched{2 * t - 3}{n}")
+                add_term(WIDE, STRIP, t, n, last_terms[:, t - 2, n, :])
         turn_back(LAST, 1)
-        gate_sigmoid(2, "fetched32")
+        late_gates = keep.tile([P, 2, TILES, STRIP], F32, name="late_gates", tag="room12", align_bytes=64)
+        gate_sigmoid(2, late_gates[:, 0])
         z_bf.append(interleave(LAST, nc.scalar.copy))
-        gate_sigmoid(3, "fetched31")
+        gate_sigmoid(3, late_gates[:, 1])
         for b in range(LAST):
             project(b, z_bf[b])
         gate_and_store(0)

@@ -37,7 +37,7 @@ Y0_BANKS = (0, 4, 5, 6)
 
 SUM_BANKS = (4, 5, 6, 7)
 LAST_SUM_BANK = 7
-FETCHED = ((3, 0), (0, 1), (1, 1), (3, 1), (1, 2), (3, 2))
+FETCHED = ((3, 0), (1, 1), (3, 1), (1, 2), (3, 2))
 TERMS = ((0, 0), (1, 0), (2, 0), (3, 0), (0, 1), (2, 1), (1, 1), (3, 1), (0, 2), (1, 2), (2, 2), (3, 2))
 BACK_PLACES = ((4, 0), (5, 0), (5, 1), (4, 1))
 O_BANKS = ((0,), (1,), (6,), (7, 2))
@@ -122,7 +122,7 @@ def tile_picked_gatehead_none_po_kernel(
         make_identity(nc, ident[:])
 
         w23s_dealt = keep.tile([P, 2 * N], U8, name="w23s_dealt", align_bytes=64)
-        nc.vector.tensor_copy(
+        nc.gpsimd.tensor_copy(
             out=w23s_dealt[:].rearrange("p (w t m) -> p w t m", w=2, t=TILES),
             in_=w23s_raw[:].rearrange("p (w m t) -> p w t m", w=2, t=TILES),
         )
@@ -200,16 +200,15 @@ def tile_picked_gatehead_none_po_kernel(
         for t in range(2, TILES):
             make_y(t, slice(0, S), t)
 
-        def deal_words(raw, name):
-            tile = keep.tile([P, TILES, P], I32, name=name, align_bytes=64)
-            nc.vector.tensor_copy(
+        def deal_words(raw, name, copy):
+            tile = keep.tile([P, TILES, P], U32, name=name, align_bytes=64)
+            copy(
                 out=tile[:].rearrange("p (s e) (c i) -> p c s i e", e=2, i=4),
-                in_=raw[:].rearrange("p (c i s e) -> p c s i e", s=2, e=2, i=4),
+                in_=raw[:].bitcast(U32).rearrange("p (c i s e) -> p c s i e", s=2, e=2, i=4),
             )
             return tile
 
-        w3_dealt = deal_words(w3_raw, "w3_dealt")
-        w2_dealt = deal_words(w2_raw, "w2_dealt")
+        w3_dealt = deal_words(w3_raw, "w3_dealt", nc.vector.tensor_copy)
 
         zt = [
             keep.tile([P, STRIPS, H // 2], BF16, name="zt0", tag="zt0", align_bytes=64),
@@ -348,6 +347,7 @@ def tile_picked_gatehead_none_po_kernel(
         for t, n in TERMS:
             if (t, n) == (0, POINTS - 1):
                 gate_sigmoid(0, "room31")
+                w2_dealt = deal_words(w2_raw, "w2_dealt", nc.scalar.copy)
             add_term(0, widths[t], t, n, f"room{t}{n}", fetched.get((t, n)))
         for b in range(STRIPS):
             turn_back(b, 0)

@@ -32,13 +32,13 @@ LAST = STRIPS - 1
 WHOLE_TILES = 2
 WIDE = LAST * STRIP
 SCALAR_HEADS = 2
-Y_WIDTH = (2 * S, 2 * S, S, 2 * WIDE)
+Y_WIDTH = (2 * S, 2 * S, 2 * WIDE, 2 * WIDE)
 Y0_BANKS = (0, 4, 5, 6)
 
 SUM_BANKS = (4, 5, 6, 7)
 LAST_SUM_BANK = 7
-FETCHED = ((3, 0), (1, 1), (3, 1), (1, 2), (3, 2))
-TERMS = ((0, 0), (1, 0), (2, 0), (3, 0), (0, 1), (2, 1), (1, 1), (3, 1), (0, 2), (1, 2), (2, 2), (3, 2))
+FETCHED = ((1, 1), (2, 1), (3, 1), (1, 2), (3, 2))
+TERMS = ((0, 0), (1, 0), (2, 0), (3, 0), (0, 1), (1, 1), (2, 1), (3, 1), (0, 2), (1, 2), (2, 2), (3, 2))
 BACK_PLACES = ((4, 0), (5, 0), (5, 1), (4, 1))
 O_BANKS = ((0,), (1,), (6,), (7, 2))
 
@@ -115,8 +115,11 @@ def tile_picked_gatehead_none_po_kernel(
             nc.sync.dma_start(out=tile[:], in_=as_words(packed))
             return tile
 
+        lists = [load_list(p1, "places0")]
         w3_raw = load_words(w3_words, "w3_raw")
         weights = [load_weight(a1, "weight0")]
+        lists.append(load_list(p2, "places1"))
+        lists.append(load_list(p3, "places2"))
 
         ident = keep.tile([P, P], F32, name="ident")
         make_identity(nc, ident[:])
@@ -129,29 +132,28 @@ def tile_picked_gatehead_none_po_kernel(
         w23s = keep.tile([P, 2 * N], U8, name="w23s", align_bytes=64)
         nc.vector.memset(w23s[:].bitcast(I32), 0)
         load_scale_rows(nc.sync, w23s, w23s_dealt[XS_ROW:P, :], 0)
-        lists = [load_list(p1, "places0"), load_list(p2, "places1")]
         weights.append(load_weight(a2, "weight1"))
-        lists.append(load_list(p3, "places2"))
-        weights.append(load_weight(a3, "weight2"))
         w2_raw = load_words(w2_words, "w2_raw")
+        weights.append(load_weight(a3, "weight2"))
 
         xq_words = keep.tile([P, S], U32, name="xq_words", align_bytes=64)
         nc.vector.tensor_copy(out=xq_words[:], in_=xw_table[:].indirect(offs_sb[:]))
 
-        def pick_own(k, tag):
-            tile = keep.tile([P, V // 2], U32, name=f"xo_words{k}", tag=tag, align_bytes=64)
-            half_list = V // GROUP // 2
-            nc.vector.tensor_copy(out=tile[:], in_=xw_table[:].indirect(own_sb[:, k * half_list : (k + 1) * half_list]))
+        def pick_own(cols, tag):
+            tile = keep.tile([P, cols.stop - cols.start], U32, name=f"xo_words{cols.start}", tag=tag, align_bytes=64)
+            offsets = own_sb[:, cols.start // GROUP : cols.stop // GROUP]
+            nc.vector.tensor_copy(out=tile[:], in_=xw_table[:].indirect(offsets))
             return tile
 
-        xo_words = [pick_own(0, "xo_words0")]
+        xo_wide = pick_own(queries(0, LAST - 1), "xo_wide")
 
         w1_scales = keep.tile([P, H], U8, name="w1_scales", align_bytes=64)
         w1_codes = keep.tile([P, H], U32, name="w1_codes", align_bytes=64)
         y = [keep.tile([P, Y_WIDTH[t]], F32, name=f"y{t}", tag=f"y{t}", align_bytes=64) for t in range(TILES)]
         nc.vector.memset(y[0][:, S:], 0.0)
-        nc.vector.memset(y[3][:, S:], 0.0)
         nc.scalar.activation(out=y[1][:, S:], in_=y[0][:, S:], func=SIGMOID)
+        for t in range(WHOLE_TILES, TILES):
+            nc.scalar.copy(out=y[t][:, S:], in_=y[0][:, S : Y_WIDTH[t]])
         w1_bf0 = keep.tile([P, P * PACK], BF16, name="w1_bf0", tag="w1_bf0", align_bytes=64)
         w1_bf_rest = keep.tile([P, (TILES - 1) * P * PACK], BF16, name="w1_bf_rest", align_bytes=64)
 
@@ -193,7 +195,7 @@ def tile_picked_gatehead_none_po_kernel(
         quantise_w1(0, 0)
         for k in range(2):
             make_y(0, slice(k * S // 2, (k + 1) * S // 2), 4 * k)
-        xo_words.append(pick_own(1, "w1_bf0"))
+        xo_last = pick_own(queries(LAST, LAST), "w1_bf0")
         quantise_w1(1, 1)
         make_y(1, slice(0, S), 1)
         quantise_w1(2, 3)
@@ -214,7 +216,6 @@ def tile_picked_gatehead_none_po_kernel(
             keep.tile([P, STRIPS, H // 2], BF16, name="zt0", tag="zt0", align_bytes=64),
             keep.tile([P, LAST, H // 2], BF16, name="zt1", tag="zt1", align_bytes=64),
         ]
-        zt_last = keep.tile([P, 1, H // 2], BF16, name="zt_last", tag="zt_last", align_bytes=64)
         sums = {}
 
         def fetch(v0, width, t, n, tag):
@@ -225,7 +226,7 @@ def tile_picked_gatehead_none_po_kernel(
 
         def add_term(v0, width, t, n, tag, fetched=None):
             if fetched is None:
-                term = keep.tile([P, width], F32, name=f"term{t}{n}", tag=tag) if v0 == 0 else tag
+                term = keep.tile([P, width], F32, name=f"term{t}{n}", tag=tag, align_bytes=64) if v0 == 0 else tag
                 in0 = y[t][:].indirect(lists[n][:, v0 // GROUP : (v0 + width) // GROUP])
             else:
                 term = fetched
@@ -278,11 +279,11 @@ def tile_picked_gatehead_none_po_kernel(
                 nc.tensor.matmul_mx(
                     out=gate_acc[b][:, t, :],
                     lhsT=w3_dealt[:, t, :].bitcast(FP8X4), lhsT_scale=w23s[:, N + t * P : N + (t + 1) * P],
-                    rhs=xo_words[b // 2][:, queries(b % 2, b % 2)].bitcast(FP8X4), rhs_scale=xo_scales[:, cols], start=True, stop=True,
+                    rhs=(xo_wide[:, cols] if b < LAST else xo_last[:]).bitcast(FP8X4), rhs_scale=xo_scales[:, cols], start=True, stop=True,
                 )
 
         def gate_sigmoid(b, tag):
-            gate[b] = keep.tile([P, TILES, STRIP], F32, name=f"gate{b}", tag=tag, align_bytes=64) if b < 2 else tag
+            gate[b] = keep.tile([P, TILES, STRIP], F32, name=f"gate{b}", tag=tag, align_bytes=64)
             nc.scalar.activation(out=gate[b][:], in_=gate_acc[b][:], func=SIGMOID)
 
         def turn_back(b, u):
@@ -293,7 +294,7 @@ def tile_picked_gatehead_none_po_kernel(
             nc.tensor.transpose(back[number][:, place, u, :], source.bitcast(F32), ident[:])
 
         def interleave(b, copy):
-            tile = keep.tile([P, STRIP * PACK], BF16, name=f"z_bf{b}", align_bytes=64)
+            tile = keep.tile([P, STRIP * PACK], BF16, name=f"z_bf{b}", tag="zt_last" if b == 0 else f"z_bf{b}", align_bytes=64)
             copy(
                 out=tile[:].bitcast(F32).rearrange("p (v u) -> p v u", u=2),
                 in_=back[BACK_PLACES[b][0]][:, BACK_PLACES[b][1]].rearrange("p u v -> p v u"),
@@ -344,31 +345,28 @@ def tile_picked_gatehead_none_po_kernel(
         fetched = {}
         for t, n in FETCHED:
             fetched[t, n] = fetch(0, widths[t], t, n, f"room{t}{n}")
+        for b in range(LAST):
+            gate_sigmoid(b, f"gate{b}")
+        w2_dealt = deal_words(w2_raw, "w2_dealt", nc.scalar.copy)
         for t, n in TERMS:
-            if (t, n) == (0, POINTS - 1):
-                gate_sigmoid(0, "room31")
-                w2_dealt = deal_words(w2_raw, "w2_dealt", nc.scalar.copy)
             add_term(0, widths[t], t, n, f"room{t}{n}", fetched.get((t, n)))
         for b in range(STRIPS):
             turn_back(b, 0)
         for b in range(LAST):
             turn_back(b, 1)
-        z_bf = [interleave(b, nc.scalar.copy) for b in range(LAST - 1)]
-        gate_sigmoid(1, "zt0")
-        z_bf.append(interleave(LAST - 1, nc.scalar.copy))
-        last_terms = keep.tile([P, 2, POINTS, STRIP], F32, name="last_terms", tag="room12", align_bytes=64)
+        z_bf = [interleave(b, nc.scalar.copy) for b in range(LAST)]
+        zt_last = keep.tile([P, 1, H // 2], BF16, name="zt_last", tag="zt_last", align_bytes=64)
+        last_terms = keep.tile([P, 2, POINTS, STRIP], F32, name="last_terms", tag="room02", align_bytes=64)
         for t in (2, 3):
             for n in range(POINTS):
                 add_term(WIDE, STRIP, t, n, last_terms[:, t - 2, n, :])
         turn_back(LAST, 1)
-        late_gates = keep.tile([P, 2, TILES, STRIP], F32, name="late_gates", tag="room12", align_bytes=64)
-        gate_sigmoid(2, late_gates[:, 0])
-        z_bf.append(interleave(LAST, nc.scalar.copy))
-        gate_sigmoid(3, late_gates[:, 1])
+        gate_sigmoid(3, "room02")
+        z_last = interleave(LAST, nc.scalar.copy)
         for b in range(LAST):
             project(b, z_bf[b])
         gate_and_store(0)
-        project(LAST, z_bf[LAST])
+        project(LAST, z_last)
         for b in range(1, STRIPS):
             gate_and_store(b)
         for b in range(LAST):

@@ -20,35 +20,21 @@ COPY = mybir.ActivationFunctionType.Copy
 P = 128
 PACK = 4
 TILES = 4
-HEADS = 8
 POINTS = 3
 GROUP = 16
 QUADRANTS = 4
-W3_ROW = 4
-XS_ROW = P - 16
+RAW_ROW = P - 16
 STRIP = 128
 STRIPS = V // STRIP
 LAST = STRIPS - 1
-WHOLE_TILES = 2
 WIDE = LAST * STRIP
-SCALAR_HEADS = 2
-Y_WIDTH = (2 * S, 2 * S, 2 * WIDE, 2 * WIDE)
-Y0_BANKS = (0, 4, 5, 6)
-
-SUM_BANKS = (4, 5, 6, 7)
-LAST_SUM_BANK = 7
+WIDTHS = (V, V, WIDE, WIDE)
 FETCHED = ((1, 1), (2, 1), (3, 1), (1, 2), (3, 2))
-TERMS = ((0, 0), (1, 0), (2, 0), (3, 0), (0, 1), (1, 1), (2, 1), (3, 1), (0, 2), (1, 2), (2, 2), (3, 2))
-BACK_PLACES = ((4, 0), (5, 0), (5, 1), (4, 1))
-O_BANKS = ((0,), (1,), (6,), (7, 2))
 
 
-def load_scale_rows(queue, plane, rows, first):
+def move_scale_rows(queue, plane, rows):
     for q in range(QUADRANTS):
-        queue.dma_start(
-            out=plane[32 * q + first : 32 * q + first + 4, :].bitcast(I32),
-            in_=rows[4 * q : 4 * q + 4, :].bitcast(I32),
-        )
+        queue.dma_start(out=plane[32 * q : 32 * q + 4, :].bitcast(I32), in_=rows[4 * q : 4 * q + 4, :].bitcast(I32))
 
 
 def as_words(packed):
@@ -68,6 +54,9 @@ def tile_picked_gatehead_none_po_kernel(
         keep = ctx.enter_context(tc.tile_pool(name="keep", bufs=1))
         psum = ctx.enter_context(tc.psum_pool(name="psum", bufs=1))
 
+        def sbuf(shape, dtype, name, tag=None):
+            return keep.tile(shape, dtype, name=name, tag=tag or name, align_bytes=64)
+
         def bank(number, shape, name):
             return psum.tile(shape, F32, name=name, tag=f"bank{number}")
 
@@ -77,46 +66,40 @@ def tile_picked_gatehead_none_po_kernel(
             return tile
 
         def load_weight(a, name):
-            tile = keep.tile([P, V], F32, name=name, align_bytes=64)
+            tile = sbuf([P, V], F32, name)
             nc.sync.dma_start(out=tile[:], in_=a.rearrange("(p j) v -> p j v", j=PACK)[:, 0, :])
             return tile
 
-        xs_table = keep.tile([P, T], U8, name="xs_table", tag="xs_table", align_bytes=64)
-        nc.vector.memset(xs_table[0:XS_ROW, :].bitcast(I32), 0)
-        nc.scalar.dma_start(out=xs_table[XS_ROW:P, :].bitcast(I32), in_=x_scales[0].bitcast(I32))
-        w23s_raw = keep.tile([P, 2 * N], U8, name="w23s_raw", align_bytes=64)
-        nc.vector.memset(w23s_raw[0:XS_ROW, :].bitcast(I32), 0)
-        nc.scalar.dma_start(out=w23s_raw[XS_ROW:P, :N].bitcast(I32), in_=w2_scales[0].bitcast(I32))
-        nc.scalar.dma_start(out=w23s_raw[XS_ROW:P, N:].bitcast(I32), in_=w3_scales[0].bitcast(I32))
-        offs_sb = load_list(offs, "offs_sb")
-        own_sb = load_list(own, "own_sb")
-        xw_table = keep.tile([P, T], U32, name="xw_table", align_bytes=64)
-        nc.sync.dma_start(out=xw_table[:].bitcast(I32), in_=as_words(x_words))
-        w1_rows = w1.rearrange("(p j) c -> p j c", j=PACK)
-        w1_raw = []
-        for k in range(2):
-            w1_raw.append(keep.tile([P, PACK, H // 2], F32, name=f"w1_raw{k}"))
-            nc.sync.dma_start(out=w1_raw[k][:], in_=w1_rows[:, :, k * H // 2 : (k + 1) * H // 2])
-
-        picked = keep.tile([P, S + V], U8, name="picked", align_bytes=64)
-        nc.vector.tensor_copy(out=picked[:, :S], in_=xs_table[:].indirect(offs_sb[:]))
-        nc.vector.tensor_copy(out=picked[:, S:], in_=xs_table[:].indirect(own_sb[:]))
-        x_plane = keep.tile([P, S + V], U8, name="x_plane", align_bytes=64)
-        nc.vector.memset(x_plane[:].bitcast(I32), 0)
-        for q in range(QUADRANTS):
-            nc.sync.dma_start(
-                out=x_plane[32 * q : 32 * q + 4, :].bitcast(I32),
-                in_=picked[XS_ROW + 4 * q : XS_ROW + 4 * q + 4, :].bitcast(I32),
-            )
-        xq_scales, xo_scales = x_plane[:, :S], x_plane[:, S:]
-
         def load_words(packed, name):
-            tile = keep.tile([P, N], I32, name=name, align_bytes=64)
+            tile = sbuf([P, N], I32, name)
             nc.sync.dma_start(out=tile[:], in_=as_words(packed))
             return tile
 
-        lists = [load_list(p1, "places0")]
+        w1_rows = w1.rearrange("(p j) c -> p j c", j=PACK)
+        w1_raw = sbuf([P, PACK, H], F32, "w1_raw")
+        xs_table = sbuf([P, T], U8, "xs_table")
+        nc.vector.memset(xs_table[0:RAW_ROW, :].bitcast(I32), 0)
+        nc.scalar.dma_start(out=xs_table[RAW_ROW:P, :].bitcast(I32), in_=x_scales[0].bitcast(I32))
+        ws_raw = sbuf([P, 2 * N], U8, "ws_raw")
+        nc.vector.memset(ws_raw[0:RAW_ROW, :].bitcast(I32), 0)
+        nc.scalar.dma_start(out=ws_raw[RAW_ROW:P, :N].bitcast(I32), in_=w2_scales[0].bitcast(I32))
+        nc.scalar.dma_start(out=ws_raw[RAW_ROW:P, N:].bitcast(I32), in_=w3_scales[0].bitcast(I32))
+        offs_sb = load_list(offs, "offs_sb")
+        own_sb = load_list(own, "own_sb")
+        nc.sync.dma_start(out=w1_raw[:], in_=w1_rows)
+        xw_table = sbuf([P, T], U32, "xw_table")
+        nc.sync.dma_start(out=xw_table[:].bitcast(I32), in_=as_words(x_words))
+
+        picked = sbuf([P, S + V], U8, "picked")
+        nc.vector.tensor_copy(out=picked[:, :S], in_=xs_table[:].indirect(offs_sb[:]))
+        nc.vector.tensor_copy(out=picked[:, S:], in_=xs_table[:].indirect(own_sb[:]))
+        x_plane = sbuf([P, S + V], U8, "x_plane")
+        nc.vector.memset(x_plane[:].bitcast(I32), 0)
+        move_scale_rows(nc.sync, x_plane, picked[RAW_ROW:P, :])
+        xq_scales, xo_scales = x_plane[:, :S], x_plane[:, S:]
+
         w3_raw = load_words(w3_words, "w3_raw")
+        lists = [load_list(p1, "places0")]
         weights = [load_weight(a1, "weight0")]
         lists.append(load_list(p2, "places1"))
         lists.append(load_list(p3, "places2"))
@@ -124,153 +107,82 @@ def tile_picked_gatehead_none_po_kernel(
         ident = keep.tile([P, P], F32, name="ident")
         make_identity(nc, ident[:])
 
-        w23s_dealt = keep.tile([P, 2 * N], U8, name="w23s_dealt", align_bytes=64)
+        ws_dealt = sbuf([P, 2 * N], U8, "ws_dealt")
         nc.gpsimd.tensor_copy(
-            out=w23s_dealt[:].rearrange("p (w t m) -> p w t m", w=2, t=TILES),
-            in_=w23s_raw[:].rearrange("p (w m t) -> p w t m", w=2, t=TILES),
+            out=ws_dealt[:].rearrange("p (w t m) -> p w t m", w=2, t=TILES),
+            in_=ws_raw[:].rearrange("p (w m t) -> p w t m", w=2, t=TILES),
         )
-        w23s = keep.tile([P, 2 * N], U8, name="w23s", align_bytes=64)
-        nc.vector.memset(w23s[:].bitcast(I32), 0)
-        load_scale_rows(nc.sync, w23s, w23s_dealt[XS_ROW:P, :], 0)
+        w_plane = sbuf([P, 2 * N], U8, "w_plane")
+        nc.vector.memset(w_plane[:].bitcast(I32), 0)
+        move_scale_rows(nc.sync, w_plane, ws_dealt[RAW_ROW:P, :])
         weights.append(load_weight(a2, "weight1"))
         w2_raw = load_words(w2_words, "w2_raw")
         weights.append(load_weight(a3, "weight2"))
 
-        xq_words = keep.tile([P, S], U32, name="xq_words", align_bytes=64)
-        nc.vector.tensor_copy(out=xq_words[:], in_=xw_table[:].indirect(offs_sb[:]))
-
-        def pick_own(cols, tag):
-            tile = keep.tile([P, cols.stop - cols.start], U32, name=f"xo_words{cols.start}", tag=tag, align_bytes=64)
-            offsets = own_sb[:, cols.start // GROUP : cols.stop // GROUP]
-            nc.vector.tensor_copy(out=tile[:], in_=xw_table[:].indirect(offsets))
-            return tile
-
-        xo_wide = pick_own(queries(0, LAST - 1), "xo_wide")
-
-        w1_scales = keep.tile([P, H], U8, name="w1_scales", align_bytes=64)
-        w1_codes = keep.tile([P, H], U32, name="w1_codes", align_bytes=64)
-        y = [keep.tile([P, Y_WIDTH[t]], F32, name=f"y{t}", tag=f"y{t}", align_bytes=64) for t in range(TILES)]
+        y = [sbuf([P, 2 * WIDTHS[t]], F32, f"y{t}") for t in range(TILES)]
         nc.vector.memset(y[0][:, S:], 0.0)
         nc.scalar.activation(out=y[1][:, S:], in_=y[0][:, S:], func=SIGMOID)
-        for t in range(WHOLE_TILES, TILES):
-            nc.scalar.copy(out=y[t][:, S:], in_=y[0][:, S : Y_WIDTH[t]])
-        w1_bf0 = keep.tile([P, P * PACK], BF16, name="w1_bf0", tag="w1_bf0", align_bytes=64)
-        w1_bf_rest = keep.tile([P, (TILES - 1) * P * PACK], BF16, name="w1_bf_rest", align_bytes=64)
+        for t in (2, 3):
+            nc.scalar.copy(out=y[t][:, S:], in_=y[0][:, S : 2 * WIDE])
 
-        def w1_bf(start, stop):
-            if start < P * PACK:
-                return w1_bf0[:, start:stop]
-            return w1_bf_rest[:, start - P * PACK : stop - P * PACK]
-
-        def round_w1(k, t, cast):
-            width = P * PACK // 2
-            at = (2 * t + k) * width
+        w1_bf = sbuf([P, TILES, P, PACK], BF16, "w1_bf")
+        for k, cast in enumerate((nc.scalar.copy, nc.vector.tensor_copy)):
             cast(
-                out=w1_bf(at, at + width).rearrange("p (g i e j) -> p g i j e", g=HEADS // 2, e=2, j=PACK),
-                in_=w1_raw[k][:].rearrange("p j (g h i u e) -> p u h g i j e", g=HEADS // 2, h=2, u=2, e=2)[
-                    :, t // 2, t % 2
-                ],
+                out=w1_bf[:, :, k * P // 2 : (k + 1) * P // 2, :].rearrange("p t m j -> p m j t"),
+                in_=w1_raw[:, :, k * H // 2 : (k + 1) * H // 2].rearrange("p j (m t) -> p m j t", t=TILES),
             )
+        w1_scales = sbuf([P, H], U8, "w1_scales")
+        w1_codes = sbuf([P, H], U32, "w1_codes")
+        nc.vector.quantize_mx(
+            out=w1_codes[:].bitcast(FP8X4), scales=w1_scales[:], in_=w1_bf[:].rearrange("p t m j -> p (t m j)")
+        )
 
-        def quantise_w1(first, last):
-            cols = slice(first * P, (last + 1) * P)
-            nc.vector.quantize_mx(
-                out=w1_codes[:, cols].bitcast(FP8X4), scales=w1_scales[:, cols],
-                in_=w1_bf(cols.start * PACK, cols.stop * PACK),
+        def pick_words(offsets, cols, name):
+            tile = sbuf([P, cols.stop - cols.start], U32, name)
+            nc.vector.tensor_copy(
+                out=tile[:], in_=xw_table[:].indirect(offsets[:, cols.start // GROUP : cols.stop // GROUP])
             )
+            return tile
 
-        def make_y(t, part, number):
+        halves = [slice(0, S // 2), slice(S // 2, S)]
+        xq_words = [pick_words(offs_sb, halves[k], f"xq_words{k}") for k in range(2)]
+        xo_words = pick_words(own_sb, slice(0, V), "xo_words")
+
+        def make_y(t, k, acc):
             cols = slice(t * P, (t + 1) * P)
-            acc = bank(number, [P, part.stop - part.start], "y_acc")
             nc.tensor.matmul_mx(
-                out=acc[:], lhsT=w1_codes[:, cols].bitcast(FP8X4), lhsT_scale=w1_scales[:, cols],
-                rhs=xq_words[:, part].bitcast(FP8X4), rhs_scale=xq_scales[:, part], start=True, stop=True,
+                out=acc, lhsT=w1_codes[:, cols].bitcast(FP8X4), lhsT_scale=w1_scales[:, cols],
+                rhs=xq_words[k][:].bitcast(FP8X4), rhs_scale=xq_scales[:, halves[k]], start=True, stop=True,
             )
-            nc.scalar.copy(out=y[t][:, part], in_=acc[:])
 
-        for t in range(TILES):
-            round_w1(0, t, nc.scalar.copy)
-        for t in range(TILES):
-            round_w1(1, t, nc.vector.tensor_copy if t == 0 else nc.scalar.copy)
-        quantise_w1(0, 0)
         for k in range(2):
-            make_y(0, slice(k * S // 2, (k + 1) * S // 2), 4 * k)
-        xo_last = pick_own(queries(LAST, LAST), "w1_bf0")
-        quantise_w1(1, 1)
-        make_y(1, slice(0, S), 1)
-        quantise_w1(2, 3)
-        for t in range(2, TILES):
-            make_y(t, slice(0, S), t)
+            acc = bank(4 * k, [P, S // 2], "y_acc")
+            make_y(0, k, acc[:])
+            nc.scalar.copy(out=y[0][:, halves[k]], in_=acc[:])
+        for t in range(1, TILES):
+            acc = bank(t, [P, S], "y_acc")
+            for k in range(2):
+                make_y(t, k, acc[:, halves[k]])
+            nc.scalar.copy(out=y[t][:, :S], in_=acc[:])
 
         def deal_words(raw, name, copy):
-            tile = keep.tile([P, TILES, P], U32, name=name, align_bytes=64)
+            tile = sbuf([P, TILES, P], U32, name)
             copy(
                 out=tile[:].rearrange("p (s e) (c i) -> p c s i e", e=2, i=4),
                 in_=raw[:].bitcast(U32).rearrange("p (c i s e) -> p c s i e", s=2, e=2, i=4),
             )
             return tile
 
-        w3_dealt = deal_words(w3_raw, "w3_dealt", nc.vector.tensor_copy)
+        w3_dealt = sbuf([P, TILES, P], U32, "w3_dealt")
+        nc.gpsimd.tensor_copy(out=w3_dealt[:], in_=w3_raw[:].bitcast(U32).rearrange("p (m t) -> p t m", t=TILES))
 
-        zt = [
-            keep.tile([P, STRIPS, H // 2], BF16, name="zt0", tag="zt0", align_bytes=64),
-            keep.tile([P, LAST, H // 2], BF16, name="zt1", tag="zt1", align_bytes=64),
-        ]
-        sums = {}
-
-        def fetch(v0, width, t, n, tag):
-            term = keep.tile([P, width], F32, name=f"term{t}{n}", tag=tag, align_bytes=64)
-            offsets = lists[n][:, v0 // GROUP : (v0 + width) // GROUP]
-            nc.scalar.activation(out=term[:], in_=y[t][:].indirect(offsets), func=COPY)
-            return term
-
-        def add_term(v0, width, t, n, tag, fetched=None):
-            if fetched is None:
-                term = keep.tile([P, width], F32, name=f"term{t}{n}", tag=tag, align_bytes=64) if v0 == 0 else tag
-                in0 = y[t][:].indirect(lists[n][:, v0 // GROUP : (v0 + width) // GROUP])
-            else:
-                term = fetched
-                in0 = fetched[:]
-            nc.vector.tensor_tensor(out=term[:], in0=in0, in1=weights[n][:, v0 : v0 + width], op=MULT)
-            strips = width // STRIP
-            if v0 == 0:
-                if n == 0:
-                    sums[t] = bank(SUM_BANKS[t], [P, strips, P], "z_sum")
-                for b in range(strips):
-                    nc.tensor.matmul(
-                        sums[t][:, b, :], lhsT=term[:, b * STRIP : (b + 1) * STRIP], rhs=ident[:],
-                        start=(n == 0 and b == 0), stop=(n == POINTS - 1 and b == strips - 1), is_transpose=True,
-                    )
-                if n == POINTS - 1:
-                    u, h = divmod(t, 2)
-                    nc.scalar.copy(
-                        out=zt[u][:].rearrange("v b (g h r) -> v b g h r", g=HEADS, h=2)[:, :, :, h, :],
-                        in_=sums[t][:].rearrange("v b (g r) -> v b g r", g=HEADS),
-                    )
-            else:
-                h = t % 2
-                if n == 0 and h == 0:
-                    sums["last"] = bank(LAST_SUM_BANK, [P, 2, P], "z_sum")
-                nc.tensor.matmul(
-                    sums["last"][:, h, :], lhsT=term[:], rhs=ident[:],
-                    start=(n == 0), stop=(n == POINTS - 1), is_transpose=True,
-                )
-                if n == POINTS - 1 and h == 1:
-                    nc.scalar.copy(
-                        out=zt_last[:, 0, :].rearrange("v (g h r) -> v g h r", g=HEADS, h=2),
-                        in_=sums["last"][:].rearrange("v h (g r) -> v g h r", g=HEADS),
-                    )
-
-        z_scales = keep.tile([P, V], U8, name="z_scales", align_bytes=64)
-        out_codes = keep.tile([P, V], U32, name="out_codes", align_bytes=64)
-        out_scales = keep.tile([P, V], U8, name="out_scales", align_bytes=64)
-        res = keep.tile([P, TILES, V], F32, name="res")
+        z_scales = sbuf([P, V], U8, "z_scales")
+        out_codes = sbuf([P, V], U32, "out_codes")
+        out_scales = sbuf([P, V], U8, "out_scales")
+        res = sbuf([P, TILES, V], F32, "res")
         out_rows = out_0.rearrange("(p t) v -> p t v", t=TILES)
         out_words = as_words(out_1)
-        back = {}
-        o = {}
-        gate_acc = {}
-        gate = {}
+        gate_acc, gate, o, back, sums, zt = {}, {}, {}, {}, {}, {}
 
         def gate_product(b):
             cols = queries(b, b)
@@ -278,32 +190,74 @@ def tile_picked_gatehead_none_po_kernel(
             for t in range(TILES):
                 nc.tensor.matmul_mx(
                     out=gate_acc[b][:, t, :],
-                    lhsT=w3_dealt[:, t, :].bitcast(FP8X4), lhsT_scale=w23s[:, N + t * P : N + (t + 1) * P],
-                    rhs=(xo_wide[:, cols] if b < LAST else xo_last[:]).bitcast(FP8X4), rhs_scale=xo_scales[:, cols], start=True, stop=True,
+                    lhsT=w3_dealt[:, t, :].bitcast(FP8X4), lhsT_scale=w_plane[:, N + t * P : N + (t + 1) * P],
+                    rhs=xo_words[:, cols].bitcast(FP8X4), rhs_scale=xo_scales[:, cols], start=True, stop=True,
                 )
 
-        def gate_sigmoid(b, tag):
-            gate[b] = keep.tile([P, TILES, STRIP], F32, name=f"gate{b}", tag=tag, align_bytes=64)
+        def gate_sigmoid(b, tag=None):
+            gate[b] = sbuf([P, TILES, STRIP], F32, f"gate{b}", tag)
             nc.scalar.activation(out=gate[b][:], in_=gate_acc[b][:], func=SIGMOID)
+
+        def places(n, cols):
+            return lists[n][:, cols.start // GROUP : cols.stop // GROUP]
+
+        def fetch(t, n, cols):
+            term = sbuf([P, cols.stop - cols.start], F32, f"term{t}{n}")
+            nc.scalar.activation(out=term[:], in_=y[t][:].indirect(places(n, cols)), func=COPY)
+            return term
+
+        GROUPS = ((0, 0, 1, 4), (0, 2, 3, 5), (1, 0, 1, 6), (1, 2, 2, 7), (1, 3, 3, 7))
+        seen = {g: 0 for g in GROUPS}
+
+        def add_term(term, t, cols):
+            u, e = divmod(t, 2)
+            for g in GROUPS:
+                half, first, last, number = g
+                strips = [b for b in range(first, last + 1) if cols.start <= b * STRIP < cols.stop]
+                if half != u or not strips:
+                    continue
+                count = last - first + 1
+                if seen[g] == 0:
+                    sums[g] = bank(number, [P, 2, count, P], "z_sum")
+                for b in strips:
+                    at = b * STRIP - cols.start
+                    nc.tensor.matmul(
+                        sums[g][:, e, b - first, :], lhsT=term[:, at : at + STRIP], rhs=ident[:],
+                        start=(seen[g] == 0), stop=(seen[g] == 2 * count * POINTS - 1), is_transpose=True,
+                    )
+                    seen[g] = seen[g] + 1
+                if seen[g] == 2 * count * POINTS:
+                    rounded = sbuf([P, count, P, 2], BF16, f"zt{u}{first}", "zt_last" if first == LAST else None)
+                    nc.scalar.copy(out=rounded[:], in_=sums[g][:].rearrange("v e b p -> v b p e"))
+                    for b in range(first, last + 1):
+                        zt[u, b] = rounded[:, b - first].rearrange("v p e -> v (p e)").bitcast(F32)
+
+        def weigh(t, n, cols, term, in0):
+            nc.vector.tensor_tensor(out=term, in0=in0, in1=weights[n][:, cols], op=MULT)
+            add_term(term, t, cols)
+
+        BACK_PLACES = ((4, 0), (5, 0), (5, 1), (4, 1))
 
         def turn_back(b, u):
             number, place = BACK_PLACES[b]
-            if u == 0 and place == 0:
+            if number not in back:
                 back[number] = bank(number, [P, 2, 2, STRIP], "back")
-            source = zt_last[:, 0, :] if (b == LAST and u == 1) else zt[u][:, b, :]
-            nc.tensor.transpose(back[number][:, place, u, :], source.bitcast(F32), ident[:])
+            nc.tensor.transpose(back[number][:, place, u, :], zt[u, b], ident[:])
 
-        def interleave(b, copy):
-            tile = keep.tile([P, STRIP * PACK], BF16, name=f"z_bf{b}", tag="zt_last" if b == 0 else f"z_bf{b}", align_bytes=64)
-            copy(
+        def interleave(b):
+            tile = sbuf([P, STRIP * PACK], BF16, f"z_bf{b}", "zt_last" if b == 0 else None)
+            number, place = BACK_PLACES[b]
+            nc.scalar.copy(
                 out=tile[:].bitcast(F32).rearrange("p (v u) -> p v u", u=2),
-                in_=back[BACK_PLACES[b][0]][:, BACK_PLACES[b][1]].rearrange("p u v -> p v u"),
+                in_=back[number][:, place].rearrange("p u v -> p v u"),
             )
             return tile
 
+        O_BANKS = ((0,), (1,), (6,), (7, 2))
+
         def project(b, z_strip):
             cols = queries(b, b)
-            z_codes = keep.tile([P, STRIP], U32, name=f"z_codes{b}", align_bytes=64)
+            z_codes = sbuf([P, STRIP], U32, f"z_codes{b}")
             nc.vector.quantize_mx(out=z_codes[:].bitcast(FP8X4), scales=z_scales[:, cols], in_=z_strip[:])
             o[b] = []
             per_bank = TILES // len(O_BANKS[b])
@@ -312,7 +266,7 @@ def tile_picked_gatehead_none_po_kernel(
                     o[b].append(bank(O_BANKS[b][t // per_bank], [P, per_bank, STRIP], "o"))
                 nc.tensor.matmul_mx(
                     out=o[b][-1][:, t % per_bank, :],
-                    lhsT=w2_dealt[:, t, :].bitcast(FP8X4), lhsT_scale=w23s[:, t * P : (t + 1) * P],
+                    lhsT=w2_dealt[:, t, :].bitcast(FP8X4), lhsT_scale=w_plane[:, t * P : (t + 1) * P],
                     rhs=z_codes[:].bitcast(FP8X4), rhs_scale=z_scales[:, cols], start=True, stop=True,
                 )
 
@@ -321,14 +275,12 @@ def tile_picked_gatehead_none_po_kernel(
             per_bank = TILES // len(o[b])
             for k, part in enumerate(o[b]):
                 rows = slice(k * per_bank, (k + 1) * per_bank)
-                nc.vector.tensor_tensor(
-                    out=res[:, rows, cols], in0=part[:], in1=gate[b][:, rows, :], op=MULT
-                )
+                nc.vector.tensor_tensor(out=res[:, rows, cols], in0=part[:], in1=gate[b][:, rows, :], op=MULT)
             nc.sync.dma_start(out=out_rows[:, :, cols], in_=res[:, :, cols])
 
         def quantise_out(b, cast):
             cols = queries(b, b)
-            res_bf = keep.tile([P, STRIP * PACK], BF16, name=f"res_bf{b}", tag="zt_last" if b == 0 else f"res_bf{b}", align_bytes=64)
+            res_bf = sbuf([P, STRIP * PACK], BF16, f"res_bf{b}", "zt_last" if b == 0 else None)
             cast(
                 out=res_bf[:].rearrange("p (c e t) -> p c t e", e=2, t=TILES),
                 in_=res[:, :, cols].rearrange("p t (c e) -> p c t e", e=2),
@@ -339,30 +291,33 @@ def tile_picked_gatehead_none_po_kernel(
             cols = queries(first, last)
             nc.sync.dma_start(out=out_words[:, cols], in_=out_codes[:, cols].bitcast(I32))
 
-        widths = (V, V, WIDE, WIDE)
         for b in range(STRIPS):
             gate_product(b)
-        fetched = {}
-        for t, n in FETCHED:
-            fetched[t, n] = fetch(0, widths[t], t, n, f"room{t}{n}")
+        fetched = {(t, n): fetch(t, n, slice(0, WIDTHS[t])) for t, n in FETCHED}
         for b in range(LAST):
-            gate_sigmoid(b, f"gate{b}")
+            gate_sigmoid(b)
         w2_dealt = deal_words(w2_raw, "w2_dealt", nc.scalar.copy)
-        for t, n in TERMS:
-            add_term(0, widths[t], t, n, f"room{t}{n}", fetched.get((t, n)))
+        for n in range(POINTS):
+            for t in range(TILES):
+                cols = slice(0, WIDTHS[t])
+                if (t, n) in fetched:
+                    weigh(t, n, cols, fetched[t, n][:], fetched[t, n][:])
+                else:
+                    term = sbuf([P, WIDTHS[t]], F32, f"term{t}{n}")
+                    weigh(t, n, cols, term[:], y[t][:].indirect(places(n, cols)))
         for b in range(STRIPS):
             turn_back(b, 0)
         for b in range(LAST):
             turn_back(b, 1)
-        z_bf = [interleave(b, nc.scalar.copy) for b in range(LAST)]
-        zt_last = keep.tile([P, 1, H // 2], BF16, name="zt_last", tag="zt_last", align_bytes=64)
-        last_terms = keep.tile([P, 2, POINTS, STRIP], F32, name="last_terms", tag="room02", align_bytes=64)
+        z_bf = [interleave(b) for b in range(LAST)]
+        last_terms = sbuf([P, 2, POINTS, STRIP], F32, "last_terms", "term02")
+        cols = queries(LAST, LAST)
         for t in (2, 3):
             for n in range(POINTS):
-                add_term(WIDE, STRIP, t, n, last_terms[:, t - 2, n, :])
+                weigh(t, n, cols, last_terms[:, t - 2, n, :], y[t][:].indirect(places(n, cols)))
         turn_back(LAST, 1)
-        gate_sigmoid(3, "room02")
-        z_last = interleave(LAST, nc.scalar.copy)
+        gate_sigmoid(LAST, "term02")
+        z_last = interleave(LAST)
         for b in range(LAST):
             project(b, z_bf[b])
         gate_and_store(0)

@@ -108,7 +108,7 @@ def tile_picked_gatehead_none_po_kernel(
         make_identity(nc, ident[:])
 
         ws_dealt = sbuf([P, 2 * N], U8, "ws_dealt")
-        nc.gpsimd.tensor_copy(
+        nc.vector.tensor_copy(
             out=ws_dealt[:].rearrange("p (w t m) -> p w t m", w=2, t=TILES),
             in_=ws_raw[:].rearrange("p (w m t) -> p w t m", w=2, t=TILES),
         )
@@ -173,8 +173,7 @@ def tile_picked_gatehead_none_po_kernel(
             )
             return tile
 
-        w3_dealt = sbuf([P, TILES, P], U32, "w3_dealt")
-        nc.gpsimd.tensor_copy(out=w3_dealt[:], in_=w3_raw[:].bitcast(U32).rearrange("p (m t) -> p t m", t=TILES))
+        w3_dealt = deal_words(w3_raw, "w3_dealt", nc.scalar.copy)
 
         z_scales = sbuf([P, V], U8, "z_scales")
         out_codes = sbuf([P, V], U32, "out_codes")

@@ -14,6 +14,7 @@ U16 = mybir.dt.uint16
 U8 = mybir.dt.uint8
 FP8X4 = mybir.dt.float8_e4m3fn_x4
 MULT = mybir.AluOpType.mult
+ADD = mybir.AluOpType.add
 SIGMOID = mybir.ActivationFunctionType.Sigmoid
 COPY = mybir.ActivationFunctionType.Copy
 
@@ -29,7 +30,6 @@ STRIPS = V // STRIP
 LAST = STRIPS - 1
 WIDE = LAST * STRIP
 WIDTHS = (V, V, WIDE, WIDE)
-FETCHED = ((1, 1), (2, 1), (3, 1), (1, 2), (3, 2))
 
 
 def move_scale_rows(queue, plane, rows):
@@ -173,7 +173,8 @@ def tile_picked_gatehead_none_po_kernel(
             )
             return tile
 
-        w3_dealt = deal_words(w3_raw, "w3_dealt", nc.scalar.copy)
+        w3_dealt = sbuf([P, TILES, P], U32, "w3_dealt")
+        nc.gpsimd.tensor_copy(out=w3_dealt[:], in_=w3_raw[:].bitcast(U32).rearrange("p (m t) -> p t m", t=TILES))
 
         z_scales = sbuf([P, V], U8, "z_scales")
         out_codes = sbuf([P, V], U32, "out_codes")
@@ -200,12 +201,10 @@ def tile_picked_gatehead_none_po_kernel(
         def places(n, cols):
             return lists[n][:, cols.start // GROUP : cols.stop // GROUP]
 
-        def fetch(t, n, cols):
-            term = sbuf([P, cols.stop - cols.start], F32, f"term{t}{n}")
-            nc.scalar.activation(out=term[:], in_=y[t][:].indirect(places(n, cols)), func=COPY)
-            return term
+        def fetch(t, n, term, cols):
+            nc.scalar.activation(out=term[:, cols], in_=y[t][:].indirect(places(n, cols)), func=COPY)
 
-        GROUPS = ((0, 0, 1, 4), (0, 2, 3, 5), (1, 0, 1, 6), (1, 2, 2, 7), (1, 3, 3, 7))
+        GROUPS = ((0, 2, 3, 5), (0, 0, 1, 4), (1, 2, 2, 6), (1, 0, 1, 7))
         seen = {g: 0 for g in GROUPS}
 
         def add_term(term, t, cols):
@@ -219,23 +218,39 @@ def tile_picked_gatehead_none_po_kernel(
                 if seen[g] == 0:
                     sums[g] = bank(number, [P, 2, count, P], "z_sum")
                 for b in strips:
-                    at = b * STRIP - cols.start
                     nc.tensor.matmul(
-                        sums[g][:, e, b - first, :], lhsT=term[:, at : at + STRIP], rhs=ident[:],
+                        sums[g][:, e, b - first, :], lhsT=term[:, queries(b, b)], rhs=ident[:],
                         start=(seen[g] == 0), stop=(seen[g] == 2 * count * POINTS - 1), is_transpose=True,
                     )
                     seen[g] = seen[g] + 1
-                if seen[g] == 2 * count * POINTS:
-                    rounded = sbuf([P, count, P, 2], BF16, f"zt{u}{first}", "zt_last" if first == LAST else None)
-                    nc.scalar.copy(out=rounded[:], in_=sums[g][:].rearrange("v e b p -> v b p e"))
-                    for b in range(first, last + 1):
-                        zt[u, b] = rounded[:, b - first].rearrange("v p e -> v (p e)").bitcast(F32)
 
-        def weigh(t, n, cols, term, in0):
-            nc.vector.tensor_tensor(out=term, in0=in0, in1=weights[n][:, cols], op=MULT)
+        def round_sums(g):
+            u, first, last, number = g
+            rounded = sbuf([P, last - first + 1, P, 2], BF16, f"zt{u}{first}")
+            nc.scalar.copy(out=rounded[:], in_=sums[g][:].rearrange("v e b p -> v b p e"))
+            for b in range(first, last + 1):
+                zt[u, b] = rounded[:, b - first].rearrange("v p e -> v (p e)").bitcast(F32)
+
+        def look_up(t, n, term, cols):
+            nc.vector.tensor_tensor(
+                out=term[:, cols], in0=y[t][:].indirect(places(n, cols)), in1=weights[n][:, cols], op=MULT
+            )
             add_term(term, t, cols)
 
-        BACK_PLACES = ((4, 0), (5, 0), (5, 1), (4, 1))
+        def weigh(t, n, term, cols):
+            nc.vector.tensor_tensor(out=term[:, cols], in0=term[:, cols], in1=weights[n][:, cols], op=MULT)
+            add_term(term, t, cols)
+
+        def weigh_pair(n, pair, cols):
+            width = cols.stop - cols.start
+            nc.vector.tensor_tensor(
+                out=pair[:, :, cols], in0=pair[:, :, cols],
+                in1=weights[n][:, cols].unsqueeze(1).to_broadcast([P, 2, width]), op=MULT,
+            )
+            for e in range(2):
+                add_term(pair[:, e, :], 2 + e, cols)
+
+        BACK_PLACES = ((4, 0), (4, 1), (5, 0), (5, 1))
 
         def turn_back(b, u):
             number, place = BACK_PLACES[b]
@@ -244,7 +259,7 @@ def tile_picked_gatehead_none_po_kernel(
             nc.tensor.transpose(back[number][:, place, u, :], zt[u, b], ident[:])
 
         def interleave(b):
-            tile = sbuf([P, STRIP * PACK], BF16, f"z_bf{b}", "zt_last" if b == 0 else None)
+            tile = sbuf([P, STRIP * PACK], BF16, f"z_bf{b}")
             number, place = BACK_PLACES[b]
             nc.scalar.copy(
                 out=tile[:].bitcast(F32).rearrange("p (v u) -> p v u", u=2),
@@ -252,7 +267,7 @@ def tile_picked_gatehead_none_po_kernel(
             )
             return tile
 
-        O_BANKS = ((0,), (1,), (6,), (7, 2))
+        O_BANKS = ((6,), (1,), (7,), (4,))
 
         def project(b, z_strip):
             cols = queries(b, b)
@@ -269,17 +284,20 @@ def tile_picked_gatehead_none_po_kernel(
                     rhs=z_codes[:].bitcast(FP8X4), rhs_scale=z_scales[:, cols], start=True, stop=True,
                 )
 
-        def gate_and_store(b):
+        def gate_strip(b):
             cols = queries(b, b)
             per_bank = TILES // len(o[b])
             for k, part in enumerate(o[b]):
                 rows = slice(k * per_bank, (k + 1) * per_bank)
                 nc.vector.tensor_tensor(out=res[:, rows, cols], in0=part[:], in1=gate[b][:, rows, :], op=MULT)
+
+        def store_out(first, last):
+            cols = queries(first, last)
             nc.sync.dma_start(out=out_rows[:, :, cols], in_=res[:, :, cols])
 
         def quantise_out(b, cast):
             cols = queries(b, b)
-            res_bf = sbuf([P, STRIP * PACK], BF16, f"res_bf{b}", "zt_last" if b == 0 else None)
+            res_bf = sbuf([P, STRIP * PACK], BF16, f"res_bf{b}")
             cast(
                 out=res_bf[:].rearrange("p (c e t) -> p c t e", e=2, t=TILES),
                 in_=res[:, :, cols].rearrange("p t (c e) -> p c t e", e=2),
@@ -290,40 +308,80 @@ def tile_picked_gatehead_none_po_kernel(
             cols = queries(first, last)
             nc.sync.dma_start(out=out_words[:, cols], in_=out_codes[:, cols].bitcast(I32))
 
-        for b in range(STRIPS):
+        for b in (2, 1, 3, 0):
             gate_product(b)
-        fetched = {(t, n): fetch(t, n, slice(0, WIDTHS[t])) for t, n in FETCHED}
-        for b in range(LAST):
+        single, pairs = {}, {}
+        for n in (1, 2):
+            single[n] = sbuf([P, V], F32, f"term1{n}")
+            fetch(1, n, single[n], slice(0, V))
+            pairs[n] = sbuf([P, 2, WIDE], F32, f"pair{n}")
+            for e in range(n - 1, 2):
+                fetch(2 + e, n, pairs[n][:, e, :], slice(0, WIDE))
+        fetch(2, 2, pairs[2][:, 0, :], queries(0, 1))
+        for b in (2, 1):
             gate_sigmoid(b)
         w2_dealt = deal_words(w2_raw, "w2_dealt", nc.scalar.copy)
-        for n in range(POINTS):
-            for t in range(TILES):
-                cols = slice(0, WIDTHS[t])
-                if (t, n) in fetched:
-                    weigh(t, n, cols, fetched[t, n][:], fetched[t, n][:])
-                else:
-                    term = sbuf([P, WIDTHS[t]], F32, f"term{t}{n}")
-                    weigh(t, n, cols, term[:], y[t][:].indirect(places(n, cols)))
-        for b in range(STRIPS):
-            turn_back(b, 0)
-        for b in range(LAST):
-            turn_back(b, 1)
-        z_bf = [interleave(b) for b in range(LAST)]
-        last_terms = sbuf([P, 2, POINTS, STRIP], F32, "last_terms", "term02")
+        for t in range(TILES):
+            look_up(t, 0, sbuf([P, WIDTHS[t]], F32, f"term{t}0"), slice(0, WIDTHS[t]))
+        look_up(0, 1, sbuf([P, V], F32, "term01"), slice(0, V))
+        weigh(1, 1, single[1], slice(0, V))
+        weigh_pair(1, pairs[1], slice(0, WIDE))
+        term02 = sbuf([P, V], F32, "term02")
+        look_up(0, 2, term02, queries(2, 3))
+        weigh(1, 2, single[2], queries(2, 3))
+        round_sums(GROUPS[0])
+        look_up(2, 2, pairs[2][:, 0, :], queries(2, 2))
+        weigh(3, 2, pairs[2][:, 1, :], queries(2, 2))
+        round_sums(GROUPS[2])
+        look_up(0, 2, term02, queries(0, 1))
+        weigh(1, 2, single[2], queries(0, 1))
+        round_sums(GROUPS[1])
+        weigh_pair(2, pairs[2], queries(0, 1))
+        round_sums(GROUPS[3])
+        for b, u in ((2, 0), (2, 1), (1, 0), (0, 0), (1, 1), (0, 1)):
+            turn_back(b, u)
+        z_bf = {2: interleave(2)}
+        for b in (1, 0):
+            z_bf[b] = interleave(b)
+        turn_back(LAST, 0)
+        z_last = sbuf([P, STRIP * PACK], BF16, "z_last")
+        number, place = BACK_PLACES[LAST]
+        nc.scalar.copy(
+            out=z_last[:].bitcast(F32).rearrange("p (v u) -> p v u", u=2)[:, :, 0], in_=back[number][:, place, 0, :]
+        )
+        last_terms = sbuf([P, 2, 2, STRIP], F32, "last_terms", "term01")
         cols = queries(LAST, LAST)
-        for t in (2, 3):
-            for n in range(POINTS):
-                weigh(t, n, cols, last_terms[:, t - 2, n, :], y[t][:].indirect(places(n, cols)))
-        turn_back(LAST, 1)
-        gate_sigmoid(LAST, "term02")
-        z_last = interleave(LAST)
-        for b in range(LAST):
-            project(b, z_bf[b])
-        gate_and_store(0)
+        pair = sbuf([P, 2, STRIP], F32, "pair")
+
+        def short_terms(n, into):
+            for e in range(2):
+                nc.vector.tensor_tensor(
+                    out=into[:, e, :], in0=y[2 + e][:].indirect(places(n, cols)), in1=weights[n][:, cols], op=MULT
+                )
+
+        for n in range(2):
+            short_terms(n, last_terms[:, :, n, :])
+        project(2, z_bf[2])
+        third = sbuf([P, 2, STRIP], F32, "third", "zt00")
+        short_terms(2, third)
+        project(1, z_bf[1])
+        nc.vector.tensor_tensor(out=pair[:], in0=last_terms[:, :, 0, :], in1=third[:], op=ADD)
+        project(0, z_bf[0])
+        nc.vector.tensor_tensor(
+            out=z_last[:].rearrange("p (v u e) -> p v u e", u=2, e=2)[:, :, 1, :],
+            in0=pair[:].rearrange("p e v -> p v e"), in1=last_terms[:, :, 1, :].rearrange("p e v -> p v e"), op=ADD,
+        )
+        gate_sigmoid(0, "zt10")
+        gate_sigmoid(LAST, "z_bf1")
+        gate_strip(2)
+        store_out(2, 2)
         project(LAST, z_last)
-        for b in range(1, STRIPS):
-            gate_and_store(b)
-        for b in range(LAST):
+        for b in (1, 0):
+            gate_strip(b)
+            store_out(b, b)
+        gate_strip(LAST)
+        store_out(LAST, LAST)
+        for b in (2, 1, 0):
             quantise_out(b, nc.scalar.copy)
         store_codes(0, LAST - 1)
         quantise_out(LAST, nc.vector.tensor_copy)

@@ -107,8 +107,20 @@ def tile_picked_gatehead_none_po_kernel(
         ident = keep.tile([P, P], F32, name="ident")
         make_identity(nc, ident[:])
 
-        ws_dealt = sbuf([P, 2 * N], U8, "ws_dealt")
-        nc.vector.tensor_copy(
+        w1_bf = sbuf([P, TILES, P, PACK], BF16, "w1_bf")
+        for k, cast in enumerate((nc.scalar.copy, nc.vector.tensor_copy)):
+            cast(
+                out=w1_bf[:, :, k * P // 2 : (k + 1) * P // 2, :].rearrange("p t m j -> p m j t"),
+                in_=w1_raw[:, :, k * H // 2 : (k + 1) * H // 2].rearrange("p j (m t) -> p m j t", t=TILES),
+            )
+        w1_scales = sbuf([P, H], U8, "w1_scales")
+        w1_codes = sbuf([P, H], U32, "w1_codes")
+        nc.vector.quantize_mx(
+            out=w1_codes[:].bitcast(FP8X4), scales=w1_scales[:], in_=w1_bf[:].rearrange("p t m j -> p (t m j)")
+        )
+
+        ws_dealt = sbuf([P, 2 * N], U8, "ws_dealt", "w1_bf")
+        nc.gpsimd.tensor_copy(
             out=ws_dealt[:].rearrange("p (w t m) -> p w t m", w=2, t=TILES),
             in_=ws_raw[:].rearrange("p (w m t) -> p w t m", w=2, t=TILES),
         )
@@ -124,18 +136,6 @@ def tile_picked_gatehead_none_po_kernel(
         nc.scalar.activation(out=y[1][:, S:], in_=y[0][:, S:], func=SIGMOID)
         for t in (2, 3):
             nc.scalar.copy(out=y[t][:, S:], in_=y[0][:, S : 2 * WIDE])
-
-        w1_bf = sbuf([P, TILES, P, PACK], BF16, "w1_bf")
-        for k, cast in enumerate((nc.scalar.copy, nc.vector.tensor_copy)):
-            cast(
-                out=w1_bf[:, :, k * P // 2 : (k + 1) * P // 2, :].rearrange("p t m j -> p m j t"),
-                in_=w1_raw[:, :, k * H // 2 : (k + 1) * H // 2].rearrange("p j (m t) -> p m j t", t=TILES),
-            )
-        w1_scales = sbuf([P, H], U8, "w1_scales")
-        w1_codes = sbuf([P, H], U32, "w1_codes")
-        nc.vector.quantize_mx(
-            out=w1_codes[:].bitcast(FP8X4), scales=w1_scales[:], in_=w1_bf[:].rearrange("p t m j -> p (t m j)")
-        )
 
         def pick_words(offsets, cols, name):
             tile = sbuf([P, cols.stop - cols.start], U32, name)
@@ -323,9 +323,9 @@ def tile_picked_gatehead_none_po_kernel(
         w2_dealt = deal_words(w2_raw, "w2_dealt", nc.scalar.copy)
         for t in range(TILES):
             look_up(t, 0, sbuf([P, WIDTHS[t]], F32, f"term{t}0"), slice(0, WIDTHS[t]))
-        look_up(0, 1, sbuf([P, V], F32, "term01"), slice(0, V))
         weigh(1, 1, single[1], slice(0, V))
         weigh_pair(1, pairs[1], slice(0, WIDE))
+        look_up(0, 1, sbuf([P, V], F32, "term01"), slice(0, V))
         term02 = sbuf([P, V], F32, "term02")
         look_up(0, 2, term02, queries(2, 3))
         weigh(1, 2, single[2], queries(2, 3))
@@ -349,7 +349,7 @@ def tile_picked_gatehead_none_po_kernel(
         nc.scalar.copy(
             out=z_last[:].bitcast(F32).rearrange("p (v u) -> p v u", u=2)[:, :, 0], in_=back[number][:, place, 0, :]
         )
-        last_terms = sbuf([P, 2, 2, STRIP], F32, "last_terms", "term01")
+        last_terms = sbuf([P, 2, 2, STRIP], F32, "last_terms", "term11")
         cols = queries(LAST, LAST)
         pair = sbuf([P, 2, STRIP], F32, "pair")
 

@@ -156,10 +156,11 @@ def tile_picked_gatehead_none_po_kernel(
             )
 
         for k in range(2):
-            acc = bank(4 * k, [P, S // 2], "y_acc")
-            make_y(0, k, acc[:])
-            nc.scalar.copy(out=y[0][:, halves[k]], in_=acc[:])
-        for t in range(1, TILES):
+            for t in range(2):
+                acc = bank(t + 4 * k, [P, S // 2], "y_acc")
+                make_y(t, k, acc[:])
+                nc.scalar.copy(out=y[t][:, halves[k]], in_=acc[:])
+        for t in range(2, TILES):
             acc = bank(t, [P, S], "y_acc")
             for k in range(2):
                 make_y(t, k, acc[:, halves[k]])
@@ -323,9 +324,9 @@ def tile_picked_gatehead_none_po_kernel(
         w2_dealt = deal_words(w2_raw, "w2_dealt", nc.scalar.copy)
         for t in range(TILES):
             look_up(t, 0, sbuf([P, WIDTHS[t]], F32, f"term{t}0"), slice(0, WIDTHS[t]))
+        look_up(0, 1, sbuf([P, V], F32, "term01"), slice(0, V))
         weigh(1, 1, single[1], slice(0, V))
         weigh_pair(1, pairs[1], slice(0, WIDE))
-        look_up(0, 1, sbuf([P, V], F32, "term01"), slice(0, V))
         term02 = sbuf([P, V], F32, "term02")
         look_up(0, 2, term02, queries(2, 3))
         weigh(1, 2, single[2], queries(2, 3))
@@ -349,7 +350,7 @@ def tile_picked_gatehead_none_po_kernel(
         nc.scalar.copy(
             out=z_last[:].bitcast(F32).rearrange("p (v u) -> p v u", u=2)[:, :, 0], in_=back[number][:, place, 0, :]
         )
-        last_terms = sbuf([P, 2, 2, STRIP], F32, "last_terms", "term11")
+        last_terms = sbuf([P, 2, 2, STRIP], F32, "last_terms", "term01")
         cols = queries(LAST, LAST)
         pair = sbuf([P, 2, STRIP], F32, "pair")
 

@@ -242,14 +242,14 @@ def tile_picked_gatehead_none_po_kernel(
             nc.vector.tensor_tensor(out=term[:, cols], in0=term[:, cols], in1=weights[n][:, cols], op=MULT)
             add_term(term, t, cols)
 
-        def weigh_pair(n, pair, cols):
+        def weigh_pair(u, n, pair, cols):
             width = cols.stop - cols.start
             nc.vector.tensor_tensor(
                 out=pair[:, :, cols], in0=pair[:, :, cols],
                 in1=weights[n][:, cols].unsqueeze(1).to_broadcast([P, 2, width]), op=MULT,
             )
             for e in range(2):
-                add_term(pair[:, e, :], 2 + e, cols)
+                add_term(pair[:, e, :], 2 * u + e, cols)
 
         BACK_PLACES = ((4, 0), (4, 1), (5, 0), (5, 1))
 
@@ -268,7 +268,7 @@ def tile_picked_gatehead_none_po_kernel(
             )
             return tile
 
-        O_BANKS = ((6,), (1,), (7,), (4,))
+        O_BANKS = ((6,), (2,), (7,), (4,))
 
         def project(b, z_strip):
             cols = queries(b, b)
@@ -312,32 +312,31 @@ def tile_picked_gatehead_none_po_kernel(
         for b in (2, 1, 3, 0):
             gate_product(b)
         single, pairs = {}, {}
+        low_pair = sbuf([P, 2, V], F32, "low_pair")
         for n in (1, 2):
-            single[n] = sbuf([P, V], F32, f"term1{n}")
+            single[n] = sbuf([P, V], F32, "term11") if n == 1 else low_pair[:, 1, :]
             fetch(1, n, single[n], slice(0, V))
             pairs[n] = sbuf([P, 2, WIDE], F32, f"pair{n}")
             for e in range(n - 1, 2):
                 fetch(2 + e, n, pairs[n][:, e, :], slice(0, WIDE))
+        fetch(0, 2, low_pair[:, 0, :], queries(0, 1))
         fetch(2, 2, pairs[2][:, 0, :], queries(0, 1))
-        for b in (2, 1):
-            gate_sigmoid(b)
+        gate_sigmoid(2)
         w2_dealt = deal_words(w2_raw, "w2_dealt", nc.scalar.copy)
         for t in range(TILES):
             look_up(t, 0, sbuf([P, WIDTHS[t]], F32, f"term{t}0"), slice(0, WIDTHS[t]))
         look_up(0, 1, sbuf([P, V], F32, "term01"), slice(0, V))
         weigh(1, 1, single[1], slice(0, V))
-        weigh_pair(1, pairs[1], slice(0, WIDE))
-        term02 = sbuf([P, V], F32, "term02")
-        look_up(0, 2, term02, queries(2, 3))
+        weigh_pair(1, 1, pairs[1], slice(0, WIDE))
+        look_up(0, 2, low_pair[:, 0, :], queries(2, 3))
         weigh(1, 2, single[2], queries(2, 3))
         round_sums(GROUPS[0])
         look_up(2, 2, pairs[2][:, 0, :], queries(2, 2))
         weigh(3, 2, pairs[2][:, 1, :], queries(2, 2))
         round_sums(GROUPS[2])
-        look_up(0, 2, term02, queries(0, 1))
-        weigh(1, 2, single[2], queries(0, 1))
+        weigh_pair(0, 2, low_pair, queries(0, 1))
         round_sums(GROUPS[1])
-        weigh_pair(2, pairs[2], queries(0, 1))
+        weigh_pair(1, 2, pairs[2], queries(0, 1))
         round_sums(GROUPS[3])
         for b, u in ((2, 0), (2, 1), (1, 0), (0, 0), (1, 1), (0, 1)):
             turn_back(b, u)
@@ -372,8 +371,9 @@ def tile_picked_gatehead_none_po_kernel(
             out=z_last[:].rearrange("p (v u e) -> p v u e", u=2, e=2)[:, :, 1, :],
             in0=pair[:].rearrange("p e v -> p v e"), in1=last_terms[:, :, 1, :].rearrange("p e v -> p v e"), op=ADD,
         )
-        gate_sigmoid(0, "zt10")
-        gate_sigmoid(LAST, "z_bf1")
+        gate_sigmoid(1, "zt10")
+        gate_sigmoid(0, "z_bf1")
+        gate_sigmoid(LAST, "z_bf0")
         gate_strip(2)
         store_out(2, 2)
         project(LAST, z_last)

@@ -251,7 +251,7 @@ def tile_picked_gatehead_none_po_kernel(
             for e in range(2):
                 add_term(pair[:, e, :], 2 * u + e, cols)
 
-        BACK_PLACES = ((4, 0), (4, 1), (5, 0), (5, 1))
+        BACK_PLACES = ((7, 0), (7, 1), (5, 0), (5, 1))
 
         def turn_back(b, u):
             number, place = BACK_PLACES[b]
@@ -268,7 +268,7 @@ def tile_picked_gatehead_none_po_kernel(
             )
             return tile
 
-        O_BANKS = ((6,), (2,), (7,), (4,))
+        O_BANKS = ((6,), (2,), (4,), (7,))
 
         def project(b, z_strip):
             cols = queries(b, b)
@@ -325,7 +325,8 @@ def tile_picked_gatehead_none_po_kernel(
         w2_dealt = deal_words(w2_raw, "w2_dealt", nc.scalar.copy)
         for t in range(TILES):
             look_up(t, 0, sbuf([P, WIDTHS[t]], F32, f"term{t}0"), slice(0, WIDTHS[t]))
-        look_up(0, 1, sbuf([P, V], F32, "term01"), slice(0, V))
+        term01 = sbuf([P, V], F32, "term01")
+        look_up(0, 1, term01, queries(2, 3))
         weigh(1, 1, single[1], slice(0, V))
         weigh_pair(1, 1, pairs[1], slice(0, WIDE))
         look_up(0, 2, low_pair[:, 0, :], queries(2, 3))
@@ -334,11 +335,12 @@ def tile_picked_gatehead_none_po_kernel(
         look_up(2, 2, pairs[2][:, 0, :], queries(2, 2))
         weigh(3, 2, pairs[2][:, 1, :], queries(2, 2))
         round_sums(GROUPS[2])
-        weigh_pair(0, 2, low_pair, queries(0, 1))
-        round_sums(GROUPS[1])
         weigh_pair(1, 2, pairs[2], queries(0, 1))
         round_sums(GROUPS[3])
-        for b, u in ((2, 0), (2, 1), (1, 0), (0, 0), (1, 1), (0, 1)):
+        weigh_pair(0, 2, low_pair, queries(0, 1))
+        look_up(0, 1, term01, queries(0, 1))
+        round_sums(GROUPS[1])
+        for b, u in ((2, 0), (2, 1), (1, 1), (0, 1), (1, 0), (0, 0)):
             turn_back(b, u)
         z_bf = {2: interleave(2)}
         for b in (1, 0):
@@ -349,7 +351,7 @@ def tile_picked_gatehead_none_po_kernel(
         nc.scalar.copy(
             out=z_last[:].bitcast(F32).rearrange("p (v u) -> p v u", u=2)[:, :, 0], in_=back[number][:, place, 0, :]
         )
-        last_terms = sbuf([P, 2, 2, STRIP], F32, "last_terms", "term01")
+        last_terms = sbuf([P, 2, 2, STRIP], F32, "last_terms", "term11")
         cols = queries(LAST, LAST)
         pair = sbuf([P, 2, STRIP], F32, "pair")
 
@@ -362,7 +364,7 @@ def tile_picked_gatehead_none_po_kernel(
         for n in range(2):
             short_terms(n, last_terms[:, :, n, :])
         project(2, z_bf[2])
-        third = sbuf([P, 2, STRIP], F32, "third", "zt00")
+        third = sbuf([P, 2, STRIP], F32, "third", "zt10")
         short_terms(2, third)
         project(1, z_bf[1])
         nc.vector.tensor_tensor(out=pair[:], in0=last_terms[:, :, 0, :], in1=third[:], op=ADD)
@@ -371,7 +373,7 @@ def tile_picked_gatehead_none_po_kernel(
             out=z_last[:].rearrange("p (v u e) -> p v u e", u=2, e=2)[:, :, 1, :],
             in0=pair[:].rearrange("p e v -> p v e"), in1=last_terms[:, :, 1, :].rearrange("p e v -> p v e"), op=ADD,
         )
-        gate_sigmoid(1, "zt10")
+        gate_sigmoid(1, "zt00")
         gate_sigmoid(0, "z_bf1")
         gate_sigmoid(LAST, "z_bf0")
         gate_strip(2)

from contextlib import ExitStack

import concourse.mybir as mybir
from concourse.masks import make_identity

K, T, S, V, N, H = 512, 2048, 512, 512, 512, 512
FLOPS = 2 * K * H * S + 2 * H * N * V + 2 * K * N * V

F32 = mybir.dt.float32
BF16 = mybir.dt.bfloat16
I32 = mybir.dt.int32
U32 = mybir.dt.uint32
U16 = mybir.dt.uint16
U8 = mybir.dt.uint8
FP8X4 = mybir.dt.float8_e4m3fn_x4
MULT = mybir.AluOpType.mult
ADD = mybir.AluOpType.add
SIGMOID = mybir.ActivationFunctionType.Sigmoid
COPY = mybir.ActivationFunctionType.Copy

P = 128
PACK = 4
TILES = 4
POINTS = 3
GROUP = 16
QUADRANTS = 4
RAW_ROW = P - 16
STRIP = 128
STRIPS = V // STRIP
LAST = STRIPS - 1
WIDE = LAST * STRIP
WIDTHS = (V, V, WIDE, WIDE)


def move_scale_rows(queue, plane, rows):
    for q in range(QUADRANTS):
        queue.dma_start(out=plane[32 * q : 32 * q + 4, :].bitcast(I32), in_=rows[4 * q : 4 * q + 4, :].bitcast(I32))


def as_words(packed):
    return packed[0].rearrange("p n j -> p (n j)").bitcast(I32)


def queries(first, last):
    return slice(first * STRIP, (last + 1) * STRIP)


def tile_picked_gatehead_none_po_kernel(
    tc, x_words, x_scales, w1, a1, a2, a3, w2_words, w2_scales, w3_words, w3_scales,
    offs, p1, p2, p3, own, out_0, out_1, out_2,
):
    nc = tc.nc
    with ExitStack() as ctx:
        keep = ctx.enter_context(tc.tile_pool(name="keep", bufs=1))
        psum = ctx.enter_context(tc.psum_pool(name="psum", bufs=1))

        def sbuf(shape, dtype, name, tag=None):
            return keep.tile(shape, dtype, name=name, tag=tag or name, align_bytes=64)

        def bank(number, shape, name):
            return psum.tile(shape, F32, name=name, tag=f"bank{number}")

        def load_list(src, name):
            tile = keep.tile([P, S // GROUP], U16, name=name)
            nc.sync.dma_start(tile[:], src)
            return tile

        def load_weight(a, name):
            tile = sbuf([P, V], F32, name)
            nc.sync.dma_start(out=tile[:], in_=a.rearrange("(p j) v -> p j v", j=PACK)[:, 0, :])
            return tile

        def load_words(packed, name):
            tile = sbuf([P, N], I32, name)
            nc.sync.dma_start(out=tile[:], in_=as_words(packed))
            return tile

        w1_rows = w1.rearrange("(p j) c -> p j c", j=PACK)
        w1_raw = sbuf([P, PACK, H], F32, "w1_raw")
        xs_table = sbuf([P, T], U8, "xs_table")
        nc.vector.memset(xs_table[0:RAW_ROW, :].bitcast(I32), 0)
        nc.scalar.dma_start(out=xs_table[RAW_ROW:P, :].bitcast(I32), in_=x_scales[0].bitcast(I32))
        ws_raw = sbuf([P, 2 * N], U8, "ws_raw")
        nc.vector.memset(ws_raw[0:RAW_ROW, :].bitcast(I32), 0)
        nc.scalar.dma_start(out=ws_raw[RAW_ROW:P, :N].bitcast(I32), in_=w2_scales[0].bitcast(I32))
        nc.scalar.dma_start(out=ws_raw[RAW_ROW:P, N:].bitcast(I32), in_=w3_scales[0].bitcast(I32))
        offs_sb = load_list(offs, "offs_sb")
        own_sb = load_list(own, "own_sb")
        nc.sync.dma_start(out=w1_raw[:], in_=w1_rows)
        xw_table = sbuf([P, T], U32, "xw_table")
        nc.sync.dma_start(out=xw_table[:].bitcast(I32), in_=as_words(x_words))

        picked = sbuf([P, S + V], U8, "picked")
        nc.vector.tensor_copy(out=picked[:, :S], in_=xs_table[:].indirect(offs_sb[:]))
        nc.vector.tensor_copy(out=picked[:, S:], in_=xs_table[:].indirect(own_sb[:]))
        x_plane = sbuf([P, S + V], U8, "x_plane")
        nc.vector.memset(x_plane[:].bitcast(I32), 0)
        move_scale_rows(nc.sync, x_plane, picked[RAW_ROW:P, :])
        xq_scales, xo_scales = x_plane[:, :S], x_plane[:, S:]

        w3_raw = load_words(w3_words, "w3_raw")
        lists = [load_list(p1, "places0")]
        weights = [load_weight(a1, "weight0")]
        lists.append(load_list(p2, "places1"))
        lists.append(load_list(p3, "places2"))

        ident = keep.tile([P, P], F32, name="ident")
        make_identity(nc, ident[:])

        w1_bf = sbuf([P, TILES, P, PACK], BF16, "w1_bf")
        for k, cast in enumerate((nc.scalar.copy, nc.vector.tensor_copy)):
            cast(
                out=w1_bf[:, :, k * P // 2 : (k + 1) * P // 2, :].rearrange("p t m j -> p m j t"),
                in_=w1_raw[:, :, k * H // 2 : (k + 1) * H // 2].rearrange("p j (m t) -> p m j t", t=TILES),
            )
        w1_scales = sbuf([P, H], U8, "w1_scales")
        w1_codes = sbuf([P, H], U32, "w1_codes")
        nc.vector.quantize_mx(
            out=w1_codes[:].bitcast(FP8X4), scales=w1_scales[:], in_=w1_bf[:].rearrange("p t m j -> p (t m j)")
        )

        ws_dealt = sbuf([P, 2 * N], U8, "ws_dealt", "w1_bf")
        nc.gpsimd.tensor_copy(
            out=ws_dealt[:].rearrange("p (w t m) -> p w t m", w=2, t=TILES),
            in_=ws_raw[:].rearrange("p (w m t) -> p w t m", w=2, t=TILES),
        )
        w_plane = sbuf([P, 2 * N], U8, "w_plane")
        nc.vector.memset(w_plane[:].bitcast(I32), 0)
        move_scale_rows(nc.sync, w_plane, ws_dealt[RAW_ROW:P, :])
        weights.append(load_weight(a2, "weight1"))
        w2_raw = load_words(w2_words, "w2_raw")
        weights.append(load_weight(a3, "weight2"))

        y = [sbuf([P, 2 * WIDTHS[t]], F32, f"y{t}") for t in range(TILES)]
        nc.vector.memset(y[0][:, S:], 0.0)
        nc.scalar.activation(out=y[1][:, S:], in_=y[0][:, S:], func=SIGMOID)
        for t in (2, 3):
            nc.scalar.copy(out=y[t][:, S:], in_=y[0][:, S : 2 * WIDE])

        def pick_words(offsets, cols, name):
            tile = sbuf([P, cols.stop - cols.start], U32, name)
            nc.vector.tensor_copy(
                out=tile[:], in_=xw_table[:].indirect(offsets[:, cols.start // GROUP : cols.stop // GROUP])
            )
            return tile

        halves = [slice(0, S // 2), slice(S // 2, S)]
        xq_words = [pick_words(offs_sb, halves[k], f"xq_words{k}") for k in range(2)]
        xo_words = pick_words(own_sb, slice(0, V), "xo_words")

        def make_y(t, k, acc):
            cols = slice(t * P, (t + 1) * P)
            nc.tensor.matmul_mx(
                out=acc, lhsT=w1_codes[:, cols].bitcast(FP8X4), lhsT_scale=w1_scales[:, cols],
                rhs=xq_words[k][:].bitcast(FP8X4), rhs_scale=xq_scales[:, halves[k]], start=True, stop=True,
            )

        for k in range(2):
            for t in range(2):
                acc = bank(t + 4 * k, [P, S // 2], "y_acc")
                make_y(t, k, acc[:])
                nc.scalar.copy(out=y[t][:, halves[k]], in_=acc[:])
        for t in range(2, TILES):
            acc = bank(t, [P, S], "y_acc")
            for k in range(2):
                make_y(t, k, acc[:, halves[k]])
            nc.scalar.copy(out=y[t][:, :S], in_=acc[:])

        def deal_words(raw, name, copy):
            tile = sbuf([P, TILES, P], U32, name)
            copy(
                out=tile[:].rearrange("p (s e) (c i) -> p c s i e", e=2, i=4),
                in_=raw[:].bitcast(U32).rearrange("p (c i s e) -> p c s i e", s=2, e=2, i=4),
            )
            return tile

        w3_dealt = sbuf([P, TILES, P], U32, "w3_dealt")
        nc.gpsimd.tensor_copy(out=w3_dealt[:], in_=w3_raw[:].bitcast(U32).rearrange("p (m t) -> p t m", t=TILES))

        z_scales = sbuf([P, V], U8, "z_scales")
        out_codes = sbuf([P, V], U32, "out_codes")
        out_scales = sbuf([P, V], U8, "out_scales")
        res = sbuf([P, TILES, V], F32, "res")
        out_rows = out_0.rearrange("(p t) v -> p t v", t=TILES)
        out_words = as_words(out_1)
        gate_acc, gate, o, back, sums, zt = {}, {}, {}, {}, {}, {}

        def gate_product(b):
            cols = queries(b, b)
            gate_acc[b] = bank(b, [P, TILES, STRIP], "gate_acc")
            for t in range(TILES):
                nc.tensor.matmul_mx(
                    out=gate_acc[b][:, t, :],
                    lhsT=w3_dealt[:, t, :].bitcast(FP8X4), lhsT_scale=w_plane[:, N + t * P : N + (t + 1) * P],
                    rhs=xo_words[:, cols].bitcast(FP8X4), rhs_scale=xo_scales[:, cols], start=True, stop=True,
                )

        def gate_sigmoid(b, tag=None):
            gate[b] = sbuf([P, TILES, STRIP], F32, f"gate{b}", tag)
            nc.scalar.activation(out=gate[b][:], in_=gate_acc[b][:], func=SIGMOID)

        def places(n, cols):
            return lists[n][:, cols.start // GROUP : cols.stop // GROUP]

        def fetch(t, n, term, cols):
            nc.scalar.activation(out=term[:, cols], in_=y[t][:].indirect(places(n, cols)), func=COPY)

        GROUPS = ((0, 2, 3, 5), (0, 0, 1, 4), (1, 2, 2, 6), (1, 0, 1, 7))
        seen = {g: 0 for g in GROUPS}

        def add_term(term, t, cols):
            u, e = divmod(t, 2)
            for g in GROUPS:
                half, first, last, number = g
                strips = [b for b in range(first, last + 1) if cols.start <= b * STRIP < cols.stop]
                if half != u or not strips:
                    continue
                count = last - first + 1
                if seen[g] == 0:
                    sums[g] = bank(number, [P, 2, count, P], "z_sum")
                for b in strips:
                    nc.tensor.matmul(
                        sums[g][:, e, b - first, :], lhsT=term[:, queries(b, b)], rhs=ident[:],
                        start=(seen[g] == 0), stop=(seen[g] == 2 * count * POINTS - 1), is_transpose=True,
                    )
                    seen[g] = seen[g] + 1

        def round_sums(g):
            u, first, last, number = g
            rounded = sbuf([P, last - first + 1, P, 2], BF16, f"zt{u}{first}")
            nc.scalar.copy(out=rounded[:], in_=sums[g][:].rearrange("v e b p -> v b p e"))
            for b in range(first, last + 1):
                zt[u, b] = rounded[:, b - first].rearrange("v p e -> v (p e)").bitcast(F32)

        def look_up(t, n, term, cols):
            nc.vector.tensor_tensor(
                out=term[:, cols], in0=y[t][:].indirect(places(n, cols)), in1=weights[n][:, cols], op=MULT
            )
            add_term(term, t, cols)

        def weigh(t, n, term, cols):
            nc.vector.tensor_tensor(out=term[:, cols], in0=term[:, cols], in1=weights[n][:, cols], op=MULT)
            add_term(term, t, cols)

        def weigh_pair(u, n, pair, cols):
            width = cols.stop - cols.start
            nc.vector.tensor_tensor(
                out=pair[:, :, cols], in0=pair[:, :, cols],
                in1=weights[n][:, cols].unsqueeze(1).to_broadcast([P, 2, width]), op=MULT,
            )
            for e in range(2):
                add_term(pair[:, e, :], 2 * u + e, cols)

        BACK_PLACES = ((7, 0), (7, 1), (5, 0), (5, 1))

        def turn_back(b, u):
            number, place = BACK_PLACES[b]
            if number not in back:
                back[number] = bank(number, [P, 2, 2, STRIP], "back")
            nc.tensor.transpose(back[number][:, place, u, :], zt[u, b], ident[:])

        def interleave(b):
            tile = sbuf([P, STRIP * PACK], BF16, f"z_bf{b}")
            number, place = BACK_PLACES[b]
            nc.scalar.copy(
                out=tile[:].bitcast(F32).rearrange("p (v u) -> p v u", u=2),
                in_=back[number][:, place].rearrange("p u v -> p v u"),
            )
            return tile

        O_BANKS = ((6,), (2,), (4,), (7,))

        def project(b, z_strip):
            cols = queries(b, b)
            z_codes = sbuf([P, STRIP], U32, f"z_codes{b}")
            nc.vector.quantize_mx(out=z_codes[:].bitcast(FP8X4), scales=z_scales[:, cols], in_=z_strip[:])
            o[b] = []
            per_bank = TILES // len(O_BANKS[b])
            for t in range(TILES):
                if t % per_bank == 0:
                    o[b].append(bank(O_BANKS[b][t // per_bank], [P, per_bank, STRIP], "o"))
                nc.tensor.matmul_mx(
                    out=o[b][-1][:, t % per_bank, :],
                    lhsT=w2_dealt[:, t, :].bitcast(FP8X4), lhsT_scale=w_plane[:, t * P : (t + 1) * P],
                    rhs=z_codes[:].bitcast(FP8X4), rhs_scale=z_scales[:, cols], start=True, stop=True,
                )

        def gate_strip(b):
            cols = queries(b, b)
            per_bank = TILES // len(o[b])
            for k, part in enumerate(o[b]):
                rows = slice(k * per_bank, (k + 1) * per_bank)
                nc.vector.tensor_tensor(out=res[:, rows, cols], in0=part[:], in1=gate[b][:, rows, :], op=MULT)

        def store_out(first, last):
            cols = queries(first, last)
            nc.sync.dma_start(out=out_rows[:, :, cols], in_=res[:, :, cols])

        def quantise_out(b, cast):
            cols = queries(b, b)
            res_bf = sbuf([P, STRIP * PACK], BF16, f"res_bf{b}")
            cast(
                out=res_bf[:].rearrange("p (c e t) -> p c t e", e=2, t=TILES),
                in_=res[:, :, cols].rearrange("p t (c e) -> p c t e", e=2),
            )
            nc.vector.quantize_mx(out=out_codes[:, cols].bitcast(FP8X4), scales=out_scales[:, cols], in_=res_bf[:])

        def store_codes(first, last):
            cols = queries(first, last)
            nc.sync.dma_start(out=out_words[:, cols], in_=out_codes[:, cols].bitcast(I32))

        for b in (2, 1, 3, 0):
            gate_product(b)
        single, pairs = {}, {}
        low_pair = sbuf([P, 2, V], F32, "low_pair")
        for n in (1, 2):
            single[n] = sbuf([P, V], F32, "term11") if n == 1 else low_pair[:, 1, :]
            fetch(1, n, single[n], slice(0, V))
            pairs[n] = sbuf([P, 2, WIDE], F32, f"pair{n}")
            for e in range(n - 1, 2):
                fetch(2 + e, n, pairs[n][:, e, :], slice(0, WIDE))
        fetch(0, 2, low_pair[:, 0, :], queries(0, 1))
        fetch(2, 2, pairs[2][:, 0, :], queries(0, 1))
        gate_sigmoid(2)
        w2_dealt = deal_words(w2_raw, "w2_dealt", nc.scalar.copy)
        for t in range(TILES):
            look_up(t, 0, sbuf([P, WIDTHS[t]], F32, f"term{t}0"), slice(0, WIDTHS[t]))
        term01 = sbuf([P, V], F32, "term01")
        look_up(0, 1, term01, queries(2, 3))
        weigh(1, 1, single[1], slice(0, V))
        weigh_pair(1, 1, pairs[1], slice(0, WIDE))
        look_up(0, 2, low_pair[:, 0, :], queries(2, 3))
        weigh(1, 2, single[2], queries(2, 3))
        round_sums(GROUPS[0])
        look_up(2, 2, pairs[2][:, 0, :], queries(2, 2))
        weigh(3, 2, pairs[2][:, 1, :], queries(2, 2))
        round_sums(GROUPS[2])
        weigh_pair(1, 2, pairs[2], queries(0, 1))
        round_sums(GROUPS[3])
        weigh_pair(0, 2, low_pair, queries(0, 1))
        look_up(0, 1, term01, queries(0, 1))
        round_sums(GROUPS[1])
        for b, u in ((2, 0), (2, 1), (1, 1), (0, 1), (1, 0), (0, 0)):
            turn_back(b, u)
        z_bf = {2: interleave(2)}
        for b in (1, 0):
            z_bf[b] = interleave(b)
        turn_back(LAST, 0)
        z_last = sbuf([P, STRIP * PACK], BF16, "z_last")
        number, place = BACK_PLACES[LAST]
        nc.scalar.copy(
            out=z_last[:].bitcast(F32).rearrange("p (v u) -> p v u", u=2)[:, :, 0], in_=back[number][:, place, 0, :]
        )
        last_terms = sbuf([P, 2, 2, STRIP], F32, "last_terms", "term11")
        cols = queries(LAST, LAST)
        pair = sbuf([P, 2, STRIP], F32, "pair")

        def short_terms(n, into):
            for e in range(2):
                nc.vector.tensor_tensor(
                    out=into[:, e, :], in0=y[2 + e][:].indirect(places(n, cols)), in1=weights[n][:, cols], op=MULT
                )

        for n in range(2):
            short_terms(n, last_terms[:, :, n, :])
        project(2, z_bf[2])
        third = sbuf([P, 2, STRIP], F32, "third", "zt10")
        short_terms(2, third)
        project(1, z_bf[1])
        nc.vector.tensor_tensor(out=pair[:], in0=last_terms[:, :, 0, :], in1=third[:], op=ADD)
        project(0, z_bf[0])
        nc.vector.tensor_tensor(
            out=z_last[:].rearrange("p (v u e) -> p v u e", u=2, e=2)[:, :, 1, :],
            in0=pair[:].rearrange("p e v -> p v e"), in1=last_terms[:, :, 1, :].rearrange("p e v -> p v e"), op=ADD,
        )
        gate_sigmoid(1, "zt00")
        gate_sigmoid(0, "z_bf1")
        gate_sigmoid(LAST, "z_bf0")
        gate_strip(2)
        store_out(2, 2)
        project(LAST, z_last)
        for b in (1, 0):
            gate_strip(b)
            store_out(b, b)
        gate_strip(LAST)
        store_out(LAST, LAST)
        for b in (2, 1, 0):
            quantise_out(b, nc.scalar.copy)
        store_codes(0, LAST - 1)
        quantise_out(LAST, nc.vector.tensor_copy)
        store_codes(LAST, LAST)

        for q in range(QUADRANTS):
            queue = nc.scalar if q % 2 else nc.sync
            queue.dma_start(
                out=out_2[0][4 * q : 4 * q + 4, :].bitcast(I32),
                in_=out_scales[32 * q : 32 * q + 4, :].bitcast(I32),
            )
